import numpy as np
import ml_dtypes


def mxq(x, axis, fmt="e4m3"):
    dtype, down = {"e4m3": (ml_dtypes.float8_e4m3fn, 7), "e5m2": (ml_dtypes.float8_e5m2, 14)}[fmt]
    v = np.moveaxis(np.asarray(x, np.float32).astype(ml_dtypes.bfloat16).astype(np.float64), axis, -1)
    blocks = v.reshape(v.shape[:-1] + (-1, 32))
    amax = np.abs(blocks).max(-1, keepdims=True)
    byte = np.maximum(np.where(amax > 0, np.frexp(amax)[1] - 1 + 127, 0) - down, 1)
    scale = np.exp2(byte - 127.0)
    codes = (blocks / scale).astype(np.float32).astype(dtype).astype(np.float64)
    return np.moveaxis((codes * scale).reshape(v.shape), -1, axis)


WIDE = False


def mx_kscale(k):
    if not WIDE:
        return np.ones(k)
    levels = np.array([10, -10, 5, -5, 0])
    if k % 512:
        return np.exp2(np.random.permutation(np.resize(levels, k // 32))).repeat(32)
    a = np.empty((k // 512, 16))
    for p in range(k // 512):
        a[p, :8] = np.random.permutation(np.resize(levels, 8))
        for g in range(8):
            far = levels[np.abs(levels - a[p, g]) >= 10]
            a[p, g + 8] = far[np.random.randint(len(far))]
    return np.exp2(a.ravel()).repeat(32)


def f64(x):
    return np.asarray(x).astype(np.float64)


def striped(idx):
    return np.tile(idx.reshape(-1, 16).T, (8, 1)).astype(np.uint16)


def unstriped(offs):
    return offs[:16].T.reshape(-1).astype(np.int64)


E2M1 = np.array([0.0, 0.5, 1.0, 1.5, 2.0, 3.0, 4.0, 6.0, -0.0, -0.5, -1.0, -1.5, -2.0, -3.0, -4.0, -6.0])


def pack_weight(w, fmt):
    k, n = w.shape
    w = f64(np.asarray(w, np.float32).astype(ml_dtypes.bfloat16)).reshape(k // 32, 32, n)
    amax = np.abs(w).max(1)
    if fmt == "e4m3":
        byte = np.frexp(amax)[1] - 1 + 127 - 7
    else:
        mant, ex = np.frexp(amax / 6.0)
        byte = np.where(mant > 0.5, ex, ex - 1) + 127
    byte = np.clip(np.where(amax > 0, byte, 1), 1, 254)
    scaled = (w * np.exp2(127.0 - byte)[:, None, :]).reshape(k, n).astype(np.float32)
    by_word = np.ascontiguousarray(scaled.reshape(k // 512, 128, 4, n).transpose(0, 1, 3, 2))
    if fmt == "e4m3":
        words = by_word.astype(ml_dtypes.float8_e4m3fn).view(np.uint8)
    else:
        c = by_word.astype(ml_dtypes.float4_e2m1fn).view(np.uint8) & 0xF
        words = (c[..., 0::2] | (c[..., 1::2] << 4)).reshape(k // 512, 128, 2 * n)
    return np.ascontiguousarray(words), np.ascontiguousarray(byte.astype(np.uint8).reshape(k // 512, 16, n))


def unpack_weight(words, scales, fmt):
    g, _, n = scales.shape
    words = np.ascontiguousarray(words).reshape(g, 128, n, -1)
    if fmt == "e4m3":
        vals = words.view(ml_dtypes.float8_e4m3fn).astype(np.float64)
    else:
        nib = np.empty((g, 128, n, 4), np.uint8)
        nib[..., 0::2] = words & 0xF
        nib[..., 1::2] = words >> 4
        vals = E2M1[nib]
    vals = vals * np.repeat(np.exp2(scales.astype(np.float64) - 127.0), 8, axis=1)[..., None]
    return vals.transpose(0, 1, 3, 2).reshape(g * 512, n)


def gelu(v):
    return 0.5 * v * (1.0 + np.tanh(np.sqrt(2.0 / np.pi) * (v + 0.044715 * v**3)))


def striped8(idx):
    return np.concatenate([v.reshape(-1, 16).T for v in idx]).astype(np.uint16)


def unstriped8(offs):
    return np.stack([offs[16 * g:16 * g + 16].T.reshape(-1) for g in range(8)]).astype(np.int64)


def heads(h, wgt, idx8):
    r = np.arange(h.shape[0])
    return wgt[r // 4 % 128] * h[r[:, None], idx8[r % 512 // 64]]


def bf(x):
    return np.asarray(x, np.float32).astype(ml_dtypes.bfloat16)


def planes(Y):
    n, m = Y.shape
    b = f64(bf(Y)).reshape(n // 32, 32, m)
    amax = np.abs(b).max(1)
    byte = np.clip(np.where(amax > 0, np.frexp(amax)[1] - 1 + 127 - 7, 1), 1, 254)
    codes = (b * np.exp2(127.0 - byte)[:, None, :]).reshape(n, m).astype(np.float32).astype(ml_dtypes.float8_e4m3fn).view(np.uint8)
    words = codes.reshape(n // 512, 128, 4, m).transpose(0, 1, 3, 2)
    return np.ascontiguousarray(words), np.ascontiguousarray(byte.astype(np.uint8).reshape(n // 512, 16, m))


K, H, N, T, S, P = 512, 1024, 1024, 4096, 2048, 1024

def setup_inputs():
    n = np.random.standard_normal
    s = mx_kscale(K)[:, None]
    u = mx_kscale(H)[:, None]
    tab_words, tab_scales = pack_weight(n((K, T)) * s, "e4m3")
    w1_words, w1_scales = pack_weight(n((K, H)) / np.sqrt(K) / s, "e2m1")
    size = np.exp(0.8 * n(N))
    return {
        "tab_words": tab_words, "tab_scales": tab_scales,
        "offs": striped(np.random.permutation(T)[:S]),
        "w1_words": w1_words, "w1_scales": w1_scales,
        "offs2": striped8(np.stack([np.random.permutation(S)[:P] for _ in range(8)])),
        "wgt": np.repeat(np.random.uniform(0.5, 2.0, (8, P)), 16, axis=0).astype(np.float32),
        "half": np.exp(0.3 * n(H)).astype(np.float32),
        "gain": (np.random.uniform(0.5, 1.5, H) * u[:, 0]).astype(np.float32),
        "spread": (2.0 * n((H, N)) / np.sqrt(H) / u * size[None, :]).astype(np.float32),
        "comfort": (0.8 * np.random.uniform(0.5, 1.5, N) * size).astype(np.float32),
    }

def reference(tab_words, tab_scales, offs, w1_words, w1_scales, offs2, wgt, half, gain, spread, comfort):
    v = unpack_weight(tab_words, tab_scales, "e4m3")[:, unstriped(offs)]
    w1 = unpack_weight(w1_words, w1_scales, "e2m1")
    h = np.square(w1.T @ v)
    x = heads(h, f64(wgt), unstriped8(offs2))
    sat = x / (x + f64(half)[:, None])
    z = sat * f64(gain)[:, None]
    e = mxq(f64(spread), 0, "e4m3").T @ mxq(z, 0, "e4m3")
    y = np.minimum(e, f64(comfort)[:, None])
    words, scales = planes(y)
    return y, words, scales

@@ -1,0 +1,257 @@
+from contextlib import ExitStack
+
+import concourse.mybir as mybir
+
+K, H, N, T, S, M = 512, 1024, 1024, 4096, 2048, 1024
+FLOPS = 2 * K * H * S + 2 * H * N * M
+
+F32 = mybir.dt.float32
+BF16 = mybir.dt.bfloat16
+I32 = mybir.dt.int32
+U32 = mybir.dt.uint32
+U16 = mybir.dt.uint16
+U8 = mybir.dt.uint8
+FP8X4 = mybir.dt.float8_e4m3fn_x4
+FP4X4 = mybir.dt.float4_e2m1fn_x4
+ACT = mybir.ActivationFunctionType
+ALU = mybir.AluOpType
+
+P = 128
+PACK = 4
+PASS = P * PACK
+BANK = 512
+PER_COL = 16
+WIDTHS = (256, 256, 256, 128, 128)
+WG_ON_SCALAR = 5
+EARLY_TILES = 3
+WHOLE_PICKS = 6
+
+
+def tile_list_cochlear_spread_levels_kernel(
+    tc, tab_words, tab_scales, offs, w1_words, w1_scales, offs2, wgt, half, gain, spread, comfort,
+    out_0, out_1, out_2,
+):
+    nc = tc.nc
+    passes = H // PASS
+    slots = passes * PACK
+    groups = N // PASS
+    starts = [sum(WIDTHS[:k]) for k in range(len(WIDTHS))]
+
+    with ExitStack() as ctx:
+        lists = ctx.enter_context(tc.tile_pool(name="lists", bufs=1))
+        keep = ctx.enter_context(tc.tile_pool(name="keep", bufs=1))
+        hpool = ctx.enter_context(tc.tile_pool(name="hpool", bufs=5))
+        big = ctx.enter_context(tc.tile_pool(name="big", bufs=4))
+        ring = ctx.enter_context(tc.tile_pool(name="ring", bufs=2))
+        psum = ctx.enter_context(tc.psum_pool(name="psum", bufs=8))
+
+        idx = lists.tile([P, S // PER_COL], U16, name="idx")
+        idx2 = lists.tile([P, M // PER_COL], U16, name="idx2")
+
+        tab_w = keep.tile([P, T], U32, name="tab_w", align_bytes=64)
+        tab_s = keep.tile([P, T], U8, name="tab_s", align_bytes=64)
+        w1_w_raw = keep.tile([P, 2 * H], U8, name="w1_w_raw", align_bytes=64)
+        w1_s_raw = keep.tile([P, H], U8, name="w1_s_raw", align_bytes=64)
+        w1_w = keep.tile([P, 2 * H], U8, name="w1_w", align_bytes=64)
+        w1_s = keep.tile([P, H], U8, name="w1_s", align_bytes=64)
+        wgt_sb = keep.tile([P, M], F32, name="wgt_sb")
+        half_sb = keep.tile([P, slots], F32, name="half_sb")
+        gain_sb = keep.tile([P, slots], F32, name="gain_sb")
+        comfort_sb = keep.tile([P, groups * PACK], F32, name="comfort_sb")
+
+        zero_words = T // 4 // 2
+        nc.vector.memset(tab_s[:].bitcast(I32)[:, :zero_words], 0)
+        nc.gpsimd.memset(tab_s[:].bitcast(I32)[:, zero_words:], 0)
+        nc.gpsimd.memset(w1_s_raw[:].bitcast(I32), 0)
+
+        def load_by_slot(tile, vector):
+            nc.sync.dma_start(
+                tile[:].rearrange("p (b i) -> p b i", i=PACK), vector.rearrange("(b p i) -> p b i", p=P, i=PACK)
+            )
+
+        def load_scale_rows(tile, rows):
+            for q in range(4):
+                nc.sync.dma_start(tile[32 * q : 32 * q + 4, :].bitcast(I32), rows[4 * q : 4 * q + 4, :].bitcast(I32))
+
+        nc.sync.dma_start(idx[:], offs)
+        nc.sync.dma_start(idx2[:], offs2)
+        load_by_slot(gain_sb, gain)
+        load_by_slot(half_sb, half)
+        load_scale_rows(tab_s, tab_scales[0])
+        nc.sync.dma_start(wgt_sb[:], wgt)
+        load_scale_rows(w1_s_raw, w1_scales[0])
+        nc.sync.dma_start(w1_w_raw[:].bitcast(I32), w1_words[0].bitcast(I32))
+        nc.sync.dma_start(tab_w[:].bitcast(I32), tab_words[0].rearrange("p t i -> p (t i)").bitcast(I32))
+        load_by_slot(comfort_sb, comfort)
+        spread_raw = {}
+        for g in range(groups):
+            for b in range(passes):
+                raw = big.tile([P, PACK, PASS], F32, name="big")
+                rows = spread[b * PASS : (b + 1) * PASS, g * PASS : (g + 1) * PASS]
+                nc.sync.dma_start(raw[:], rows.rearrange("(p j) n -> p j n", j=PACK))
+                spread_raw[b, g] = raw
+
+        pieces = S // BANK
+        v_s = [keep.tile([P, BANK], U8, name="v_s%d" % c, align_bytes=64) for c in range(pieces)]
+        v_w = [keep.tile([P, BANK], U32, name="v_w%d" % c, align_bytes=64) for c in range(pieces)]
+        piece_cols = [slice(c * BANK // PER_COL, (c + 1) * BANK // PER_COL) for c in range(pieces)]
+        for c in range(pieces):
+            nc.vector.tensor_copy(v_s[c][:], tab_s[:].indirect(idx[:, piece_cols[c]]))
+        nc.vector.tensor_copy(
+            w1_s[:].rearrange("p (b i m) -> p b i m", b=passes, i=PACK),
+            w1_s_raw[:].rearrange("p (b m i) -> p b i m", b=passes, i=PACK),
+        )
+        nc.vector.tensor_copy(
+            w1_w[:].bitcast(U16).rearrange("p (b i m) -> p b i m", b=passes, i=PACK),
+            w1_w_raw[:].bitcast(U16).rearrange("p (b m i) -> p b i m", b=passes, i=PACK),
+        )
+        for c in range(pieces):
+            nc.vector.tensor_copy(v_w[c][:], tab_w[:].indirect(idx[:, piece_cols[c]]))
+
+        root = keep.tile([P, slots], F32, name="root")
+        gain_inv = keep.tile([P, slots], F32, name="gain_inv")
+        sign = keep.tile([P, slots], F32, name="sign")
+        half_signed = keep.tile([P, slots], F32, name="half_signed")
+        nc.scalar.activation(root[:], gain_sb[:], ACT.Abs_reciprocal_sqrt)
+        nc.gpsimd.tensor_scalar(root[:], root[:], 2.0**60, None, ALU.min)
+        nc.gpsimd.tensor_tensor(gain_inv[:], root[:], root[:], ALU.mult)
+        nc.gpsimd.tensor_scalar(sign[:], gain_sb[:], 0.0, 0.5, ALU.is_ge, ALU.subtract)
+        nc.gpsimd.tensor_tensor(sign[:], sign[:], half_sb[:], ALU.mult)
+        nc.gpsimd.tensor_scalar(half_signed[:], sign[:], 2.0, None, ALU.mult)
+
+        wg = []
+        for s in range(slots):
+            scaled = keep.tile([P, M], F32, name="wg%d" % s)
+            if s < WG_ON_SCALAR:
+                nc.scalar.activation(scaled[:], wgt_sb[:], ACT.Copy, scale=gain_sb[:, s : s + 1])
+            else:
+                nc.gpsimd.tensor_scalar(scaled[:], wgt_sb[:], gain_sb[:, s : s + 1], 0.0, ALU.mult, ALU.add)
+            wg.append(scaled)
+
+        h = [hpool.tile([P, S], F32, name="h") for s in range(EARLY_TILES)]
+
+        def band_response(s, c):
+            bank = psum.tile([P, BANK], F32, name="bank")
+            nc.tensor.matmul_mx(
+                out=bank[:],
+                lhsT=w1_w[:, 2 * P * s : 2 * P * (s + 1)].bitcast(FP4X4),
+                lhsT_scale=w1_s[:, P * s : P * (s + 1)],
+                rhs=v_w[c][:].bitcast(FP8X4),
+                rhs_scale=v_s[c][:],
+                start=True,
+                stop=True,
+            )
+            nc.scalar.activation(h[s][:, c * BANK : (c + 1) * BANK], bank[:], ACT.Square)
+
+        xg_all = [keep.tile([P, PACK, M], F32, name="xg%d" % b) for b in range(passes)]
+
+        def pick(s, m0, w):
+            cols = slice(m0 // PER_COL, (m0 + w) // PER_COL)
+            out = xg_all[s // PACK][:, s % PACK, m0 : m0 + w]
+            nc.vector.tensor_tensor(out, h[s][:].indirect(idx2[:, cols]), wg[s][:, m0 : m0 + w], ALU.mult)
+
+        for c in range(S // BANK):
+            for s in range(EARLY_TILES):
+                band_response(s, c)
+        for s in range(slots):
+            if s >= EARLY_TILES:
+                h.append(hpool.tile([P, S], F32, name="h"))
+                for c in range(S // BANK):
+                    band_response(s, c)
+            if s < WHOLE_PICKS:
+                pick(s, 0, M)
+
+        sp_w = keep.tile([P, passes, N], U32, name="sp_w", align_bytes=64)
+        sp_s = keep.tile([P, passes, N], U8, name="sp_s", align_bytes=64)
+
+        def quantise_spread(b, g):
+            grouped = ring.tile([P, PASS * PACK], BF16, name="sp_bf", align_bytes=64)
+            cast = nc.vector.tensor_copy if g == 0 else nc.scalar.copy
+            cast(
+                grouped[:].rearrange("p (u e m j) -> p u m j e", u=2, e=2, j=PACK),
+                spread_raw[b, g][:].rearrange("p j (m u e) -> p u m j e", u=2, e=2),
+            )
+            cols = slice(g * PASS, (g + 1) * PASS)
+            nc.vector.quantize_mx(out=sp_w[:, b, cols].bitcast(FP8X4), scales=sp_s[:, b, cols], in_=grouped[:])
+
+        z_w = keep.tile([P, passes, M], U32, name="z_w", align_bytes=64)
+        z_s = keep.tile([P, passes, M], U8, name="z_s", align_bytes=64)
+        y_w = keep.tile([P, groups, M], U32, name="y_w", align_bytes=64)
+        y_s = keep.tile([P, groups, M], U8, name="y_s", align_bytes=64)
+
+        def saturate(b, k):
+            m0, w = starts[k], WIDTHS[k]
+            for s in range(max(PACK * b, WHOLE_PICKS), PACK * (b + 1)):
+                pick(s, m0, w)
+            xg = xg_all[b][:, :, m0 : m0 + w]
+            inv = ring.tile([P, PACK, w], F32, name="inv", bufs=3)
+            for i in range(PACK):
+                s = PACK * b + i
+                nc.scalar.activation(
+                    inv[:, i, :], xg[:, i, :], ACT.Abs_reciprocal_sqrt,
+                    bias=half_signed[:, s : s + 1], scale=gain_inv[:, s : s + 1],
+                )
+            nc.scalar.activation(inv[:], inv[:], ACT.Square)
+            z_bf = ring.tile([P, w * PACK], BF16, name="z_bf", align_bytes=64)
+            nc.vector.tensor_tensor(
+                z_bf[:].rearrange("p (c e i) -> p c i e", e=2, i=PACK),
+                xg.rearrange("p i (c e) -> p c i e", e=2),
+                inv[:].rearrange("p i (c e) -> p c i e", e=2),
+                ALU.mult,
+            )
+            cols = slice(m0, m0 + w)
+            nc.vector.quantize_mx(out=z_w[:, b, cols].bitcast(FP8X4), scales=z_s[:, b, cols], in_=z_bf[:])
+
+        def levels(k):
+            m0, w = starts[k], WIDTHS[k]
+            cols = slice(m0, m0 + w)
+            per_bank = BANK // w
+            y = big.tile([P, groups, PACK, w], F32, name="big")
+            for g in range(groups):
+                for t0 in range(0, PACK, per_bank):
+                    bank = psum.tile([P, per_bank, w], F32, name="bank")
+                    for t in range(t0, t0 + per_bank):
+                        n_cols = slice(g * PASS + t * P, g * PASS + (t + 1) * P)
+                        for b in range(passes):
+                            nc.tensor.matmul_mx(
+                                out=bank[:, t - t0, :],
+                                lhsT=sp_w[:, b, n_cols].bitcast(FP8X4),
+                                lhsT_scale=sp_s[:, b, n_cols],
+                                rhs=z_w[:, b, cols].bitcast(FP8X4),
+                                rhs_scale=z_s[:, b, cols],
+                                start=(b == 0),
+                                stop=(b == passes - 1),
+                            )
+                    limit = comfort_sb[:, PACK * g + t0 : PACK * g + t0 + per_bank]
+                    nc.vector.tensor_tensor(
+                        y[:, g, t0 : t0 + per_bank, :], bank[:],
+                        limit.unsqueeze(2).to_broadcast([P, per_bank, w]), ALU.min,
+                    )
+                rows = out_0[g * PASS : (g + 1) * PASS, cols]
+                nc.sync.dma_start(rows.rearrange("(p t) m -> p t m", t=PACK), y[:, g])
+                y_bf = ring.tile([P, w * PACK], BF16, name="y_bf", align_bytes=64)
+                nc.scalar.copy(
+                    y_bf[:].rearrange("p (c e t) -> p c t e", e=2, t=PACK),
+                    y[:, g].rearrange("p t (c e) -> p c t e", e=2),
+                )
+                nc.vector.quantize_mx(out=y_w[:, g, cols].bitcast(FP8X4), scales=y_s[:, g, cols], in_=y_bf[:])
+            nc.sync.dma_start(
+                out_1[:, :, cols, :].rearrange("g p m t -> p g (m t)").bitcast(I32), y_w[:, :, cols].bitcast(I32)
+            )
+
+        for b in range(passes):
+            quantise_spread(b, 0)
+        saturate(0, 0)
+        saturate(1, 0)
+        for b in range(passes):
+            quantise_spread(b, 1)
+        for k in range(len(WIDTHS)):
+            if k + 1 < len(WIDTHS):
+                saturate(0, k + 1)
+                saturate(1, k + 1)
+            levels(k)
+        for q in range(4):
+            nc.scalar.dma_start(
+                out_2[:, 4 * q : 4 * q + 4, :].rearrange("g r m -> r g m").bitcast(I32),
+                y_s[32 * q : 32 * q + 4].bitcast(I32),
+            )

@@ -22,9 +22,14 @@ PASS = P * PACK
 BANK = 512
 PER_COL = 16
 WIDTHS = (256, 256, 256, 128, 128)
-WG_ON_SCALAR = 5
-EARLY_TILES = 3
-WHOLE_PICKS = 6
+EARLY_TILES = 2
+WHOLE_PICKS = 8
+STAGE = 5
+LEAD = 2
+AHEAD = 2
+FIRST = 4
+YV = 1
+SPREAD_ON_VECTOR = ((0, 0), (1, 0))
 
 
 def tile_list_cochlear_spread_levels_kernel(
@@ -105,28 +110,24 @@ def tile_list_cochlear_spread_levels_kernel(
             w1_w[:].bitcast(U16).rearrange("p (b i m) -> p b i m", b=passes, i=PACK),
             w1_w_raw[:].bitcast(U16).rearrange("p (b m i) -> p b i m", b=passes, i=PACK),
         )
-        for c in range(pieces):
-            nc.vector.tensor_copy(v_w[c][:], tab_w[:].indirect(idx[:, piece_cols[c]]))
-
         root = keep.tile([P, slots], F32, name="root")
         gain_inv = keep.tile([P, slots], F32, name="gain_inv")
         sign = keep.tile([P, slots], F32, name="sign")
         half_signed = keep.tile([P, slots], F32, name="half_signed")
         nc.scalar.activation(root[:], gain_sb[:], ACT.Abs_reciprocal_sqrt)
-        nc.gpsimd.tensor_scalar(root[:], root[:], 2.0**60, None, ALU.min)
-        nc.gpsimd.tensor_tensor(gain_inv[:], root[:], root[:], ALU.mult)
-        nc.gpsimd.tensor_scalar(sign[:], gain_sb[:], 0.0, 0.5, ALU.is_ge, ALU.subtract)
-        nc.gpsimd.tensor_tensor(sign[:], sign[:], half_sb[:], ALU.mult)
-        nc.gpsimd.tensor_scalar(half_signed[:], sign[:], 2.0, None, ALU.mult)
 
         wg = []
         for s in range(slots):
             scaled = keep.tile([P, M], F32, name="wg%d" % s)
-            if s < WG_ON_SCALAR:
-                nc.scalar.activation(scaled[:], wgt_sb[:], ACT.Copy, scale=gain_sb[:, s : s + 1])
-            else:
-                nc.gpsimd.tensor_scalar(scaled[:], wgt_sb[:], gain_sb[:, s : s + 1], 0.0, ALU.mult, ALU.add)
+            nc.scalar.activation(scaled[:], wgt_sb[:], ACT.Copy, scale=gain_sb[:, s : s + 1])
             wg.append(scaled)
+
+        nc.vector.tensor_scalar(root[:], root[:], 2.0**60, None, ALU.min)
+        nc.vector.tensor_scalar(sign[:], gain_sb[:], 0.0, 0.5, ALU.is_ge, ALU.subtract)
+        nc.vector.tensor_tensor(gain_inv[:], root[:], root[:], ALU.mult)
+        nc.vector.scalar_tensor_tensor(half_signed[:], sign[:], 2.0, half_sb[:], ALU.mult, ALU.mult)
+        for c in range(pieces):
+            nc.vector.tensor_copy(v_w[c][:], tab_w[:].indirect(idx[:, piece_cols[c]]))
 
         h = [hpool.tile([P, S], F32, name="h") for s in range(EARLY_TILES)]
 
@@ -163,93 +164,128 @@ def tile_list_cochlear_spread_levels_kernel(
 
         sp_w = keep.tile([P, passes, N], U32, name="sp_w", align_bytes=64)
         sp_s = keep.tile([P, passes, N], U8, name="sp_s", align_bytes=64)
-
-        def quantise_spread(b, g):
-            grouped = ring.tile([P, PASS * PACK], BF16, name="sp_bf", align_bytes=64)
-            cast = nc.vector.tensor_copy if g == 0 else nc.scalar.copy
-            cast(
-                grouped[:].rearrange("p (u e m j) -> p u m j e", u=2, e=2, j=PACK),
-                spread_raw[b, g][:].rearrange("p j (m u e) -> p u m j e", u=2, e=2),
-            )
-            cols = slice(g * PASS, (g + 1) * PASS)
-            nc.vector.quantize_mx(out=sp_w[:, b, cols].bitcast(FP8X4), scales=sp_s[:, b, cols], in_=grouped[:])
-
-        z_w = keep.tile([P, passes, M], U32, name="z_w", align_bytes=64)
-        z_s = keep.tile([P, passes, M], U8, name="z_s", align_bytes=64)
+        z_w = [keep.tile([P, passes, w], U32, name="z_w%d" % k, align_bytes=64) for k, w in enumerate(WIDTHS)]
+        z_s = [keep.tile([P, passes, w], U8, name="z_s%d" % k, align_bytes=64) for k, w in enumerate(WIDTHS)]
         y_w = keep.tile([P, groups, M], U32, name="y_w", align_bytes=64)
         y_s = keep.tile([P, groups, M], U8, name="y_s", align_bytes=64)
+        chunks = len(WIDTHS)
+        inv, z_bf, y, y_bf, sp_bf = {}, {}, {}, {}, {}
 
-        def saturate(b, k):
-            m0, w = starts[k], WIDTHS[k]
-            for s in range(max(PACK * b, WHOLE_PICKS), PACK * (b + 1)):
-                pick(s, m0, w)
-            xg = xg_all[b][:, :, m0 : m0 + w]
-            inv = ring.tile([P, PACK, w], F32, name="inv", bufs=3)
+        def cols_of(k):
+            return slice(starts[k], starts[k] + WIDTHS[k])
+
+        def round_spread(b, g):
+            sp_bf[b, g] = ring.tile([P, PASS * PACK], BF16, name="stage", bufs=STAGE, align_bytes=64)
+            cast = nc.vector.tensor_copy if (b, g) in SPREAD_ON_VECTOR else nc.scalar.copy
+            cast(
+                sp_bf[b, g][:].rearrange("p (u e m j) -> p u m j e", u=2, e=2, j=PACK),
+                spread_raw[b, g][:].rearrange("p j (m u e) -> p u m j e", u=2, e=2),
+            )
+
+        def quantise_spread(b, g):
+            cols = slice(g * PASS, (g + 1) * PASS)
+            nc.vector.quantize_mx(out=sp_w[:, b, cols].bitcast(FP8X4), scales=sp_s[:, b, cols], in_=sp_bf[b, g][:])
+
+        def late_picks(k):
+            for s in range(WHOLE_PICKS, slots):
+                pick(s, starts[k], WIDTHS[k])
+
+        def inverse(b, k):
+            inv[b, k] = ring.tile([P, PACK, WIDTHS[k]], F32, name="stage", bufs=STAGE, align_bytes=64)
             for i in range(PACK):
                 s = PACK * b + i
                 nc.scalar.activation(
-                    inv[:, i, :], xg[:, i, :], ACT.Abs_reciprocal_sqrt,
+                    inv[b, k][:, i, :], xg_all[b][:, i, cols_of(k)], ACT.Abs_reciprocal_sqrt,
                     bias=half_signed[:, s : s + 1], scale=gain_inv[:, s : s + 1],
                 )
-            nc.scalar.activation(inv[:], inv[:], ACT.Square)
-            z_bf = ring.tile([P, w * PACK], BF16, name="z_bf", align_bytes=64)
+            nc.scalar.activation(inv[b, k][:], inv[b, k][:], ACT.Square)
+
+        def saturate(b, k):
+            if b == 0:
+                z_bf[k] = ring.tile([P, passes, WIDTHS[k] * PACK], BF16, name="z_bf", align_bytes=64)
             nc.vector.tensor_tensor(
-                z_bf[:].rearrange("p (c e i) -> p c i e", e=2, i=PACK),
-                xg.rearrange("p i (c e) -> p c i e", e=2),
-                inv[:].rearrange("p i (c e) -> p c i e", e=2),
+                z_bf[k][:, b, :].rearrange("p (c e i) -> p c i e", e=2, i=PACK),
+                xg_all[b][:, :, cols_of(k)].rearrange("p i (c e) -> p c i e", e=2),
+                inv[b, k][:].rearrange("p i (c e) -> p c i e", e=2),
                 ALU.mult,
             )
-            cols = slice(m0, m0 + w)
-            nc.vector.quantize_mx(out=z_w[:, b, cols].bitcast(FP8X4), scales=z_s[:, b, cols], in_=z_bf[:])
 
-        def levels(k):
-            m0, w = starts[k], WIDTHS[k]
-            cols = slice(m0, m0 + w)
-            per_bank = BANK // w
-            y = big.tile([P, groups, PACK, w], F32, name="big")
-            for g in range(groups):
-                for t0 in range(0, PACK, per_bank):
-                    bank = psum.tile([P, per_bank, w], F32, name="bank")
-                    for t in range(t0, t0 + per_bank):
-                        n_cols = slice(g * PASS + t * P, g * PASS + (t + 1) * P)
-                        for b in range(passes):
-                            nc.tensor.matmul_mx(
-                                out=bank[:, t - t0, :],
-                                lhsT=sp_w[:, b, n_cols].bitcast(FP8X4),
-                                lhsT_scale=sp_s[:, b, n_cols],
-                                rhs=z_w[:, b, cols].bitcast(FP8X4),
-                                rhs_scale=z_s[:, b, cols],
-                                start=(b == 0),
-                                stop=(b == passes - 1),
-                            )
-                    limit = comfort_sb[:, PACK * g + t0 : PACK * g + t0 + per_bank]
-                    nc.vector.tensor_tensor(
-                        y[:, g, t0 : t0 + per_bank, :], bank[:],
-                        limit.unsqueeze(2).to_broadcast([P, per_bank, w]), ALU.min,
-                    )
-                rows = out_0[g * PASS : (g + 1) * PASS, cols]
-                nc.sync.dma_start(rows.rearrange("(p t) m -> p t m", t=PACK), y[:, g])
-                y_bf = ring.tile([P, w * PACK], BF16, name="y_bf", align_bytes=64)
-                nc.scalar.copy(
-                    y_bf[:].rearrange("p (c e t) -> p c t e", e=2, t=PACK),
-                    y[:, g].rearrange("p t (c e) -> p c t e", e=2),
-                )
-                nc.vector.quantize_mx(out=y_w[:, g, cols].bitcast(FP8X4), scales=y_s[:, g, cols], in_=y_bf[:])
-            nc.sync.dma_start(
-                out_1[:, :, cols, :].rearrange("g p m t -> p g (m t)").bitcast(I32), y_w[:, :, cols].bitcast(I32)
+        def quantise_z(k):
+            nc.vector.quantize_mx(
+                out=z_w[k][:].rearrange("p b m -> p (b m)").bitcast(FP8X4),
+                scales=z_s[k][:].rearrange("p b m -> p (b m)"),
+                in_=z_bf[k][:].rearrange("p b m -> p (b m)"),
             )
 
-        for b in range(passes):
-            quantise_spread(b, 0)
-        saturate(0, 0)
-        saturate(1, 0)
-        for b in range(passes):
-            quantise_spread(b, 1)
-        for k in range(len(WIDTHS)):
-            if k + 1 < len(WIDTHS):
-                saturate(0, k + 1)
-                saturate(1, k + 1)
-            levels(k)
+        def levels(g, k):
+            w, cols = WIDTHS[k], cols_of(k)
+            per_bank = BANK // w
+            if g == 0:
+                y[k] = big.tile([P, groups, PACK, w], F32, name="big")
+            for t0 in range(0, PACK, per_bank):
+                bank = psum.tile([P, per_bank, w], F32, name="bank")
+                for t in range(t0, t0 + per_bank):
+                    n_cols = slice(g * PASS + t * P, g * PASS + (t + 1) * P)
+                    for b in range(passes):
+                        nc.tensor.matmul_mx(
+                            out=bank[:, t - t0, :],
+                            lhsT=sp_w[:, b, n_cols].bitcast(FP8X4),
+                            lhsT_scale=sp_s[:, b, n_cols],
+                            rhs=z_w[k][:, b, :].bitcast(FP8X4),
+                            rhs_scale=z_s[k][:, b, :],
+                            start=(b == 0),
+                            stop=(b == passes - 1),
+                        )
+                limit = comfort_sb[:, PACK * g + t0 : PACK * g + t0 + per_bank]
+                nc.vector.tensor_tensor(
+                    y[k][:, g, t0 : t0 + per_bank, :], bank[:],
+                    limit.unsqueeze(2).to_broadcast([P, per_bank, w]), ALU.min,
+                )
+            rows = out_0[g * PASS : (g + 1) * PASS, cols]
+            nc.sync.dma_start(rows.rearrange("(p t) m -> p t m", t=PACK), y[k][:, g])
+            y_bf[g, k] = ring.tile([P, w * PACK], BF16, name="y_bf", align_bytes=64)
+            cast = nc.vector.tensor_copy if groups * (chunks - k) - g <= YV else nc.scalar.copy
+            cast(
+                y_bf[g, k][:].rearrange("p (c e t) -> p c t e", e=2, t=PACK),
+                y[k][:, g].rearrange("p t (c e) -> p c t e", e=2),
+            )
+
+        def quantise_y(g, k):
+            cols = cols_of(k)
+            nc.vector.quantize_mx(out=y_w[:, g, cols].bitcast(FP8X4), scales=y_s[:, g, cols], in_=y_bf[g, k][:])
+            if g == groups - 1:
+                nc.sync.dma_start(
+                    out_1[:, :, cols, :].rearrange("g p m t -> p g (m t)").bitcast(I32),
+                    y_w[:, :, cols].bitcast(I32),
+                )
+
+        pairs = [(b, g) for g in range(groups) for b in range(passes)]
+        for b, g in pairs[:FIRST]:
+            round_spread(b, g)
+            quantise_spread(b, g)
+        for k in range(LEAD):
+            inverse(0, k)
+        for b, g in pairs[FIRST:]:
+            round_spread(b, g)
+            quantise_spread(b, g)
+        for k in range(chunks + AHEAD):
+            done = k - AHEAD
+            if k < chunks:
+                inverse(1, k)
+                saturate(0, k)
+            if done >= 0:
+                levels(0, done)
+            if k + LEAD < chunks:
+                inverse(0, k + LEAD)
+            if k < chunks:
+                saturate(1, k)
+            if done >= 0:
+                levels(1, done)
+            if k < chunks:
+                quantise_z(k)
+            if done >= 0:
+                quantise_y(0, done)
+                quantise_y(1, done)
         for q in range(4):
             nc.scalar.dma_start(
                 out_2[:, 4 * q : 4 * q + 4, :].rearrange("g r m -> r g m").bitcast(I32),

@@ -19,17 +19,20 @@ ALU = mybir.AluOpType
 P = 128
 PACK = 4
 PASS = P * PACK
+QUADRANTS = 4
 BANK = 512
 PER_COL = 16
+PAIR = 2
+ALIGN = 64
+
 WIDTHS = (256, 256, 256, 128, 128)
-EARLY_TILES = 2
-WHOLE_PICKS = 8
-STAGE = 5
+HALF = M // 2
+ZEROED_BY_VECTOR = 256
+WEIGHTS_BY_SCALAR = 5
+EARLY_SLOTS = 2
 LEAD = 2
 AHEAD = 2
-FIRST = 4
-YV = 1
-SPREAD_ON_VECTOR = ((0, 0), (1, 0))
+ROOT_CAP = 2.0**60
 
 
 def tile_list_cochlear_spread_levels_kernel(
@@ -40,65 +43,63 @@ def tile_list_cochlear_spread_levels_kernel(
     passes = H // PASS
     slots = passes * PACK
     groups = N // PASS
-    starts = [sum(WIDTHS[:k]) for k in range(len(WIDTHS))]
+    pieces = S // BANK
+    chunks = len(WIDTHS)
+    starts = [sum(WIDTHS[:k]) for k in range(chunks)]
 
     with ExitStack() as ctx:
         lists = ctx.enter_context(tc.tile_pool(name="lists", bufs=1))
         keep = ctx.enter_context(tc.tile_pool(name="keep", bufs=1))
-        hpool = ctx.enter_context(tc.tile_pool(name="hpool", bufs=5))
-        big = ctx.enter_context(tc.tile_pool(name="big", bufs=4))
-        ring = ctx.enter_context(tc.tile_pool(name="ring", bufs=2))
+        h_pool = ctx.enter_context(tc.tile_pool(name="h_pool", bufs=PACK + 1))
+        ring = ctx.enter_context(tc.tile_pool(name="ring", bufs=3))
         psum = ctx.enter_context(tc.psum_pool(name="psum", bufs=8))
 
         idx = lists.tile([P, S // PER_COL], U16, name="idx")
         idx2 = lists.tile([P, M // PER_COL], U16, name="idx2")
-
-        tab_w = keep.tile([P, T], U32, name="tab_w", align_bytes=64)
-        tab_s = keep.tile([P, T], U8, name="tab_s", align_bytes=64)
-        w1_w_raw = keep.tile([P, 2 * H], U8, name="w1_w_raw", align_bytes=64)
-        w1_s_raw = keep.tile([P, H], U8, name="w1_s_raw", align_bytes=64)
-        w1_w = keep.tile([P, 2 * H], U8, name="w1_w", align_bytes=64)
-        w1_s = keep.tile([P, H], U8, name="w1_s", align_bytes=64)
-        wgt_sb = keep.tile([P, M], F32, name="wgt_sb")
+        tab_w = keep.tile([P, T], U32, name="tab_w", align_bytes=ALIGN)
+        tab_s = keep.tile([P, T], U8, name="tab_s", align_bytes=ALIGN)
+        w1_w_raw = keep.tile([P, 2 * H], U8, name="w1_w_raw", align_bytes=ALIGN)
+        w1_s_raw = keep.tile([P, H], U8, name="w1_s_raw", align_bytes=ALIGN)
+        w1_w = keep.tile([P, 2 * H], U8, name="w1_w", align_bytes=ALIGN)
+        w1_s = keep.tile([P, H], U8, name="w1_s", align_bytes=ALIGN)
+        wgt_sb = keep.tile([P, M], F32, name="wgt_sb", align_bytes=ALIGN)
         half_sb = keep.tile([P, slots], F32, name="half_sb")
         gain_sb = keep.tile([P, slots], F32, name="gain_sb")
         comfort_sb = keep.tile([P, groups * PACK], F32, name="comfort_sb")
 
-        zero_words = T // 4 // 2
-        nc.vector.memset(tab_s[:].bitcast(I32)[:, :zero_words], 0)
-        nc.gpsimd.memset(tab_s[:].bitcast(I32)[:, zero_words:], 0)
+        nc.vector.memset(tab_s[:].bitcast(I32)[:, :ZEROED_BY_VECTOR], 0)
+        nc.gpsimd.memset(tab_s[:].bitcast(I32)[:, ZEROED_BY_VECTOR:], 0)
         nc.gpsimd.memset(w1_s_raw[:].bitcast(I32), 0)
 
         def load_by_slot(tile, vector):
             nc.sync.dma_start(
-                tile[:].rearrange("p (b i) -> p b i", i=PACK), vector.rearrange("(b p i) -> p b i", p=P, i=PACK)
+                tile[:].rearrange("p (a i) -> p a i", i=PACK), vector.rearrange("(a p i) -> p a i", p=P, i=PACK)
             )
 
         def load_scale_rows(tile, rows):
-            for q in range(4):
+            for q in range(QUADRANTS):
                 nc.sync.dma_start(tile[32 * q : 32 * q + 4, :].bitcast(I32), rows[4 * q : 4 * q + 4, :].bitcast(I32))
 
         nc.sync.dma_start(idx[:], offs)
         nc.sync.dma_start(idx2[:], offs2)
         load_by_slot(gain_sb, gain)
         load_by_slot(half_sb, half)
+        load_by_slot(comfort_sb, comfort)
         load_scale_rows(tab_s, tab_scales[0])
         nc.sync.dma_start(wgt_sb[:], wgt)
-        load_scale_rows(w1_s_raw, w1_scales[0])
         nc.sync.dma_start(w1_w_raw[:].bitcast(I32), w1_words[0].bitcast(I32))
+        load_scale_rows(w1_s_raw, w1_scales[0])
         nc.sync.dma_start(tab_w[:].bitcast(I32), tab_words[0].rearrange("p t i -> p (t i)").bitcast(I32))
-        load_by_slot(comfort_sb, comfort)
         spread_raw = {}
         for g in range(groups):
             for b in range(passes):
-                raw = big.tile([P, PACK, PASS], F32, name="big")
+                raw = keep.tile([P, PACK, PASS], F32, name="spread_raw%d%d" % (b, g), align_bytes=ALIGN)
                 rows = spread[b * PASS : (b + 1) * PASS, g * PASS : (g + 1) * PASS]
                 nc.sync.dma_start(raw[:], rows.rearrange("(p j) n -> p j n", j=PACK))
                 spread_raw[b, g] = raw
 
-        pieces = S // BANK
-        v_s = [keep.tile([P, BANK], U8, name="v_s%d" % c, align_bytes=64) for c in range(pieces)]
-        v_w = [keep.tile([P, BANK], U32, name="v_w%d" % c, align_bytes=64) for c in range(pieces)]
+        v_s = [keep.tile([P, BANK], U8, name="v_s%d" % c, align_bytes=ALIGN) for c in range(pieces)]
+        v_w = [keep.tile([P, BANK], U32, name="v_w%d" % c, align_bytes=ALIGN) for c in range(pieces)]
         piece_cols = [slice(c * BANK // PER_COL, (c + 1) * BANK // PER_COL) for c in range(pieces)]
         for c in range(pieces):
             nc.vector.tensor_copy(v_s[c][:], tab_s[:].indirect(idx[:, piece_cols[c]]))
@@ -110,26 +111,31 @@ def tile_list_cochlear_spread_levels_kernel(
             w1_w[:].bitcast(U16).rearrange("p (b i m) -> p b i m", b=passes, i=PACK),
             w1_w_raw[:].bitcast(U16).rearrange("p (b m i) -> p b i m", b=passes, i=PACK),
         )
+
         root = keep.tile([P, slots], F32, name="root")
         gain_inv = keep.tile([P, slots], F32, name="gain_inv")
         sign = keep.tile([P, slots], F32, name="sign")
         half_signed = keep.tile([P, slots], F32, name="half_signed")
         nc.scalar.activation(root[:], gain_sb[:], ACT.Abs_reciprocal_sqrt)
-
-        wg = []
+        weights = []
         for s in range(slots):
-            scaled = keep.tile([P, M], F32, name="wg%d" % s)
-            nc.scalar.activation(scaled[:], wgt_sb[:], ACT.Copy, scale=gain_sb[:, s : s + 1])
-            wg.append(scaled)
-
-        nc.vector.tensor_scalar(root[:], root[:], 2.0**60, None, ALU.min)
+            scaled = keep.tile([P, M], F32, name="weights%d" % s, align_bytes=ALIGN)
+            if s < WEIGHTS_BY_SCALAR:
+                nc.scalar.activation(scaled[:], wgt_sb[:], ACT.Copy, scale=gain_sb[:, s : s + 1])
+            else:
+                nc.gpsimd.tensor_scalar(scaled[:], wgt_sb[:], gain_sb[:, s : s + 1], 0.0, ALU.mult, ALU.add)
+            weights.append(scaled)
+        nc.vector.tensor_scalar(root[:], root[:], ROOT_CAP, None, ALU.min)
         nc.vector.tensor_scalar(sign[:], gain_sb[:], 0.0, 0.5, ALU.is_ge, ALU.subtract)
         nc.vector.tensor_tensor(gain_inv[:], root[:], root[:], ALU.mult)
         nc.vector.scalar_tensor_tensor(half_signed[:], sign[:], 2.0, half_sb[:], ALU.mult, ALU.mult)
+
         for c in range(pieces):
             nc.vector.tensor_copy(v_w[c][:], tab_w[:].indirect(idx[:, piece_cols[c]]))
 
-        h = [hpool.tile([P, S], F32, name="h") for s in range(EARLY_TILES)]
+        h = [h_pool.tile([P, S], F32, name="h") for s in range(EARLY_SLOTS)]
+        xg_first = keep.tile([P, PACK, M], F32, name="xg_first")
+        xg_low = keep.tile([P, PACK, HALF], F32, name="xg_low")
 
         def band_response(s, c):
             bank = psum.tile([P, BANK], F32, name="bank")
@@ -144,69 +150,64 @@ def tile_list_cochlear_spread_levels_kernel(
             )
             nc.scalar.activation(h[s][:, c * BANK : (c + 1) * BANK], bank[:], ACT.Square)
 
-        xg_all = [keep.tile([P, PACK, M], F32, name="xg%d" % b) for b in range(passes)]
+        def pick(s, out, m0, width):
+            entries = idx2[:, m0 // PER_COL : (m0 + width) // PER_COL]
+            nc.vector.tensor_tensor(out, h[s][:].indirect(entries), weights[s][:, m0 : m0 + width], ALU.mult)
 
-        def pick(s, m0, w):
-            cols = slice(m0 // PER_COL, (m0 + w) // PER_COL)
-            out = xg_all[s // PACK][:, s % PACK, m0 : m0 + w]
-            nc.vector.tensor_tensor(out, h[s][:].indirect(idx2[:, cols]), wg[s][:, m0 : m0 + w], ALU.mult)
-
-        for c in range(S // BANK):
-            for s in range(EARLY_TILES):
+        for c in range(pieces):
+            for s in range(EARLY_SLOTS):
                 band_response(s, c)
         for s in range(slots):
-            if s >= EARLY_TILES:
-                h.append(hpool.tile([P, S], F32, name="h"))
-                for c in range(S // BANK):
+            if s >= EARLY_SLOTS:
+                h.append(h_pool.tile([P, S], F32, name="h"))
+                for c in range(pieces):
                     band_response(s, c)
-            if s < WHOLE_PICKS:
-                pick(s, 0, M)
+            if s < PACK:
+                pick(s, xg_first[:, s, :], 0, M)
+            else:
+                pick(s, xg_low[:, s - PACK, :], 0, HALF)
 
-        sp_w = keep.tile([P, passes, N], U32, name="sp_w", align_bytes=64)
-        sp_s = keep.tile([P, passes, N], U8, name="sp_s", align_bytes=64)
-        z_w = [keep.tile([P, passes, w], U32, name="z_w%d" % k, align_bytes=64) for k, w in enumerate(WIDTHS)]
-        z_s = [keep.tile([P, passes, w], U8, name="z_s%d" % k, align_bytes=64) for k, w in enumerate(WIDTHS)]
-        y_w = keep.tile([P, groups, M], U32, name="y_w", align_bytes=64)
-        y_s = keep.tile([P, groups, M], U8, name="y_s", align_bytes=64)
-        chunks = len(WIDTHS)
-        inv, z_bf, y, y_bf, sp_bf = {}, {}, {}, {}, {}
+        sp_w = keep.tile([P, passes, N], U32, name="sp_w", align_bytes=ALIGN)
+        sp_s = keep.tile([P, passes, N], U8, name="sp_s", align_bytes=ALIGN)
+        z_w = [keep.tile([P, passes, w], U32, name="z_w%d" % k, align_bytes=ALIGN) for k, w in enumerate(WIDTHS)]
+        z_s = [keep.tile([P, passes, w], U8, name="z_s%d" % k, align_bytes=ALIGN) for k, w in enumerate(WIDTHS)]
+        y_w = keep.tile([P, groups, M], U32, name="y_w", align_bytes=ALIGN)
+        y_s = keep.tile([P, groups, M], U8, name="y_s", align_bytes=ALIGN)
+        y_home = ("spread_raw00", "spread_raw10", "tab_w", "spread_raw11", "weights0")
+        xg, inv, z_bf, y, y_bf = {}, {}, {}, {}, {}
 
         def cols_of(k):
             return slice(starts[k], starts[k] + WIDTHS[k])
 
-        def round_spread(b, g):
-            sp_bf[b, g] = ring.tile([P, PASS * PACK], BF16, name="stage", bufs=STAGE, align_bytes=64)
-            cast = nc.vector.tensor_copy if (b, g) in SPREAD_ON_VECTOR else nc.scalar.copy
-            cast(
-                sp_bf[b, g][:].rearrange("p (u e m j) -> p u m j e", u=2, e=2, j=PACK),
-                spread_raw[b, g][:].rearrange("p j (m u e) -> p u m j e", u=2, e=2),
+        def stage_tile(shape, dtype):
+            return ring.tile(shape, dtype, name="stage", bufs=2 * passes + 1, align_bytes=ALIGN)
+
+        def quantise_spread(b, g, copy):
+            rounded = stage_tile([P, PASS * PACK], BF16)
+            copy(
+                rounded[:].rearrange("p (u e m j) -> p u m j e", u=PACK // PAIR, e=PAIR, j=PACK),
+                spread_raw[b, g][:].rearrange("p j (m u e) -> p u m j e", u=PACK // PAIR, e=PAIR),
             )
-
-        def quantise_spread(b, g):
             cols = slice(g * PASS, (g + 1) * PASS)
-            nc.vector.quantize_mx(out=sp_w[:, b, cols].bitcast(FP8X4), scales=sp_s[:, b, cols], in_=sp_bf[b, g][:])
-
-        def late_picks(k):
-            for s in range(WHOLE_PICKS, slots):
-                pick(s, starts[k], WIDTHS[k])
+            nc.vector.quantize_mx(out=sp_w[:, b, cols].bitcast(FP8X4), scales=sp_s[:, b, cols], in_=rounded[:])
 
         def inverse(b, k):
-            inv[b, k] = ring.tile([P, PACK, WIDTHS[k]], F32, name="stage", bufs=STAGE, align_bytes=64)
+            inv[b, k] = stage_tile([P, PACK, WIDTHS[k]], F32)
             for i in range(PACK):
                 s = PACK * b + i
                 nc.scalar.activation(
-                    inv[b, k][:, i, :], xg_all[b][:, i, cols_of(k)], ACT.Abs_reciprocal_sqrt,
+                    inv[b, k][:, i, :], xg[b, k][:, i, :], ACT.Abs_reciprocal_sqrt,
                     bias=half_signed[:, s : s + 1], scale=gain_inv[:, s : s + 1],
                 )
             nc.scalar.activation(inv[b, k][:], inv[b, k][:], ACT.Square)
 
         def saturate(b, k):
             if b == 0:
-                z_bf[k] = ring.tile([P, passes, WIDTHS[k] * PACK], BF16, name="z_bf", align_bytes=64)
+                z_bf[k] = ring.tile([P, passes, WIDTHS[k] * PACK], BF16, name="z_bf", align_bytes=ALIGN)
             nc.vector.tensor_tensor(
-                z_bf[k][:, b, :].rearrange("p (c e i) -> p c i e", e=2, i=PACK),
-                xg_all[b][:, :, cols_of(k)].rearrange("p i (c e) -> p c i e", e=2),
-                inv[b, k][:].rearrange("p i (c e) -> p c i e", e=2),
+                z_bf[k][:, b, :].rearrange("p (c e i) -> p c i e", e=PAIR, i=PACK),
+                xg[b, k].rearrange("p i (c e) -> p c i e", e=PAIR),
+                inv[b, k][:].rearrange("p i (c e) -> p c i e", e=PAIR),
                 ALU.mult,
             )
 
@@ -218,12 +219,12 @@ def tile_list_cochlear_spread_levels_kernel(
             )
 
         def levels(g, k):
-            w, cols = WIDTHS[k], cols_of(k)
-            per_bank = BANK // w
+            width, cols = WIDTHS[k], cols_of(k)
+            per_bank = BANK // width
             if g == 0:
-                y[k] = big.tile([P, groups, PACK, w], F32, name="big")
+                y[k] = keep.tile([P, groups, PACK, width], F32, name=y_home[k], align_bytes=ALIGN)
             for t0 in range(0, PACK, per_bank):
-                bank = psum.tile([P, per_bank, w], F32, name="bank")
+                bank = psum.tile([P, per_bank, width], F32, name="bank")
                 for t in range(t0, t0 + per_bank):
                     n_cols = slice(g * PASS + t * P, g * PASS + (t + 1) * P)
                     for b in range(passes):
@@ -239,15 +240,17 @@ def tile_list_cochlear_spread_levels_kernel(
                 limit = comfort_sb[:, PACK * g + t0 : PACK * g + t0 + per_bank]
                 nc.vector.tensor_tensor(
                     y[k][:, g, t0 : t0 + per_bank, :], bank[:],
-                    limit.unsqueeze(2).to_broadcast([P, per_bank, w]), ALU.min,
+                    limit.unsqueeze(2).to_broadcast([P, per_bank, width]), ALU.min,
                 )
             rows = out_0[g * PASS : (g + 1) * PASS, cols]
             nc.sync.dma_start(rows.rearrange("(p t) m -> p t m", t=PACK), y[k][:, g])
-            y_bf[g, k] = ring.tile([P, w * PACK], BF16, name="y_bf", align_bytes=64)
-            cast = nc.vector.tensor_copy if groups * (chunks - k) - g <= YV else nc.scalar.copy
-            cast(
-                y_bf[g, k][:].rearrange("p (c e t) -> p c t e", e=2, t=PACK),
-                y[k][:, g].rearrange("p t (c e) -> p c t e", e=2),
+
+        def round_y(g, k):
+            y_bf[g, k] = ring.tile([P, WIDTHS[k] * PACK], BF16, name="y_bf", align_bytes=ALIGN)
+            copy = nc.vector.tensor_copy if (g, k) == (groups - 1, chunks - 1) else nc.scalar.copy
+            copy(
+                y_bf[g, k][:].rearrange("p (c e t) -> p c t e", e=PAIR, t=PACK),
+                y[k][:, g].rearrange("p t (c e) -> p c t e", e=PAIR),
             )
 
         def quantise_y(g, k):
@@ -259,20 +262,29 @@ def tile_list_cochlear_spread_levels_kernel(
                     y_w[:, :, cols].bitcast(I32),
                 )
 
-        pairs = [(b, g) for g in range(groups) for b in range(passes)]
-        for b, g in pairs[:FIRST]:
-            round_spread(b, g)
-            quantise_spread(b, g)
+        for b in range(passes):
+            quantise_spread(b, 0, nc.vector.tensor_copy)
+        quantise_spread(0, 1, nc.scalar.copy)
+
+        xg_high = keep.tile([P, PACK, M - HALF], F32, name="spread_raw01", align_bytes=ALIGN)
+        for i in range(PACK):
+            pick(PACK + i, xg_high[:, i, :], HALF, M - HALF)
+        for k in range(chunks):
+            xg[0, k] = xg_first[:, :, cols_of(k)]
+            if starts[k] < HALF:
+                xg[1, k] = xg_low[:, :, cols_of(k)]
+            else:
+                xg[1, k] = xg_high[:, :, starts[k] - HALF : starts[k] - HALF + WIDTHS[k]]
+
         for k in range(LEAD):
             inverse(0, k)
-        for b, g in pairs[FIRST:]:
-            round_spread(b, g)
-            quantise_spread(b, g)
         for k in range(chunks + AHEAD):
             done = k - AHEAD
             if k < chunks:
                 inverse(1, k)
                 saturate(0, k)
+            if k == 0:
+                quantise_spread(1, 1, nc.scalar.copy)
             if done >= 0:
                 levels(0, done)
             if k + LEAD < chunks:
@@ -284,9 +296,12 @@ def tile_list_cochlear_spread_levels_kernel(
             if k < chunks:
                 quantise_z(k)
             if done >= 0:
-                quantise_y(0, done)
-                quantise_y(1, done)
-        for q in range(4):
+                for g in range(groups):
+                    round_y(g, done)
+                for g in range(groups):
+                    quantise_y(g, done)
+
+        for q in range(QUADRANTS):
             nc.scalar.dma_start(
                 out_2[:, 4 * q : 4 * q + 4, :].rearrange("g r m -> r g m").bitcast(I32),
                 y_s[32 * q : 32 * q + 4].bitcast(I32),

@@ -23,6 +23,7 @@ QUADRANTS = 4
 BANK = 512
 PER_COL = 16
 PAIR = 2
+RUN = 4
 ALIGN = 64
 
 WIDTHS = (256, 256, 256, 128, 128)
@@ -205,9 +206,9 @@ def tile_list_cochlear_spread_levels_kernel(
             if b == 0:
                 z_bf[k] = ring.tile([P, passes, WIDTHS[k] * PACK], BF16, name="z_bf", align_bytes=ALIGN)
             nc.vector.tensor_tensor(
-                z_bf[k][:, b, :].rearrange("p (c e i) -> p c i e", e=PAIR, i=PACK),
-                xg[b, k].rearrange("p i (c e) -> p c i e", e=PAIR),
-                inv[b, k][:].rearrange("p i (c e) -> p c i e", e=PAIR),
+                z_bf[k][:, b, :].rearrange("p (c e i) -> p c i e", e=RUN, i=PACK),
+                xg[b, k].rearrange("p i (c e) -> p c i e", e=RUN),
+                inv[b, k][:].rearrange("p i (c e) -> p c i e", e=RUN),
                 ALU.mult,
             )
 
@@ -249,8 +250,8 @@ def tile_list_cochlear_spread_levels_kernel(
             y_bf[g, k] = ring.tile([P, WIDTHS[k] * PACK], BF16, name="y_bf", align_bytes=ALIGN)
             copy = nc.vector.tensor_copy if (g, k) == (groups - 1, chunks - 1) else nc.scalar.copy
             copy(
-                y_bf[g, k][:].rearrange("p (c e t) -> p c t e", e=PAIR, t=PACK),
-                y[k][:, g].rearrange("p t (c e) -> p c t e", e=PAIR),
+                y_bf[g, k][:].rearrange("p (c e t) -> p c t e", e=RUN, t=PACK),
+                y[k][:, g].rearrange("p t (c e) -> p c t e", e=RUN),
             )
 
         def quantise_y(g, k):

@@ -24,6 +24,7 @@ BANK = 512
 PER_COL = 16
 PAIR = 2
 RUN = 4
+SPAN = BANK // PACK
 ALIGN = 64
 
 WIDTHS = (256, 256, 256, 128, 128)
@@ -32,7 +33,7 @@ ZEROED_BY_VECTOR = 256
 WEIGHTS_BY_SCALAR = 5
 EARLY_SLOTS = 2
 LEAD = 2
-AHEAD = 2
+AHEAD = 1
 ROOT_CAP = 2.0**60
 
 
@@ -77,40 +78,45 @@ def tile_list_cochlear_spread_levels_kernel(
                 tile[:].rearrange("p (a i) -> p a i", i=PACK), vector.rearrange("(a p i) -> p a i", p=P, i=PACK)
             )
 
-        def load_scale_rows(tile, rows):
+        def load_scale_rows(queue, tile, rows):
             for q in range(QUADRANTS):
-                nc.sync.dma_start(tile[32 * q : 32 * q + 4, :].bitcast(I32), rows[4 * q : 4 * q + 4, :].bitcast(I32))
+                queue.dma_start(tile[32 * q : 32 * q + 4, :].bitcast(I32), rows[4 * q : 4 * q + 4, :].bitcast(I32))
 
+        nc.sync.dma_start(w1_w_raw[:].bitcast(I32), w1_words[0].bitcast(I32))
         nc.sync.dma_start(idx[:], offs)
-        nc.sync.dma_start(idx2[:], offs2)
         load_by_slot(gain_sb, gain)
+        load_scale_rows(nc.sync, tab_s, tab_scales[0])
+        nc.sync.dma_start(wgt_sb[:], wgt)
+        load_scale_rows(nc.sync, w1_s_raw, w1_scales[0])
+        nc.sync.dma_start(tab_w[:].bitcast(I32), tab_words[0].rearrange("p t i -> p (t i)").bitcast(I32))
+        nc.sync.dma_start(idx2[:], offs2)
         load_by_slot(half_sb, half)
         load_by_slot(comfort_sb, comfort)
-        load_scale_rows(tab_s, tab_scales[0])
-        nc.sync.dma_start(wgt_sb[:], wgt)
-        nc.sync.dma_start(w1_w_raw[:].bitcast(I32), w1_words[0].bitcast(I32))
-        load_scale_rows(w1_s_raw, w1_scales[0])
-        nc.sync.dma_start(tab_w[:].bitcast(I32), tab_words[0].rearrange("p t i -> p (t i)").bitcast(I32))
         spread_raw = {}
         for g in range(groups):
             for b in range(passes):
-                raw = keep.tile([P, PACK, PASS], F32, name="spread_raw%d%d" % (b, g), align_bytes=ALIGN)
-                rows = spread[b * PASS : (b + 1) * PASS, g * PASS : (g + 1) * PASS]
-                nc.sync.dma_start(raw[:], rows.rearrange("(p j) n -> p j n", j=PACK))
-                spread_raw[b, g] = raw
+                parts = 2 if (b, g) == (0, 0) else 1
+                width = PASS // parts
+                spread_raw[b, g] = []
+                for part in range(parts):
+                    raw = keep.tile([P, PACK, width], F32, name="spread_raw%d%d%d" % (b, g, part), align_bytes=ALIGN)
+                    n0 = g * PASS + part * width
+                    rows = spread[b * PASS : (b + 1) * PASS, n0 : n0 + width]
+                    nc.sync.dma_start(raw[:], rows.rearrange("(p j) n -> p j n", j=PACK))
+                    spread_raw[b, g].append(raw)
 
         v_s = [keep.tile([P, BANK], U8, name="v_s%d" % c, align_bytes=ALIGN) for c in range(pieces)]
         v_w = [keep.tile([P, BANK], U32, name="v_w%d" % c, align_bytes=ALIGN) for c in range(pieces)]
         piece_cols = [slice(c * BANK // PER_COL, (c + 1) * BANK // PER_COL) for c in range(pieces)]
+        nc.vector.tensor_copy(
+            w1_w[:].bitcast(U16).rearrange("p (b i m) -> p b i m", b=passes, i=PACK),
+            w1_w_raw[:].bitcast(U16).rearrange("p (b m i) -> p b i m", b=passes, i=PACK),
+        )
         for c in range(pieces):
             nc.vector.tensor_copy(v_s[c][:], tab_s[:].indirect(idx[:, piece_cols[c]]))
         nc.vector.tensor_copy(
             w1_s[:].rearrange("p (b i m) -> p b i m", b=passes, i=PACK),
             w1_s_raw[:].rearrange("p (b m i) -> p b i m", b=passes, i=PACK),
-        )
-        nc.vector.tensor_copy(
-            w1_w[:].bitcast(U16).rearrange("p (b i m) -> p b i m", b=passes, i=PACK),
-            w1_w_raw[:].bitcast(U16).rearrange("p (b m i) -> p b i m", b=passes, i=PACK),
         )
 
         root = keep.tile([P, slots], F32, name="root")
@@ -118,18 +124,24 @@ def tile_list_cochlear_spread_levels_kernel(
         sign = keep.tile([P, slots], F32, name="sign")
         half_signed = keep.tile([P, slots], F32, name="half_signed")
         nc.scalar.activation(root[:], gain_sb[:], ACT.Abs_reciprocal_sqrt)
-        weights = []
+        nc.gpsimd.tensor_scalar(root[:], root[:], ROOT_CAP, 0.0, ALU.min, ALU.add)
+        nc.gpsimd.tensor_tensor(gain_inv[:], root[:], root[:], ALU.mult)
+        nc.gpsimd.tensor_scalar(sign[:], gain_sb[:], 0.0, 0.5, ALU.is_ge, ALU.subtract)
+        nc.gpsimd.tensor_scalar(sign[:], sign[:], 2.0, 0.0, ALU.mult, ALU.add)
+        nc.gpsimd.tensor_tensor(half_signed[:], sign[:], half_sb[:], ALU.mult)
+        weights = {}
         for s in range(slots):
-            scaled = keep.tile([P, M], F32, name="weights%d" % s, align_bytes=ALIGN)
-            if s < WEIGHTS_BY_SCALAR:
-                nc.scalar.activation(scaled[:], wgt_sb[:], ACT.Copy, scale=gain_sb[:, s : s + 1])
-            else:
-                nc.gpsimd.tensor_scalar(scaled[:], wgt_sb[:], gain_sb[:, s : s + 1], 0.0, ALU.mult, ALU.add)
-            weights.append(scaled)
-        nc.vector.tensor_scalar(root[:], root[:], ROOT_CAP, None, ALU.min)
-        nc.vector.tensor_scalar(sign[:], gain_sb[:], 0.0, 0.5, ALU.is_ge, ALU.subtract)
-        nc.vector.tensor_tensor(gain_inv[:], root[:], root[:], ALU.mult)
-        nc.vector.scalar_tensor_tensor(half_signed[:], sign[:], 2.0, half_sb[:], ALU.mult, ALU.mult)
+            for m0, width in ((0, M),) if s < slots - 1 else ((0, HALF), (HALF, M - HALF)):
+                scaled = keep.tile([P, width], F32, name="weights%d_%d" % (s, m0), align_bytes=ALIGN)
+                if s < WEIGHTS_BY_SCALAR:
+                    nc.scalar.activation(scaled[:], wgt_sb[:, m0 : m0 + width], ACT.Copy, scale=gain_sb[:, s : s + 1])
+                else:
+                    nc.gpsimd.tensor_scalar(
+                        scaled[:], wgt_sb[:, m0 : m0 + width], gain_sb[:, s : s + 1], 0.0, ALU.mult, ALU.add
+                    )
+                weights[s, m0] = scaled[:]
+            if s < slots - 1:
+                weights[s, HALF] = weights[s, 0][:, HALF:]
 
         for c in range(pieces):
             nc.vector.tensor_copy(v_w[c][:], tab_w[:].indirect(idx[:, piece_cols[c]]))
@@ -153,7 +165,7 @@ def tile_list_cochlear_spread_levels_kernel(
 
         def pick(s, out, m0, width):
             entries = idx2[:, m0 // PER_COL : (m0 + width) // PER_COL]
-            nc.vector.tensor_tensor(out, h[s][:].indirect(entries), weights[s][:, m0 : m0 + width], ALU.mult)
+            nc.vector.tensor_tensor(out, h[s][:].indirect(entries), weights[s, m0][:, :width], ALU.mult)
 
         for c in range(pieces):
             for s in range(EARLY_SLOTS):
@@ -167,6 +179,9 @@ def tile_list_cochlear_spread_levels_kernel(
                 pick(s, xg_first[:, s, :], 0, M)
             else:
                 pick(s, xg_low[:, s - PACK, :], 0, HALF)
+        xg_high = keep.tile([P, PACK, M - HALF], F32, name="weights%d_0" % (slots - 1), align_bytes=ALIGN)
+        for i in range(PACK):
+            pick(PACK + i, xg_high[:, i, :], HALF, M - HALF)
 
         sp_w = keep.tile([P, passes, N], U32, name="sp_w", align_bytes=ALIGN)
         sp_s = keep.tile([P, passes, N], U8, name="sp_s", align_bytes=ALIGN)
@@ -174,33 +189,52 @@ def tile_list_cochlear_spread_levels_kernel(
         z_s = [keep.tile([P, passes, w], U8, name="z_s%d" % k, align_bytes=ALIGN) for k, w in enumerate(WIDTHS)]
         y_w = keep.tile([P, groups, M], U32, name="y_w", align_bytes=ALIGN)
         y_s = keep.tile([P, groups, M], U8, name="y_s", align_bytes=ALIGN)
-        y_home = ("spread_raw00", "spread_raw10", "tab_w", "spread_raw11", "weights0")
+        y_home = ("spread_raw100", "tab_w", "spread_raw110", "spread_raw010", "spread_raw000")
         xg, inv, z_bf, y, y_bf = {}, {}, {}, {}, {}
 
         def cols_of(k):
             return slice(starts[k], starts[k] + WIDTHS[k])
 
-        def stage_tile(shape, dtype):
-            return ring.tile(shape, dtype, name="stage", bufs=2 * passes + 1, align_bytes=ALIGN)
+        for k in range(chunks):
+            xg[0, k] = xg_first[:, :, cols_of(k)]
+            if starts[k] < HALF:
+                xg[1, k] = xg_low[:, :, cols_of(k)]
+            else:
+                xg[1, k] = xg_high[:, :, starts[k] - HALF : starts[k] - HALF + WIDTHS[k]]
 
-        def quantise_spread(b, g, copy):
-            rounded = stage_tile([P, PASS * PACK], BF16)
-            copy(
-                rounded[:].rearrange("p (u e m j) -> p u m j e", u=PACK // PAIR, e=PAIR, j=PACK),
-                spread_raw[b, g][:].rearrange("p j (m u e) -> p u m j e", u=PACK // PAIR, e=PAIR),
-            )
+        def quantise_spread(b, g, engine):
+            rounded = ring.tile([P, PASS * PACK], BF16, name="rounded", bufs=2, align_bytes=ALIGN)
+            if engine == "gpsimd":
+                dealt = rounded[:].rearrange("p (t m j) -> p t m j", t=PACK, j=PACK)
+                for part, raw in enumerate(spread_raw[b, g]):
+                    width = P // len(spread_raw[b, g])
+                    nc.gpsimd.tensor_scalar(
+                        dealt[:, :, part * width : (part + 1) * width, :],
+                        raw[:].rearrange("p j (m t) -> p t m j", t=PACK),
+                        1.0, 0.0, ALU.mult, ALU.add,
+                    )
+            else:
+                copy = nc.vector.tensor_copy if engine == "vector" else nc.scalar.copy
+                copy(
+                    rounded[:].rearrange("p (u e m j) -> p u m j e", u=PACK // PAIR, e=PAIR, j=PACK),
+                    spread_raw[b, g][0][:].rearrange("p j (m u e) -> p u m j e", u=PACK // PAIR, e=PAIR),
+                )
             cols = slice(g * PASS, (g + 1) * PASS)
             nc.vector.quantize_mx(out=sp_w[:, b, cols].bitcast(FP8X4), scales=sp_s[:, b, cols], in_=rounded[:])
 
         def inverse(b, k):
-            inv[b, k] = stage_tile([P, PACK, WIDTHS[k]], F32)
+            home = "weights%d_0" % ((passes * k + b) % PACK)
+            inv[b, k] = keep.tile([P, PACK, WIDTHS[k]], F32, name=home, align_bytes=ALIGN)
+            roots = inv[b, k]
+            if b == passes - 1 and k > 0:
+                roots = keep.tile([P, PACK, WIDTHS[k]], F32, name=y_home[k - 1], align_bytes=ALIGN)
             for i in range(PACK):
                 s = PACK * b + i
                 nc.scalar.activation(
-                    inv[b, k][:, i, :], xg[b, k][:, i, :], ACT.Abs_reciprocal_sqrt,
+                    roots[:, i, :], xg[b, k][:, i, :], ACT.Abs_reciprocal_sqrt,
                     bias=half_signed[:, s : s + 1], scale=gain_inv[:, s : s + 1],
                 )
-            nc.scalar.activation(inv[b, k][:], inv[b, k][:], ACT.Square)
+            nc.scalar.activation(inv[b, k][:], roots[:], ACT.Square)
 
         def saturate(b, k):
             if b == 0:
@@ -219,31 +253,30 @@ def tile_list_cochlear_spread_levels_kernel(
                 in_=z_bf[k][:].rearrange("p b m -> p (b m)"),
             )
 
-        def levels(g, k):
-            width, cols = WIDTHS[k], cols_of(k)
-            per_bank = BANK // width
-            if g == 0:
-                y[k] = keep.tile([P, groups, PACK, width], F32, name=y_home[k], align_bytes=ALIGN)
-            for t0 in range(0, PACK, per_bank):
-                bank = psum.tile([P, per_bank, width], F32, name="bank")
-                for t in range(t0, t0 + per_bank):
-                    n_cols = slice(g * PASS + t * P, g * PASS + (t + 1) * P)
-                    for b in range(passes):
-                        nc.tensor.matmul_mx(
-                            out=bank[:, t - t0, :],
-                            lhsT=sp_w[:, b, n_cols].bitcast(FP8X4),
-                            lhsT_scale=sp_s[:, b, n_cols],
-                            rhs=z_w[k][:, b, :].bitcast(FP8X4),
-                            rhs_scale=z_s[k][:, b, :],
-                            start=(b == 0),
-                            stop=(b == passes - 1),
-                        )
-                limit = comfort_sb[:, PACK * g + t0 : PACK * g + t0 + per_bank]
-                nc.vector.tensor_tensor(
-                    y[k][:, g, t0 : t0 + per_bank, :], bank[:],
-                    limit.unsqueeze(2).to_broadcast([P, per_bank, width]), ALU.min,
-                )
-            rows = out_0[g * PASS : (g + 1) * PASS, cols]
+        def levels(g, k, part):
+            cols = slice(part * SPAN, (part + 1) * SPAN)
+            if (g, part) == (0, 0):
+                y[k] = keep.tile([P, groups, PACK, WIDTHS[k]], F32, name=y_home[k], align_bytes=ALIGN)
+            bank = psum.tile([P, PACK, SPAN], F32, name="bank")
+            for t in range(PACK):
+                n_cols = slice(g * PASS + t * P, g * PASS + (t + 1) * P)
+                for b in range(passes):
+                    nc.tensor.matmul_mx(
+                        out=bank[:, t, :],
+                        lhsT=sp_w[:, b, n_cols].bitcast(FP8X4),
+                        lhsT_scale=sp_s[:, b, n_cols],
+                        rhs=z_w[k][:, b, cols].bitcast(FP8X4),
+                        rhs_scale=z_s[k][:, b, cols],
+                        start=(b == 0),
+                        stop=(b == passes - 1),
+                    )
+            limit = comfort_sb[:, PACK * g : PACK * (g + 1)]
+            nc.vector.tensor_tensor(
+                y[k][:, g, :, cols], bank[:], limit.unsqueeze(2).to_broadcast([P, PACK, SPAN]), ALU.min
+            )
+
+        def store_y(g, k):
+            rows = out_0[g * PASS : (g + 1) * PASS, cols_of(k)]
             nc.sync.dma_start(rows.rearrange("(p t) m -> p t m", t=PACK), y[k][:, g])
 
         def round_y(g, k):
@@ -263,44 +296,36 @@ def tile_list_cochlear_spread_levels_kernel(
                     y_w[:, :, cols].bitcast(I32),
                 )
 
-        for b in range(passes):
-            quantise_spread(b, 0, nc.vector.tensor_copy)
-        quantise_spread(0, 1, nc.scalar.copy)
+        quantise_spread(0, 0, "gpsimd")
+        quantise_spread(1, 0, "vector")
 
-        xg_high = keep.tile([P, PACK, M - HALF], F32, name="spread_raw01", align_bytes=ALIGN)
-        for i in range(PACK):
-            pick(PACK + i, xg_high[:, i, :], HALF, M - HALF)
-        for k in range(chunks):
-            xg[0, k] = xg_first[:, :, cols_of(k)]
-            if starts[k] < HALF:
-                xg[1, k] = xg_low[:, :, cols_of(k)]
-            else:
-                xg[1, k] = xg_high[:, :, starts[k] - HALF : starts[k] - HALF + WIDTHS[k]]
+        def outputs(k):
+            for g in range(groups):
+                for part in range(WIDTHS[k] // SPAN):
+                    levels(g, k, part)
+                store_y(g, k)
 
-        for k in range(LEAD):
-            inverse(0, k)
-        for k in range(chunks + AHEAD):
-            done = k - AHEAD
+        for k in range(chunks + 2):
+            last = k == chunks - 1
             if k < chunks:
-                inverse(1, k)
-                saturate(0, k)
+                for b in range(passes):
+                    inverse(b, k)
+                    saturate(b, k)
             if k == 0:
-                quantise_spread(1, 1, nc.scalar.copy)
-            if done >= 0:
-                levels(0, done)
-            if k + LEAD < chunks:
-                inverse(0, k + LEAD)
-            if k < chunks:
-                saturate(1, k)
-            if done >= 0:
-                levels(1, done)
-            if k < chunks:
+                quantise_spread(0, 1, "scalar")
+            if k == 0:
+                quantise_spread(1, 1, "vector")
+            if last:
                 quantise_z(k)
-            if done >= 0:
+            if 0 <= k - 1 < chunks:
+                outputs(k - 1)
+            if k < chunks and not last:
+                quantise_z(k)
+            if 0 <= k - 2 < chunks:
                 for g in range(groups):
-                    round_y(g, done)
+                    round_y(g, k - 2)
                 for g in range(groups):
-                    quantise_y(g, done)
+                    quantise_y(g, k - 2)
 
         for q in range(QUADRANTS):
             nc.scalar.dma_start(

@@ -19,7 +19,7 @@ ALU = mybir.AluOpType
 P = 128
 PACK = 4
 PASS = P * PACK
-QUADRANTS = 4
+ROWS = 4
 BANK = 512
 PER_COL = 16
 PAIR = 2
@@ -33,7 +33,7 @@ ZEROED_BY_VECTOR = 256
 WEIGHTS_BY_SCALAR = 5
 EARLY_SLOTS = 2
 LEAD = 2
-AHEAD = 1
+ROUNDED_BY_GPSIMD = (0, 0)
 ROOT_CAP = 2.0**60
 
 
@@ -79,14 +79,14 @@ def tile_list_cochlear_spread_levels_kernel(
             )
 
         def load_scale_rows(queue, tile, rows):
-            for q in range(QUADRANTS):
-                queue.dma_start(tile[32 * q : 32 * q + 4, :].bitcast(I32), rows[4 * q : 4 * q + 4, :].bitcast(I32))
+            for r in range(ROWS):
+                queue.dma_start(tile[r:P:32, :].bitcast(I32), rows[r::ROWS, :].bitcast(I32))
 
-        nc.sync.dma_start(w1_w_raw[:].bitcast(I32), w1_words[0].bitcast(I32))
         nc.sync.dma_start(idx[:], offs)
-        load_by_slot(gain_sb, gain)
         load_scale_rows(nc.sync, tab_s, tab_scales[0])
+        load_by_slot(gain_sb, gain)
         nc.sync.dma_start(wgt_sb[:], wgt)
+        nc.sync.dma_start(w1_w_raw[:].bitcast(I32), w1_words[0].bitcast(I32))
         load_scale_rows(nc.sync, w1_s_raw, w1_scales[0])
         nc.sync.dma_start(tab_w[:].bitcast(I32), tab_words[0].rearrange("p t i -> p (t i)").bitcast(I32))
         nc.sync.dma_start(idx2[:], offs2)
@@ -205,12 +205,12 @@ def tile_list_cochlear_spread_levels_kernel(
         def quantise_spread(b, g, engine):
             rounded = ring.tile([P, PASS * PACK], BF16, name="rounded", bufs=2, align_bytes=ALIGN)
             if engine == "gpsimd":
-                dealt = rounded[:].rearrange("p (t m j) -> p t m j", t=PACK, j=PACK)
+                dealt = rounded[:].rearrange("p (t m j) -> p m t j", t=PACK, j=PACK)
                 for part, raw in enumerate(spread_raw[b, g]):
                     width = P // len(spread_raw[b, g])
                     nc.gpsimd.tensor_scalar(
-                        dealt[:, :, part * width : (part + 1) * width, :],
-                        raw[:].rearrange("p j (m t) -> p t m j", t=PACK),
+                        dealt[:, part * width : (part + 1) * width],
+                        raw[:].rearrange("p j (m t) -> p m t j", t=PACK),
                         1.0, 0.0, ALU.mult, ALU.add,
                     )
             else:
@@ -280,11 +280,18 @@ def tile_list_cochlear_spread_levels_kernel(
             nc.sync.dma_start(rows.rearrange("(p t) m -> p t m", t=PACK), y[k][:, g])
 
         def round_y(g, k):
-            y_bf[g, k] = ring.tile([P, WIDTHS[k] * PACK], BF16, name="y_bf", align_bytes=ALIGN)
+            y_bf[g, k] = ring.tile([P, WIDTHS[k] * PACK], BF16, name="y_bf", bufs=4, align_bytes=ALIGN)
+            lo = ROUNDED_BY_GPSIMD[g] if WIDTHS[k] > SPAN else 0
+            if lo:
+                nc.gpsimd.tensor_scalar(
+                    y_bf[g, k][:, : lo * PACK].rearrange("p (m t) -> p m t", t=PACK),
+                    y[k][:, g, :, :lo].rearrange("p t m -> p m t"),
+                    1.0, 0.0, ALU.mult, ALU.add,
+                )
             copy = nc.vector.tensor_copy if (g, k) == (groups - 1, chunks - 1) else nc.scalar.copy
             copy(
-                y_bf[g, k][:].rearrange("p (c e t) -> p c t e", e=RUN, t=PACK),
-                y[k][:, g].rearrange("p t (c e) -> p c t e", e=RUN),
+                y_bf[g, k][:, lo * PACK :].rearrange("p (c e t) -> p c t e", e=RUN, t=PACK),
+                y[k][:, g, :, lo:].rearrange("p t (c e) -> p c t e", e=RUN),
             )
 
         def quantise_y(g, k):
@@ -298,6 +305,13 @@ def tile_list_cochlear_spread_levels_kernel(
 
         quantise_spread(0, 0, "gpsimd")
         quantise_spread(1, 0, "vector")
+
+        def store_scales(queue, cols):
+            for r in range(ROWS):
+                queue.dma_start(
+                    out_2[:, r::ROWS, cols].rearrange("g q m -> q g m").bitcast(I32),
+                    y_s[r:P:32, :, cols].bitcast(I32),
+                )
 
         def outputs(k):
             for g in range(groups):
@@ -327,8 +341,4 @@ def tile_list_cochlear_spread_levels_kernel(
                 for g in range(groups):
                     quantise_y(g, k - 2)
 
-        for q in range(QUADRANTS):
-            nc.scalar.dma_start(
-                out_2[:, 4 * q : 4 * q + 4, :].rearrange("g r m -> r g m").bitcast(I32),
-                y_s[32 * q : 32 * q + 4].bitcast(I32),
-            )
+        store_scales(nc.scalar, slice(0, M))

@@ -33,7 +33,7 @@ ZEROED_BY_VECTOR = 256
 WEIGHTS_BY_SCALAR = 5
 EARLY_SLOTS = 2
 LEAD = 2
-ROUNDED_BY_GPSIMD = (0, 0)
+ROUNDED_BY_GPSIMD = 128
 ROOT_CAP = 2.0**60
 
 
@@ -281,13 +281,16 @@ def tile_list_cochlear_spread_levels_kernel(
 
         def round_y(g, k):
             y_bf[g, k] = ring.tile([P, WIDTHS[k] * PACK], BF16, name="y_bf", bufs=4, align_bytes=ALIGN)
-            lo = ROUNDED_BY_GPSIMD[g] if WIDTHS[k] > SPAN else 0
-            if lo:
+            lo = ROUNDED_BY_GPSIMD if g == 0 and WIDTHS[k] > SPAN else 0
+            for m0 in range(0, lo, SPAN):
+                m1 = min(lo, m0 + SPAN)
                 nc.gpsimd.tensor_scalar(
-                    y_bf[g, k][:, : lo * PACK].rearrange("p (m t) -> p m t", t=PACK),
-                    y[k][:, g, :, :lo].rearrange("p t m -> p m t"),
+                    y_bf[g, k][:, m0 * PACK : m1 * PACK].rearrange("p (m t) -> p m t", t=PACK),
+                    y[k][:, g, :, m0:m1].rearrange("p t m -> p m t"),
                     1.0, 0.0, ALU.mult, ALU.add,
                 )
+            if lo == WIDTHS[k]:
+                return
             copy = nc.vector.tensor_copy if (g, k) == (groups - 1, chunks - 1) else nc.scalar.copy
             copy(
                 y_bf[g, k][:, lo * PACK :].rearrange("p (c e t) -> p c t e", e=RUN, t=PACK),
@@ -327,8 +330,8 @@ def tile_list_cochlear_spread_levels_kernel(
                     saturate(b, k)
             if k == 0:
                 quantise_spread(0, 1, "scalar")
-            if k == 0:
-                quantise_spread(1, 1, "vector")
+            if k == 1:
+                quantise_spread(1, 1, "scalar")
             if last:
                 quantise_z(k)
             if 0 <= k - 1 < chunks:

@@ -29,6 +29,7 @@ ALIGN = 64
 
 WIDTHS = (256, 256, 256, 128, 128)
 HALF = M // 2
+WORD_GATHERS = (512, 512, 512, 512)
 ZEROED_BY_VECTOR = 256
 WEIGHTS_BY_SCALAR = 5
 EARLY_SLOTS = 2
@@ -105,15 +106,13 @@ def tile_list_cochlear_spread_levels_kernel(
                     nc.sync.dma_start(raw[:], rows.rearrange("(p j) n -> p j n", j=PACK))
                     spread_raw[b, g].append(raw)
 
-        v_s = [keep.tile([P, BANK], U8, name="v_s%d" % c, align_bytes=ALIGN) for c in range(pieces)]
-        v_w = [keep.tile([P, BANK], U32, name="v_w%d" % c, align_bytes=ALIGN) for c in range(pieces)]
-        piece_cols = [slice(c * BANK // PER_COL, (c + 1) * BANK // PER_COL) for c in range(pieces)]
+        v_s = keep.tile([P, S], U8, name="v_s", align_bytes=ALIGN)
+        v_w = keep.tile([P, S], U32, name="v_w", align_bytes=ALIGN)
         nc.vector.tensor_copy(
             w1_w[:].bitcast(U16).rearrange("p (b i m) -> p b i m", b=passes, i=PACK),
             w1_w_raw[:].bitcast(U16).rearrange("p (b m i) -> p b i m", b=passes, i=PACK),
         )
-        for c in range(pieces):
-            nc.vector.tensor_copy(v_s[c][:], tab_s[:].indirect(idx[:, piece_cols[c]]))
+        nc.vector.tensor_copy(v_s[:], tab_s[:].indirect(idx[:]))
         nc.vector.tensor_copy(
             w1_s[:].rearrange("p (b i m) -> p b i m", b=passes, i=PACK),
             w1_s_raw[:].rearrange("p (b m i) -> p b i m", b=passes, i=PACK),
@@ -143,8 +142,37 @@ def tile_list_cochlear_spread_levels_kernel(
             if s < slots - 1:
                 weights[s, HALF] = weights[s, 0][:, HALF:]
 
-        for c in range(pieces):
-            nc.vector.tensor_copy(v_w[c][:], tab_w[:].indirect(idx[:, piece_cols[c]]))
+        j0 = 0
+        for width in WORD_GATHERS:
+            entries = idx[:, j0 // PER_COL : (j0 + width) // PER_COL]
+            nc.vector.tensor_copy(v_w[:, j0 : j0 + width], tab_w[:].indirect(entries))
+            j0 = j0 + width
+
+        sp_w = keep.tile([P, passes, N], U32, name="sp_w", align_bytes=ALIGN)
+        sp_s = keep.tile([P, passes, N], U8, name="sp_s", align_bytes=ALIGN)
+
+        def quantise_spread(b, g, engine):
+            rounded = ring.tile([P, PASS * PACK], BF16, name="rounded", bufs=2, align_bytes=ALIGN)
+            if engine == "gpsimd":
+                dealt = rounded[:].rearrange("p (t m j) -> p m t j", t=PACK, j=PACK)
+                for part, raw in enumerate(spread_raw[b, g]):
+                    width = P // len(spread_raw[b, g])
+                    nc.gpsimd.tensor_scalar(
+                        dealt[:, part * width : (part + 1) * width],
+                        raw[:].rearrange("p j (m t) -> p m t j", t=PACK),
+                        1.0, 0.0, ALU.mult, ALU.add,
+                    )
+            else:
+                copy = nc.vector.tensor_copy if engine == "vector" else nc.scalar.copy
+                copy(
+                    rounded[:].rearrange("p (u e m j) -> p u m j e", u=PACK // PAIR, e=PAIR, j=PACK),
+                    spread_raw[b, g][0][:].rearrange("p j (m u e) -> p u m j e", u=PACK // PAIR, e=PAIR),
+                )
+            cols = slice(g * PASS, (g + 1) * PASS)
+            nc.vector.quantize_mx(out=sp_w[:, b, cols].bitcast(FP8X4), scales=sp_s[:, b, cols], in_=rounded[:])
+
+        quantise_spread(0, 0, "gpsimd")
+        quantise_spread(1, 0, "vector")
 
         h = [h_pool.tile([P, S], F32, name="h") for s in range(EARLY_SLOTS)]
         xg_first = keep.tile([P, PACK, M], F32, name="xg_first")
@@ -156,8 +184,8 @@ def tile_list_cochlear_spread_levels_kernel(
                 out=bank[:],
                 lhsT=w1_w[:, 2 * P * s : 2 * P * (s + 1)].bitcast(FP4X4),
                 lhsT_scale=w1_s[:, P * s : P * (s + 1)],
-                rhs=v_w[c][:].bitcast(FP8X4),
-                rhs_scale=v_s[c][:],
+                rhs=v_w[:, c * BANK : (c + 1) * BANK].bitcast(FP8X4),
+                rhs_scale=v_s[:, c * BANK : (c + 1) * BANK],
                 start=True,
                 stop=True,
             )
@@ -183,8 +211,6 @@ def tile_list_cochlear_spread_levels_kernel(
         for i in range(PACK):
             pick(PACK + i, xg_high[:, i, :], HALF, M - HALF)
 
-        sp_w = keep.tile([P, passes, N], U32, name="sp_w", align_bytes=ALIGN)
-        sp_s = keep.tile([P, passes, N], U8, name="sp_s", align_bytes=ALIGN)
         z_w = [keep.tile([P, passes, w], U32, name="z_w%d" % k, align_bytes=ALIGN) for k, w in enumerate(WIDTHS)]
         z_s = [keep.tile([P, passes, w], U8, name="z_s%d" % k, align_bytes=ALIGN) for k, w in enumerate(WIDTHS)]
         y_w = keep.tile([P, groups, M], U32, name="y_w", align_bytes=ALIGN)
@@ -202,31 +228,11 @@ def tile_list_cochlear_spread_levels_kernel(
             else:
                 xg[1, k] = xg_high[:, :, starts[k] - HALF : starts[k] - HALF + WIDTHS[k]]
 
-        def quantise_spread(b, g, engine):
-            rounded = ring.tile([P, PASS * PACK], BF16, name="rounded", bufs=2, align_bytes=ALIGN)
-            if engine == "gpsimd":
-                dealt = rounded[:].rearrange("p (t m j) -> p m t j", t=PACK, j=PACK)
-                for part, raw in enumerate(spread_raw[b, g]):
-                    width = P // len(spread_raw[b, g])
-                    nc.gpsimd.tensor_scalar(
-                        dealt[:, part * width : (part + 1) * width],
-                        raw[:].rearrange("p j (m t) -> p m t j", t=PACK),
-                        1.0, 0.0, ALU.mult, ALU.add,
-                    )
-            else:
-                copy = nc.vector.tensor_copy if engine == "vector" else nc.scalar.copy
-                copy(
-                    rounded[:].rearrange("p (u e m j) -> p u m j e", u=PACK // PAIR, e=PAIR, j=PACK),
-                    spread_raw[b, g][0][:].rearrange("p j (m u e) -> p u m j e", u=PACK // PAIR, e=PAIR),
-                )
-            cols = slice(g * PASS, (g + 1) * PASS)
-            nc.vector.quantize_mx(out=sp_w[:, b, cols].bitcast(FP8X4), scales=sp_s[:, b, cols], in_=rounded[:])
-
         def inverse(b, k):
             home = "weights%d_0" % ((passes * k + b) % PACK)
             inv[b, k] = keep.tile([P, PACK, WIDTHS[k]], F32, name=home, align_bytes=ALIGN)
             roots = inv[b, k]
-            if b == passes - 1 and k > 0:
+            if k > 0 and b == (0 if k == 1 else passes - 1):
                 roots = keep.tile([P, PACK, WIDTHS[k]], F32, name=y_home[k - 1], align_bytes=ALIGN)
             for i in range(PACK):
                 s = PACK * b + i
@@ -300,14 +306,13 @@ def tile_list_cochlear_spread_levels_kernel(
         def quantise_y(g, k):
             cols = cols_of(k)
             nc.vector.quantize_mx(out=y_w[:, g, cols].bitcast(FP8X4), scales=y_s[:, g, cols], in_=y_bf[g, k][:])
-            if g == groups - 1:
+            if g == groups - 1 and k != chunks - 2:
+                cols = slice(starts[min(k, chunks - 2)], cols.stop)
                 nc.sync.dma_start(
                     out_1[:, :, cols, :].rearrange("g p m t -> p g (m t)").bitcast(I32),
                     y_w[:, :, cols].bitcast(I32),
                 )
 
-        quantise_spread(0, 0, "gpsimd")
-        quantise_spread(1, 0, "vector")
 
         def store_scales(queue, cols):
             for r in range(ROWS):
@@ -328,13 +333,15 @@ def tile_list_cochlear_spread_levels_kernel(
                 for b in range(passes):
                     inverse(b, k)
                     saturate(b, k)
+                    if (b, k) == (0, 1):
+                        outputs(0)
             if k == 0:
                 quantise_spread(0, 1, "scalar")
-            if k == 1:
+            if k == 0:
                 quantise_spread(1, 1, "scalar")
             if last:
                 quantise_z(k)
-            if 0 <= k - 1 < chunks:
+            if 0 < k - 1 < chunks:
                 outputs(k - 1)
             if k < chunks and not last:
                 quantise_z(k)

@@ -34,6 +34,7 @@ ZEROED_BY_VECTOR = 256
 WEIGHTS_BY_SCALAR = 5
 EARLY_SLOTS = 2
 LEAD = 2
+SPREAD_BY_GPSIMD = 96
 ROUNDED_BY_GPSIMD = 128
 ROOT_CAP = 2.0**60
 
@@ -90,9 +91,6 @@ def tile_list_cochlear_spread_levels_kernel(
         nc.sync.dma_start(w1_w_raw[:].bitcast(I32), w1_words[0].bitcast(I32))
         load_scale_rows(nc.sync, w1_s_raw, w1_scales[0])
         nc.sync.dma_start(tab_w[:].bitcast(I32), tab_words[0].rearrange("p t i -> p (t i)").bitcast(I32))
-        nc.sync.dma_start(idx2[:], offs2)
-        load_by_slot(half_sb, half)
-        load_by_slot(comfort_sb, comfort)
         spread_raw = {}
         for g in range(groups):
             for b in range(passes):
@@ -105,6 +103,12 @@ def tile_list_cochlear_spread_levels_kernel(
                     rows = spread[b * PASS : (b + 1) * PASS, n0 : n0 + width]
                     nc.sync.dma_start(raw[:], rows.rearrange("(p j) n -> p j n", j=PACK))
                     spread_raw[b, g].append(raw)
+                    if (b, g, part) == (0, 0, 0):
+                        load_by_slot(half_sb, half)
+                    if (b, g, part) == (0, 0, 1):
+                        nc.sync.dma_start(idx2[:], offs2)
+                    if (b, g) == (1, 0):
+                        load_by_slot(comfort_sb, comfort)
 
         v_s = keep.tile([P, S], U8, name="v_s", align_bytes=ALIGN)
         v_w = keep.tile([P, S], U32, name="v_w", align_bytes=ALIGN)
@@ -148,31 +152,41 @@ def tile_list_cochlear_spread_levels_kernel(
             nc.vector.tensor_copy(v_w[:, j0 : j0 + width], tab_w[:].indirect(entries))
             j0 = j0 + width
 
-        sp_w = keep.tile([P, passes, N], U32, name="sp_w", align_bytes=ALIGN)
-        sp_s = keep.tile([P, passes, N], U8, name="sp_s", align_bytes=ALIGN)
+        sp_w = keep.tile([P, groups, passes, PASS], U32, name="sp_w", align_bytes=ALIGN)
+        sp_s = keep.tile([P, groups, passes, PASS], U8, name="sp_s", align_bytes=ALIGN)
 
-        def quantise_spread(b, g, engine):
-            rounded = ring.tile([P, PASS * PACK], BF16, name="rounded", bufs=2, align_bytes=ALIGN)
-            if engine == "gpsimd":
-                dealt = rounded[:].rearrange("p (t m j) -> p m t j", t=PACK, j=PACK)
-                for part, raw in enumerate(spread_raw[b, g]):
-                    width = P // len(spread_raw[b, g])
-                    nc.gpsimd.tensor_scalar(
-                        dealt[:, part * width : (part + 1) * width],
-                        raw[:].rearrange("p j (m t) -> p m t j", t=PACK),
-                        1.0, 0.0, ALU.mult, ALU.add,
-                    )
-            else:
-                copy = nc.vector.tensor_copy if engine == "vector" else nc.scalar.copy
-                copy(
-                    rounded[:].rearrange("p (u e m j) -> p u m j e", u=PACK // PAIR, e=PAIR, j=PACK),
-                    spread_raw[b, g][0][:].rearrange("p j (m u e) -> p u m j e", u=PACK // PAIR, e=PAIR),
+        rounded = {}
+
+        def round_spread(b, g, engine, m0, m1):
+            if g not in rounded:
+                rounded[g] = ring.tile([P, passes, PASS * PACK], BF16, name="rounded", bufs=1, align_bytes=ALIGN)
+            width = P // len(spread_raw[b, g])
+            raw = spread_raw[b, g][m0 // width][:, :, PACK * (m0 % width) : PACK * (m0 % width + m1 - m0)]
+            if engine is nc.gpsimd:
+                engine.tensor_scalar(
+                    rounded[g][:, b].rearrange("p (t m j) -> p m t j", t=PACK, j=PACK)[:, m0:m1],
+                    raw.rearrange("p j (m t) -> p m t j", t=PACK),
+                    1.0, 0.0, ALU.mult, ALU.add,
                 )
-            cols = slice(g * PASS, (g + 1) * PASS)
-            nc.vector.quantize_mx(out=sp_w[:, b, cols].bitcast(FP8X4), scales=sp_s[:, b, cols], in_=rounded[:])
+            else:
+                copy = engine.tensor_copy if engine is nc.vector else engine.copy
+                copy(
+                    rounded[g][:, b].rearrange("p (u e m j) -> p u m j e", u=PACK // PAIR, e=PAIR, j=PACK)[:, :, m0:m1],
+                    raw.rearrange("p j (m u e) -> p u m j e", u=PACK // PAIR, e=PAIR),
+                )
 
-        quantise_spread(0, 0, "gpsimd")
-        quantise_spread(1, 0, "vector")
+        def quantise_spread(g):
+            nc.vector.quantize_mx(
+                out=sp_w[:, g].rearrange("p b n -> p (b n)").bitcast(FP8X4),
+                scales=sp_s[:, g].rearrange("p b n -> p (b n)"),
+                in_=rounded[g][:].rearrange("p b n -> p (b n)"),
+            )
+
+        round_spread(0, 0, nc.gpsimd, 0, P // 2)
+        round_spread(0, 0, nc.gpsimd, P // 2, SPREAD_BY_GPSIMD)
+        round_spread(0, 0, nc.vector, SPREAD_BY_GPSIMD, P)
+        round_spread(1, 0, nc.vector, 0, P)
+        quantise_spread(0)
 
         h = [h_pool.tile([P, S], F32, name="h") for s in range(EARLY_SLOTS)]
         xg_first = keep.tile([P, PACK, M], F32, name="xg_first")
@@ -232,7 +246,7 @@ def tile_list_cochlear_spread_levels_kernel(
             home = "weights%d_0" % ((passes * k + b) % PACK)
             inv[b, k] = keep.tile([P, PACK, WIDTHS[k]], F32, name=home, align_bytes=ALIGN)
             roots = inv[b, k]
-            if k > 0 and b == (0 if k == 1 else passes - 1):
+            if b == passes - 1 and k > 0:
                 roots = keep.tile([P, PACK, WIDTHS[k]], F32, name=y_home[k - 1], align_bytes=ALIGN)
             for i in range(PACK):
                 s = PACK * b + i
@@ -265,12 +279,12 @@ def tile_list_cochlear_spread_levels_kernel(
                 y[k] = keep.tile([P, groups, PACK, WIDTHS[k]], F32, name=y_home[k], align_bytes=ALIGN)
             bank = psum.tile([P, PACK, SPAN], F32, name="bank")
             for t in range(PACK):
-                n_cols = slice(g * PASS + t * P, g * PASS + (t + 1) * P)
+                n_cols = slice(t * P, (t + 1) * P)
                 for b in range(passes):
                     nc.tensor.matmul_mx(
                         out=bank[:, t, :],
-                        lhsT=sp_w[:, b, n_cols].bitcast(FP8X4),
-                        lhsT_scale=sp_s[:, b, n_cols],
+                        lhsT=sp_w[:, g, b, n_cols].bitcast(FP8X4),
+                        lhsT_scale=sp_s[:, g, b, n_cols],
                         rhs=z_w[k][:, b, cols].bitcast(FP8X4),
                         rhs_scale=z_s[k][:, b, cols],
                         start=(b == 0),
@@ -306,8 +320,7 @@ def tile_list_cochlear_spread_levels_kernel(
         def quantise_y(g, k):
             cols = cols_of(k)
             nc.vector.quantize_mx(out=y_w[:, g, cols].bitcast(FP8X4), scales=y_s[:, g, cols], in_=y_bf[g, k][:])
-            if g == groups - 1 and k != chunks - 2:
-                cols = slice(starts[min(k, chunks - 2)], cols.stop)
+            if g == groups - 1:
                 nc.sync.dma_start(
                     out_1[:, :, cols, :].rearrange("g p m t -> p g (m t)").bitcast(I32),
                     y_w[:, :, cols].bitcast(I32),
@@ -333,15 +346,14 @@ def tile_list_cochlear_spread_levels_kernel(
                 for b in range(passes):
                     inverse(b, k)
                     saturate(b, k)
-                    if (b, k) == (0, 1):
-                        outputs(0)
             if k == 0:
-                quantise_spread(0, 1, "scalar")
-            if k == 0:
-                quantise_spread(1, 1, "scalar")
+                round_spread(0, 1, nc.scalar, 0, P)
+            if k == 1:
+                round_spread(1, 1, nc.scalar, 0, P)
+                quantise_spread(1)
             if last:
                 quantise_z(k)
-            if 0 < k - 1 < chunks:
+            if 0 <= k - 1 < chunks:
                 outputs(k - 1)
             if k < chunks and not last:
                 quantise_z(k)

@@ -31,11 +31,11 @@ WIDTHS = (256, 256, 256, 128, 128)
 HALF = M // 2
 WORD_GATHERS = (512, 512, 512, 512)
 ZEROED_BY_VECTOR = 256
-WEIGHTS_BY_SCALAR = 5
+WEIGHTS_BY_SCALAR = 6
 EARLY_SLOTS = 2
 LEAD = 2
 SPREAD_BY_GPSIMD = 96
-ROUNDED_BY_GPSIMD = 128
+ROUNDED_BY_GPSIMD = (128, 128, 64, 0, 0)
 ROOT_CAP = 2.0**60
 
 
@@ -301,7 +301,7 @@ def tile_list_cochlear_spread_levels_kernel(
 
         def round_y(g, k):
             y_bf[g, k] = ring.tile([P, WIDTHS[k] * PACK], BF16, name="y_bf", bufs=4, align_bytes=ALIGN)
-            lo = ROUNDED_BY_GPSIMD if g == 0 and WIDTHS[k] > SPAN else 0
+            lo = ROUNDED_BY_GPSIMD[k] if g == 0 else 0
             for m0 in range(0, lo, SPAN):
                 m1 = min(lo, m0 + SPAN)
                 nc.gpsimd.tensor_scalar(
@@ -346,10 +346,11 @@ def tile_list_cochlear_spread_levels_kernel(
                 for b in range(passes):
                     inverse(b, k)
                     saturate(b, k)
-            if k == 0:
-                round_spread(0, 1, nc.scalar, 0, P)
+                    if (b, k) == (0, 0):
+                        round_spread(0, 1, nc.scalar, 0, P)
             if k == 1:
-                round_spread(1, 1, nc.scalar, 0, P)
+                round_spread(1, 1, nc.vector, 0, 64)
+                round_spread(1, 1, nc.scalar, 64, P)
                 quantise_spread(1)
             if last:
                 quantise_z(k)

@@ -19,8 +19,10 @@ ALU = mybir.AluOpType
 P = 128
 PACK = 4
 PASS = P * PACK
+QUADRANT = 32
 ROWS = 4
 BANK = 512
+BANKS = 8
 PER_COL = 16
 PAIR = 2
 RUN = 4
@@ -29,13 +31,11 @@ ALIGN = 64
 
 WIDTHS = (256, 256, 256, 128, 128)
 HALF = M // 2
-WORD_GATHERS = (512, 512, 512, 512)
 ZEROED_BY_VECTOR = 256
 WEIGHTS_BY_SCALAR = 6
 EARLY_SLOTS = 2
-LEAD = 2
 SPREAD_BY_GPSIMD = 96
-ROUNDED_BY_GPSIMD = (128, 128, 64, 0, 0)
+ROUNDED_BY_GPSIMD = (SPAN, SPAN, SPAN // 2, 0, 0)
 ROOT_CAP = 2.0**60
 
 
@@ -56,7 +56,7 @@ def tile_list_cochlear_spread_levels_kernel(
         keep = ctx.enter_context(tc.tile_pool(name="keep", bufs=1))
         h_pool = ctx.enter_context(tc.tile_pool(name="h_pool", bufs=PACK + 1))
         ring = ctx.enter_context(tc.tile_pool(name="ring", bufs=3))
-        psum = ctx.enter_context(tc.psum_pool(name="psum", bufs=8))
+        psum = ctx.enter_context(tc.psum_pool(name="psum", bufs=BANKS))
 
         idx = lists.tile([P, S // PER_COL], U16, name="idx")
         idx2 = lists.tile([P, M // PER_COL], U16, name="idx2")
@@ -80,16 +80,16 @@ def tile_list_cochlear_spread_levels_kernel(
                 tile[:].rearrange("p (a i) -> p a i", i=PACK), vector.rearrange("(a p i) -> p a i", p=P, i=PACK)
             )
 
-        def load_scale_rows(queue, tile, rows):
+        def load_scale_rows(tile, rows):
             for r in range(ROWS):
-                queue.dma_start(tile[r:P:32, :].bitcast(I32), rows[r::ROWS, :].bitcast(I32))
+                nc.sync.dma_start(tile[r:P:QUADRANT, :].bitcast(I32), rows[r::ROWS, :].bitcast(I32))
 
         nc.sync.dma_start(idx[:], offs)
-        load_scale_rows(nc.sync, tab_s, tab_scales[0])
+        load_scale_rows(tab_s, tab_scales[0])
         load_by_slot(gain_sb, gain)
         nc.sync.dma_start(wgt_sb[:], wgt)
         nc.sync.dma_start(w1_w_raw[:].bitcast(I32), w1_words[0].bitcast(I32))
-        load_scale_rows(nc.sync, w1_s_raw, w1_scales[0])
+        load_scale_rows(w1_s_raw, w1_scales[0])
         nc.sync.dma_start(tab_w[:].bitcast(I32), tab_words[0].rearrange("p t i -> p (t i)").bitcast(I32))
         spread_raw = {}
         for g in range(groups):
@@ -146,15 +146,12 @@ def tile_list_cochlear_spread_levels_kernel(
             if s < slots - 1:
                 weights[s, HALF] = weights[s, 0][:, HALF:]
 
-        j0 = 0
-        for width in WORD_GATHERS:
-            entries = idx[:, j0 // PER_COL : (j0 + width) // PER_COL]
-            nc.vector.tensor_copy(v_w[:, j0 : j0 + width], tab_w[:].indirect(entries))
-            j0 = j0 + width
+        for c in range(pieces):
+            entries = idx[:, c * BANK // PER_COL : (c + 1) * BANK // PER_COL]
+            nc.vector.tensor_copy(v_w[:, c * BANK : (c + 1) * BANK], tab_w[:].indirect(entries))
 
         sp_w = keep.tile([P, groups, passes, PASS], U32, name="sp_w", align_bytes=ALIGN)
         sp_s = keep.tile([P, groups, passes, PASS], U8, name="sp_s", align_bytes=ALIGN)
-
         rounded = {}
 
         def round_spread(b, g, engine, m0, m1):
@@ -297,20 +294,18 @@ def tile_list_cochlear_spread_levels_kernel(
 
         def store_y(g, k):
             rows = out_0[g * PASS : (g + 1) * PASS, cols_of(k)]
-            nc.sync.dma_start(rows.rearrange("(p t) m -> p t m", t=PACK), y[k][:, g])
+            queue = nc.scalar if (g, k) == (groups - 1, chunks - 1) else nc.sync
+            queue.dma_start(rows.rearrange("(p t) m -> p t m", t=PACK), y[k][:, g])
 
         def round_y(g, k):
-            y_bf[g, k] = ring.tile([P, WIDTHS[k] * PACK], BF16, name="y_bf", bufs=4, align_bytes=ALIGN)
+            y_bf[g, k] = ring.tile([P, WIDTHS[k] * PACK], BF16, name="y_bf", bufs=2 * groups, align_bytes=ALIGN)
             lo = ROUNDED_BY_GPSIMD[k] if g == 0 else 0
-            for m0 in range(0, lo, SPAN):
-                m1 = min(lo, m0 + SPAN)
+            if lo:
                 nc.gpsimd.tensor_scalar(
-                    y_bf[g, k][:, m0 * PACK : m1 * PACK].rearrange("p (m t) -> p m t", t=PACK),
-                    y[k][:, g, :, m0:m1].rearrange("p t m -> p m t"),
+                    y_bf[g, k][:, : lo * PACK].rearrange("p (m t) -> p m t", t=PACK),
+                    y[k][:, g, :, :lo].rearrange("p t m -> p m t"),
                     1.0, 0.0, ALU.mult, ALU.add,
                 )
-            if lo == WIDTHS[k]:
-                return
             copy = nc.vector.tensor_copy if (g, k) == (groups - 1, chunks - 1) else nc.scalar.copy
             copy(
                 y_bf[g, k][:, lo * PACK :].rearrange("p (c e t) -> p c t e", e=RUN, t=PACK),
@@ -321,17 +316,10 @@ def tile_list_cochlear_spread_levels_kernel(
             cols = cols_of(k)
             nc.vector.quantize_mx(out=y_w[:, g, cols].bitcast(FP8X4), scales=y_s[:, g, cols], in_=y_bf[g, k][:])
             if g == groups - 1:
-                nc.sync.dma_start(
+                queue = nc.scalar if k == chunks - 1 else nc.sync
+                queue.dma_start(
                     out_1[:, :, cols, :].rearrange("g p m t -> p g (m t)").bitcast(I32),
                     y_w[:, :, cols].bitcast(I32),
-                )
-
-
-        def store_scales(queue, cols):
-            for r in range(ROWS):
-                queue.dma_start(
-                    out_2[:, r::ROWS, cols].rearrange("g q m -> q g m").bitcast(I32),
-                    y_s[r:P:32, :, cols].bitcast(I32),
                 )
 
         def outputs(k):
@@ -349,8 +337,8 @@ def tile_list_cochlear_spread_levels_kernel(
                     if (b, k) == (0, 0):
                         round_spread(0, 1, nc.scalar, 0, P)
             if k == 1:
-                round_spread(1, 1, nc.vector, 0, 64)
-                round_spread(1, 1, nc.scalar, 64, P)
+                round_spread(1, 1, nc.vector, 0, P // 2)
+                round_spread(1, 1, nc.scalar, P // 2, P)
                 quantise_spread(1)
             if last:
                 quantise_z(k)
@@ -364,4 +352,8 @@ def tile_list_cochlear_spread_levels_kernel(
                 for g in range(groups):
                     quantise_y(g, k - 2)
 
-        store_scales(nc.scalar, slice(0, M))
+        for r in range(ROWS):
+            nc.scalar.dma_start(
+                out_2[:, r::ROWS, :].rearrange("g q m -> q g m").bitcast(I32),
+                y_s[r:P:QUADRANT].bitcast(I32),
+            )

@@ -35,7 +35,8 @@ ZEROED_BY_VECTOR = 256
 WEIGHTS_BY_SCALAR = 6
 EARLY_SLOTS = 2
 SPREAD_BY_GPSIMD = 96
-ROUNDED_BY_GPSIMD = (SPAN, SPAN, SPAN // 2, 0, 0)
+ROUNDED_BY_GPSIMD = (SPAN, 0, 0, 0, 0)
+WHOLE_BY_GPSIMD = 2
 ROOT_CAP = 2.0**60
 
 
@@ -155,35 +156,30 @@ def tile_list_cochlear_spread_levels_kernel(
         rounded = {}
 
         def round_spread(b, g, engine, m0, m1):
-            if g not in rounded:
-                rounded[g] = ring.tile([P, passes, PASS * PACK], BF16, name="rounded", bufs=1, align_bytes=ALIGN)
             width = P // len(spread_raw[b, g])
             raw = spread_raw[b, g][m0 // width][:, :, PACK * (m0 % width) : PACK * (m0 % width + m1 - m0)]
             if engine is nc.gpsimd:
                 engine.tensor_scalar(
-                    rounded[g][:, b].rearrange("p (t m j) -> p m t j", t=PACK, j=PACK)[:, m0:m1],
+                    rounded[b, g].rearrange("p (t m j) -> p m t j", t=PACK, j=PACK)[:, m0:m1],
                     raw.rearrange("p j (m t) -> p m t j", t=PACK),
                     1.0, 0.0, ALU.mult, ALU.add,
                 )
             else:
                 copy = engine.tensor_copy if engine is nc.vector else engine.copy
                 copy(
-                    rounded[g][:, b].rearrange("p (u e m j) -> p u m j e", u=PACK // PAIR, e=PAIR, j=PACK)[:, :, m0:m1],
+                    rounded[b, g].rearrange("p (u e m j) -> p u m j e", u=PACK // PAIR, e=PAIR, j=PACK)[:, :, m0:m1],
                     raw.rearrange("p j (m u e) -> p u m j e", u=PACK // PAIR, e=PAIR),
                 )
 
-        def quantise_spread(g):
-            nc.vector.quantize_mx(
-                out=sp_w[:, g].rearrange("p b n -> p (b n)").bitcast(FP8X4),
-                scales=sp_s[:, g].rearrange("p b n -> p (b n)"),
-                in_=rounded[g][:].rearrange("p b n -> p (b n)"),
-            )
+        def quantise_spread(b, g):
+            nc.vector.quantize_mx(out=sp_w[:, g, b].bitcast(FP8X4), scales=sp_s[:, g, b], in_=rounded[b, g])
 
+        for b, g in ((0, 0), (0, 1), (1, 1)):
+            rounded[b, g] = ring.tile([P, PASS * PACK], BF16, name="rounded", bufs=passes, align_bytes=ALIGN)[:]
         round_spread(0, 0, nc.gpsimd, 0, P // 2)
         round_spread(0, 0, nc.gpsimd, P // 2, SPREAD_BY_GPSIMD)
         round_spread(0, 0, nc.vector, SPREAD_BY_GPSIMD, P)
-        round_spread(1, 0, nc.vector, 0, P)
-        quantise_spread(0)
+        quantise_spread(0, 0)
 
         h = [h_pool.tile([P, S], F32, name="h") for s in range(EARLY_SLOTS)]
         xg_first = keep.tile([P, PACK, M], F32, name="xg_first")
@@ -216,6 +212,10 @@ def tile_list_cochlear_spread_levels_kernel(
                     band_response(s, c)
             if s < PACK:
                 pick(s, xg_first[:, s, :], 0, M)
+                if s == 0:
+                    rounded[1, 0] = weights[0, 0].bitcast(BF16)
+                    round_spread(1, 0, nc.vector, 0, P)
+                    quantise_spread(1, 0)
             else:
                 pick(s, xg_low[:, s - PACK, :], 0, HALF)
         xg_high = keep.tile([P, PACK, M - HALF], F32, name="weights%d_0" % (slots - 1), align_bytes=ALIGN)
@@ -298,7 +298,15 @@ def tile_list_cochlear_spread_levels_kernel(
             queue.dma_start(rows.rearrange("(p t) m -> p t m", t=PACK), y[k][:, g])
 
         def round_y(g, k):
-            y_bf[g, k] = ring.tile([P, WIDTHS[k] * PACK], BF16, name="y_bf", bufs=2 * groups, align_bytes=ALIGN)
+            if g == groups - 1 and k < WHOLE_BY_GPSIMD:
+                y_bf[g, k] = inv[passes - 1, k + 2][:].rearrange("p i m -> p (i m)").bitcast(BF16)[:, : WIDTHS[k] * PACK]
+                nc.gpsimd.tensor_scalar(
+                    y_bf[g, k].rearrange("p (m t) -> p m t", t=PACK),
+                    y[k][:, g].rearrange("p t m -> p m t"),
+                    1.0, 0.0, ALU.mult, ALU.add,
+                )
+                return
+            y_bf[g, k] = ring.tile([P, WIDTHS[k] * PACK], BF16, name="y_bf", bufs=2 * groups, align_bytes=ALIGN)[:]
             lo = ROUNDED_BY_GPSIMD[k] if g == 0 else 0
             if lo:
                 nc.gpsimd.tensor_scalar(
@@ -314,7 +322,7 @@ def tile_list_cochlear_spread_levels_kernel(
 
         def quantise_y(g, k):
             cols = cols_of(k)
-            nc.vector.quantize_mx(out=y_w[:, g, cols].bitcast(FP8X4), scales=y_s[:, g, cols], in_=y_bf[g, k][:])
+            nc.vector.quantize_mx(out=y_w[:, g, cols].bitcast(FP8X4), scales=y_s[:, g, cols], in_=y_bf[g, k])
             if g == groups - 1:
                 queue = nc.scalar if k == chunks - 1 else nc.sync
                 queue.dma_start(
@@ -337,9 +345,9 @@ def tile_list_cochlear_spread_levels_kernel(
                     if (b, k) == (0, 0):
                         round_spread(0, 1, nc.scalar, 0, P)
             if k == 1:
-                round_spread(1, 1, nc.vector, 0, P // 2)
-                round_spread(1, 1, nc.scalar, P // 2, P)
-                quantise_spread(1)
+                round_spread(1, 1, nc.scalar, 0, P)
+                quantise_spread(0, 1)
+                quantise_spread(1, 1)
             if last:
                 quantise_z(k)
             if 0 <= k - 1 < chunks:

@@ -32,11 +32,20 @@ ALIGN = 64
 WIDTHS = (256, 256, 256, 128, 128)
 HALF = M // 2
 ZEROED_BY_VECTOR = 256
-WEIGHTS_BY_SCALAR = 6
+WEIGHTS_BY_SCALAR = 5
+LAST_SPREAD_BY_VECTOR = 64
 EARLY_SLOTS = 2
 SPREAD_BY_GPSIMD = 96
-ROUNDED_BY_GPSIMD = (SPAN, 0, 0, 0, 0)
-WHOLE_BY_GPSIMD = 2
+ROUNDED_BY_GPSIMD = {(0, 0): 256, (1, 0): 256, (0, 1): 128}
+DUE = {1: [(0, 0)], 2: [(1, 0), (0, 1)], 3: [(1, 1), (0, 2), (1, 2)], 4: [(0, 3), (1, 3)], 5: [(0, 4), (1, 4)]}
+PLANES = {2: [(0, 0)], 3: [(1, 0)], 4: [(0, 1), (1, 1), (0, 2), (1, 2)], 5: [(0, 3), (1, 3)], 6: [(0, 4), (1, 4)]}
+KIB = 1024
+HOME = {
+    "h": 0, "tab_w": 40, "tab_s": 56, "w1_w_raw": 60, "w1_s_raw": 62, "w1_w": 63, "w1_s": 65, "v_s": 66,
+    "v_w": 68, "wgt": 76, "weights": 80, "spread": 112, "sp_w": 144, "sp_s": 152, "xg_first": 154,
+    "xg_low": 170, "xg_high": 178, "z_w": 186, "z_s": 194, "y_w": 196, "y_s": 204, "rounded": 206,
+    "z_bf": 218,
+}
 ROOT_CAP = 2.0**60
 
 
@@ -55,22 +64,24 @@ def tile_list_cochlear_spread_levels_kernel(
     with ExitStack() as ctx:
         lists = ctx.enter_context(tc.tile_pool(name="lists", bufs=1))
         keep = ctx.enter_context(tc.tile_pool(name="keep", bufs=1))
-        h_pool = ctx.enter_context(tc.tile_pool(name="h_pool", bufs=PACK + 1))
-        ring = ctx.enter_context(tc.tile_pool(name="ring", bufs=3))
+
+        def place(name, shape, dtype, home, shift=0, bufs=1):
+            return keep.tile(shape, dtype, name=name, bufs=bufs, align_bytes=ALIGN, offset=int((HOME[home] + shift) * KIB))
+
         psum = ctx.enter_context(tc.psum_pool(name="psum", bufs=BANKS))
 
         idx = lists.tile([P, S // PER_COL], U16, name="idx")
         idx2 = lists.tile([P, M // PER_COL], U16, name="idx2")
-        tab_w = keep.tile([P, T], U32, name="tab_w", align_bytes=ALIGN)
-        tab_s = keep.tile([P, T], U8, name="tab_s", align_bytes=ALIGN)
-        w1_w_raw = keep.tile([P, 2 * H], U8, name="w1_w_raw", align_bytes=ALIGN)
-        w1_s_raw = keep.tile([P, H], U8, name="w1_s_raw", align_bytes=ALIGN)
-        w1_w = keep.tile([P, 2 * H], U8, name="w1_w", align_bytes=ALIGN)
-        w1_s = keep.tile([P, H], U8, name="w1_s", align_bytes=ALIGN)
-        wgt_sb = keep.tile([P, M], F32, name="wgt_sb", align_bytes=ALIGN)
-        half_sb = keep.tile([P, slots], F32, name="half_sb")
-        gain_sb = keep.tile([P, slots], F32, name="gain_sb")
-        comfort_sb = keep.tile([P, groups * PACK], F32, name="comfort_sb")
+        tab_w = place("tab_w", [P, T], U32, "tab_w")
+        tab_s = place("tab_s", [P, T], U8, "tab_s")
+        w1_w_raw = place("w1_w_raw", [P, 2 * H], U8, "w1_w_raw")
+        w1_s_raw = place("w1_s_raw", [P, H], U8, "w1_s_raw")
+        w1_w = place("w1_w", [P, 2 * H], U8, "w1_w")
+        w1_s = place("w1_s", [P, H], U8, "w1_s")
+        wgt_sb = place("wgt_sb", [P, M], F32, "wgt")
+        half_sb = lists.tile([P, slots], F32, name="half_sb")
+        gain_sb = lists.tile([P, slots], F32, name="gain_sb")
+        comfort_sb = lists.tile([P, groups * PACK], F32, name="comfort_sb")
 
         nc.vector.memset(tab_s[:].bitcast(I32)[:, :ZEROED_BY_VECTOR], 0)
         nc.gpsimd.memset(tab_s[:].bitcast(I32)[:, ZEROED_BY_VECTOR:], 0)
@@ -99,7 +110,7 @@ def tile_list_cochlear_spread_levels_kernel(
                 width = PASS // parts
                 spread_raw[b, g] = []
                 for part in range(parts):
-                    raw = keep.tile([P, PACK, width], F32, name="spread_raw%d%d%d" % (b, g, part), align_bytes=ALIGN)
+                    raw = place("spread_raw%d%d%d" % (b, g, part), [P, PACK, width], F32, "spread", 16 * g + 8 * b + 4 * part)
                     n0 = g * PASS + part * width
                     rows = spread[b * PASS : (b + 1) * PASS, n0 : n0 + width]
                     nc.sync.dma_start(raw[:], rows.rearrange("(p j) n -> p j n", j=PACK))
@@ -111,8 +122,8 @@ def tile_list_cochlear_spread_levels_kernel(
                     if (b, g) == (1, 0):
                         load_by_slot(comfort_sb, comfort)
 
-        v_s = keep.tile([P, S], U8, name="v_s", align_bytes=ALIGN)
-        v_w = keep.tile([P, S], U32, name="v_w", align_bytes=ALIGN)
+        v_s = place("v_s", [P, S], U8, "v_s")
+        v_w = place("v_w", [P, S], U32, "v_w")
         nc.vector.tensor_copy(
             w1_w[:].bitcast(U16).rearrange("p (b i m) -> p b i m", b=passes, i=PACK),
             w1_w_raw[:].bitcast(U16).rearrange("p (b m i) -> p b i m", b=passes, i=PACK),
@@ -123,10 +134,10 @@ def tile_list_cochlear_spread_levels_kernel(
             w1_s_raw[:].rearrange("p (b m i) -> p b i m", b=passes, i=PACK),
         )
 
-        root = keep.tile([P, slots], F32, name="root")
-        gain_inv = keep.tile([P, slots], F32, name="gain_inv")
-        sign = keep.tile([P, slots], F32, name="sign")
-        half_signed = keep.tile([P, slots], F32, name="half_signed")
+        root = lists.tile([P, slots], F32, name="root")
+        gain_inv = lists.tile([P, slots], F32, name="gain_inv")
+        sign = lists.tile([P, slots], F32, name="sign")
+        half_signed = lists.tile([P, slots], F32, name="half_signed")
         nc.scalar.activation(root[:], gain_sb[:], ACT.Abs_reciprocal_sqrt)
         nc.gpsimd.tensor_scalar(root[:], root[:], ROOT_CAP, 0.0, ALU.min, ALU.add)
         nc.gpsimd.tensor_tensor(gain_inv[:], root[:], root[:], ALU.mult)
@@ -136,7 +147,8 @@ def tile_list_cochlear_spread_levels_kernel(
         weights = {}
         for s in range(slots):
             for m0, width in ((0, M),) if s < slots - 1 else ((0, HALF), (HALF, M - HALF)):
-                scaled = keep.tile([P, width], F32, name="weights%d_%d" % (s, m0), align_bytes=ALIGN)
+                home, shift = ("xg_high", 0) if (s, m0) == (slots - 1, 0) else ("weights", 4 * s)
+                scaled = place("weights%d_%d" % (s, m0), [P, width], F32, home, shift)
                 if s < WEIGHTS_BY_SCALAR:
                     nc.scalar.activation(scaled[:], wgt_sb[:, m0 : m0 + width], ACT.Copy, scale=gain_sb[:, s : s + 1])
                 else:
@@ -151,8 +163,8 @@ def tile_list_cochlear_spread_levels_kernel(
             entries = idx[:, c * BANK // PER_COL : (c + 1) * BANK // PER_COL]
             nc.vector.tensor_copy(v_w[:, c * BANK : (c + 1) * BANK], tab_w[:].indirect(entries))
 
-        sp_w = keep.tile([P, groups, passes, PASS], U32, name="sp_w", align_bytes=ALIGN)
-        sp_s = keep.tile([P, groups, passes, PASS], U8, name="sp_s", align_bytes=ALIGN)
+        sp_w = place("sp_w", [P, groups, passes, PASS], U32, "sp_w")
+        sp_s = place("sp_s", [P, groups, passes, PASS], U8, "sp_s")
         rounded = {}
 
         def round_spread(b, g, engine, m0, m1):
@@ -174,16 +186,16 @@ def tile_list_cochlear_spread_levels_kernel(
         def quantise_spread(b, g):
             nc.vector.quantize_mx(out=sp_w[:, g, b].bitcast(FP8X4), scales=sp_s[:, g, b], in_=rounded[b, g])
 
-        for b, g in ((0, 0), (0, 1), (1, 1)):
-            rounded[b, g] = ring.tile([P, PASS * PACK], BF16, name="rounded", bufs=passes, align_bytes=ALIGN)[:]
+        for n, (b, g) in enumerate(((0, 0), (0, 1))):
+            rounded[b, g] = place("rounded%d%d" % (b, g), [P, PASS * PACK], BF16, "rounded", 4 * n)[:]
         round_spread(0, 0, nc.gpsimd, 0, P // 2)
         round_spread(0, 0, nc.gpsimd, P // 2, SPREAD_BY_GPSIMD)
         round_spread(0, 0, nc.vector, SPREAD_BY_GPSIMD, P)
         quantise_spread(0, 0)
 
-        h = [h_pool.tile([P, S], F32, name="h") for s in range(EARLY_SLOTS)]
-        xg_first = keep.tile([P, PACK, M], F32, name="xg_first")
-        xg_low = keep.tile([P, PACK, HALF], F32, name="xg_low")
+        h = [place("h", [P, S], F32, "h", bufs=PACK + 1) for s in range(EARLY_SLOTS)]
+        xg_first = place("xg_first", [P, PACK, M], F32, "xg_first")
+        xg_low = place("xg_low", [P, PACK, HALF], F32, "xg_low")
 
         def band_response(s, c):
             bank = psum.tile([P, BANK], F32, name="bank")
@@ -207,7 +219,7 @@ def tile_list_cochlear_spread_levels_kernel(
                 band_response(s, c)
         for s in range(slots):
             if s >= EARLY_SLOTS:
-                h.append(h_pool.tile([P, S], F32, name="h"))
+                h.append(place("h", [P, S], F32, "h", bufs=PACK + 1))
                 for c in range(pieces):
                     band_response(s, c)
             if s < PACK:
@@ -216,17 +228,30 @@ def tile_list_cochlear_spread_levels_kernel(
                     rounded[1, 0] = weights[0, 0].bitcast(BF16)
                     round_spread(1, 0, nc.vector, 0, P)
                     quantise_spread(1, 0)
+                if s == PACK - 1:
+                    rounded[1, 1] = place("rounded11", [P, PASS * PACK], BF16, "weights", 4 * s)[:]
+                    round_spread(1, 1, nc.vector, 0, LAST_SPREAD_BY_VECTOR)
             else:
                 pick(s, xg_low[:, s - PACK, :], 0, HALF)
-        xg_high = keep.tile([P, PACK, M - HALF], F32, name="weights%d_0" % (slots - 1), align_bytes=ALIGN)
+        xg_high = place("xg_high", [P, PACK, M - HALF], F32, "xg_high")
         for i in range(PACK):
             pick(PACK + i, xg_high[:, i, :], HALF, M - HALF)
 
-        z_w = [keep.tile([P, passes, w], U32, name="z_w%d" % k, align_bytes=ALIGN) for k, w in enumerate(WIDTHS)]
-        z_s = [keep.tile([P, passes, w], U8, name="z_s%d" % k, align_bytes=ALIGN) for k, w in enumerate(WIDTHS)]
-        y_w = keep.tile([P, groups, M], U32, name="y_w", align_bytes=ALIGN)
-        y_s = keep.tile([P, groups, M], U8, name="y_s", align_bytes=ALIGN)
-        y_home = ("spread_raw100", "tab_w", "spread_raw110", "spread_raw010", "spread_raw000")
+        z_w = [place("z_w%d" % k, [P, passes, w], U32, "z_w", starts[k] / SPAN) for k, w in enumerate(WIDTHS)]
+        z_s = [place("z_s%d" % k, [P, passes, w], U8, "z_s", starts[k] / BANK) for k, w in enumerate(WIDTHS)]
+        y_w = place("y_w", [P, groups, M], U32, "y_w")
+        y_s = place("y_s", [P, groups, M], U8, "y_s")
+        inv_home = {
+            (0, 0): ("tab_w", 0), (1, 0): ("tab_w", 4), (0, 1): ("tab_w", 8), (1, 1): ("tab_w", 12),
+            (0, 2): ("spread", 8), (1, 2): ("spread", 12), (0, 3): ("tab_s", 0), (1, 3): ("tab_s", 2),
+            (0, 4): ("wgt", 0), (1, 4): ("wgt", 2),
+        }
+        roots_home = {1: ("spread", 0), 2: ("v_w", 0), 3: ("h", 0), 4: ("h", 16)}
+        y_bf_home = {
+            (0, 0): ("spread", 12), (1, 0): ("tab_s", 1), (0, 1): ("tab_s", 3), (1, 1): ("weights", 4),
+            (0, 2): ("weights", 6), (1, 2): ("weights", 8), (0, 3): ("weights", 10), (1, 3): ("weights", 11),
+            (0, 4): ("weights", 16), (1, 4): ("weights", 17),
+        }
         xg, inv, z_bf, y, y_bf = {}, {}, {}, {}, {}
 
         def cols_of(k):
@@ -240,26 +265,27 @@ def tile_list_cochlear_spread_levels_kernel(
                 xg[1, k] = xg_high[:, :, starts[k] - HALF : starts[k] - HALF + WIDTHS[k]]
 
         def inverse(b, k):
-            home = "weights%d_0" % ((passes * k + b) % PACK)
-            inv[b, k] = keep.tile([P, PACK, WIDTHS[k]], F32, name=home, align_bytes=ALIGN)
+            inv[b, k] = place("inv%d%d" % (b, k), [P, PACK, WIDTHS[k]], F32, *inv_home[b, k])[:]
             roots = inv[b, k]
             if b == passes - 1 and k > 0:
-                roots = keep.tile([P, PACK, WIDTHS[k]], F32, name=y_home[k - 1], align_bytes=ALIGN)
+                length = sum(PACK * WIDTHS[c] for g, c in DUE[k])
+                roots = place("roots%d" % k, [P, length], F32, *roots_home[k])[:, : PACK * WIDTHS[k]]
+                roots = roots.rearrange("p (i m) -> p i m", i=PACK)
             for i in range(PACK):
                 s = PACK * b + i
                 nc.scalar.activation(
                     roots[:, i, :], xg[b, k][:, i, :], ACT.Abs_reciprocal_sqrt,
                     bias=half_signed[:, s : s + 1], scale=gain_inv[:, s : s + 1],
                 )
-            nc.scalar.activation(inv[b, k][:], roots[:], ACT.Square)
+            nc.scalar.activation(inv[b, k], roots, ACT.Square)
 
         def saturate(b, k):
             if b == 0:
-                z_bf[k] = ring.tile([P, passes, WIDTHS[k] * PACK], BF16, name="z_bf", align_bytes=ALIGN)
+                z_bf[k] = place("z_bf", [P, passes, WIDTHS[0] * PACK], BF16, "z_bf", bufs=3)[:, :, : WIDTHS[k] * PACK] if WIDTHS[k] == WIDTHS[0] else place("z_bf_narrow%d" % k, [P, passes, WIDTHS[k] * PACK], BF16, "rounded", 8 + 2 * (k % 2))[:]
             nc.vector.tensor_tensor(
                 z_bf[k][:, b, :].rearrange("p (c e i) -> p c i e", e=RUN, i=PACK),
                 xg[b, k].rearrange("p i (c e) -> p c i e", e=RUN),
-                inv[b, k][:].rearrange("p i (c e) -> p c i e", e=RUN),
+                inv[b, k].rearrange("p i (c e) -> p c i e", e=RUN),
                 ALU.mult,
             )
 
@@ -267,58 +293,49 @@ def tile_list_cochlear_spread_levels_kernel(
             nc.vector.quantize_mx(
                 out=z_w[k][:].rearrange("p b m -> p (b m)").bitcast(FP8X4),
                 scales=z_s[k][:].rearrange("p b m -> p (b m)"),
-                in_=z_bf[k][:].rearrange("p b m -> p (b m)"),
+                in_=z_bf[k].rearrange("p b m -> p (b m)"),
             )
 
-        def levels(g, k, part):
-            cols = slice(part * SPAN, (part + 1) * SPAN)
-            if (g, part) == (0, 0):
-                y[k] = keep.tile([P, groups, PACK, WIDTHS[k]], F32, name=y_home[k], align_bytes=ALIGN)
-            bank = psum.tile([P, PACK, SPAN], F32, name="bank")
-            for t in range(PACK):
-                n_cols = slice(t * P, (t + 1) * P)
-                for b in range(passes):
-                    nc.tensor.matmul_mx(
-                        out=bank[:, t, :],
-                        lhsT=sp_w[:, g, b, n_cols].bitcast(FP8X4),
-                        lhsT_scale=sp_s[:, g, b, n_cols],
-                        rhs=z_w[k][:, b, cols].bitcast(FP8X4),
-                        rhs_scale=z_s[k][:, b, cols],
-                        start=(b == 0),
-                        stop=(b == passes - 1),
-                    )
-            limit = comfort_sb[:, PACK * g : PACK * (g + 1)]
-            nc.vector.tensor_tensor(
-                y[k][:, g, :, cols], bank[:], limit.unsqueeze(2).to_broadcast([P, PACK, SPAN]), ALU.min
-            )
-
-        def store_y(g, k):
+        def levels(g, k, home, shift):
+            y[g, k] = place("y%d%d" % (g, k), [P, PACK, WIDTHS[k]], F32, home, shift)
+            for part in range(WIDTHS[k] // SPAN):
+                cols = slice(part * SPAN, (part + 1) * SPAN)
+                bank = psum.tile([P, PACK, SPAN], F32, name="bank")
+                for t in range(PACK):
+                    n_cols = slice(t * P, (t + 1) * P)
+                    for b in range(passes):
+                        nc.tensor.matmul_mx(
+                            out=bank[:, t, :],
+                            lhsT=sp_w[:, g, b, n_cols].bitcast(FP8X4),
+                            lhsT_scale=sp_s[:, g, b, n_cols],
+                            rhs=z_w[k][:, b, cols].bitcast(FP8X4),
+                            rhs_scale=z_s[k][:, b, cols],
+                            start=(b == 0),
+                            stop=(b == passes - 1),
+                        )
+                limit = comfort_sb[:, PACK * g : PACK * (g + 1)]
+                nc.vector.tensor_tensor(
+                    y[g, k][:, :, cols], bank[:], limit.unsqueeze(2).to_broadcast([P, PACK, SPAN]), ALU.min
+                )
             rows = out_0[g * PASS : (g + 1) * PASS, cols_of(k)]
             queue = nc.scalar if (g, k) == (groups - 1, chunks - 1) else nc.sync
-            queue.dma_start(rows.rearrange("(p t) m -> p t m", t=PACK), y[k][:, g])
+            queue.dma_start(rows.rearrange("(p t) m -> p t m", t=PACK), y[g, k][:])
 
         def round_y(g, k):
-            if g == groups - 1 and k < WHOLE_BY_GPSIMD:
-                y_bf[g, k] = inv[passes - 1, k + 2][:].rearrange("p i m -> p (i m)").bitcast(BF16)[:, : WIDTHS[k] * PACK]
-                nc.gpsimd.tensor_scalar(
-                    y_bf[g, k].rearrange("p (m t) -> p m t", t=PACK),
-                    y[k][:, g].rearrange("p t m -> p m t"),
-                    1.0, 0.0, ALU.mult, ALU.add,
-                )
-                return
-            y_bf[g, k] = ring.tile([P, WIDTHS[k] * PACK], BF16, name="y_bf", bufs=2 * groups, align_bytes=ALIGN)[:]
-            lo = ROUNDED_BY_GPSIMD[k] if g == 0 else 0
+            y_bf[g, k] = place("y_bf%d%d" % (g, k), [P, WIDTHS[k] * PACK], BF16, *y_bf_home[g, k])[:]
+            lo = ROUNDED_BY_GPSIMD.get((g, k), 0)
             if lo:
                 nc.gpsimd.tensor_scalar(
                     y_bf[g, k][:, : lo * PACK].rearrange("p (m t) -> p m t", t=PACK),
-                    y[k][:, g, :, :lo].rearrange("p t m -> p m t"),
+                    y[g, k][:, :, :lo].rearrange("p t m -> p m t"),
                     1.0, 0.0, ALU.mult, ALU.add,
                 )
-            copy = nc.vector.tensor_copy if (g, k) == (groups - 1, chunks - 1) else nc.scalar.copy
-            copy(
-                y_bf[g, k][:, lo * PACK :].rearrange("p (c e t) -> p c t e", e=RUN, t=PACK),
-                y[k][:, g, :, lo:].rearrange("p t (c e) -> p c t e", e=RUN),
-            )
+            if lo < WIDTHS[k]:
+                copy = nc.vector.tensor_copy if (g, k) == (groups - 1, chunks - 1) else nc.scalar.copy
+                copy(
+                    y_bf[g, k][:, lo * PACK :].rearrange("p (c e t) -> p c t e", e=RUN, t=PACK),
+                    y[g, k][:, :, lo:].rearrange("p t (c e) -> p c t e", e=RUN),
+                )
 
         def quantise_y(g, k):
             cols = cols_of(k)
@@ -330,35 +347,32 @@ def tile_list_cochlear_spread_levels_kernel(
                     y_w[:, :, cols].bitcast(I32),
                 )
 
-        def outputs(k):
-            for g in range(groups):
-                for part in range(WIDTHS[k] // SPAN):
-                    levels(g, k, part)
-                store_y(g, k)
-
+        for k in range(chunks):
+            for b in range(passes):
+                inverse(b, k)
+            if k == 1:
+                round_spread(0, 1, nc.scalar, 0, P)
+                round_spread(1, 1, nc.scalar, LAST_SPREAD_BY_VECTOR, P)
         for k in range(chunks + 2):
             last = k == chunks - 1
             if k < chunks:
                 for b in range(passes):
-                    inverse(b, k)
                     saturate(b, k)
-                    if (b, k) == (0, 0):
-                        round_spread(0, 1, nc.scalar, 0, P)
-            if k == 1:
-                round_spread(1, 1, nc.scalar, 0, P)
-                quantise_spread(0, 1)
-                quantise_spread(1, 1)
             if last:
                 quantise_z(k)
-            if 0 <= k - 1 < chunks:
-                outputs(k - 1)
+            home, shift = roots_home.get(k, ("h", 24))
+            for g, c in DUE.get(k, ()):
+                levels(g, c, home, shift)
+                shift = shift + WIDTHS[c] * PACK * 4 / KIB
             if k < chunks and not last:
                 quantise_z(k)
-            if 0 <= k - 2 < chunks:
-                for g in range(groups):
-                    round_y(g, k - 2)
-                for g in range(groups):
-                    quantise_y(g, k - 2)
+            if k == 1:
+                quantise_spread(0, 1)
+                quantise_spread(1, 1)
+            for g, c in PLANES.get(k, ()):
+                round_y(g, c)
+            for g, c in PLANES.get(k, ()):
+                quantise_y(g, c)
 
         for r in range(ROWS):
             nc.scalar.dma_start(

@@ -33,7 +33,6 @@ WIDTHS = (256, 256, 256, 128, 128)
 HALF = M // 2
 ZEROED_BY_VECTOR = 256
 WEIGHTS_BY_SCALAR = 5
-LAST_SPREAD_BY_VECTOR = 64
 EARLY_SLOTS = 2
 SPREAD_BY_GPSIMD = 96
 ROUNDED_BY_GPSIMD = {(0, 0): 256, (1, 0): 256, (0, 1): 128}
@@ -146,18 +145,12 @@ def tile_list_cochlear_spread_levels_kernel(
         nc.gpsimd.tensor_tensor(half_signed[:], sign[:], half_sb[:], ALU.mult)
         weights = {}
         for s in range(slots):
-            for m0, width in ((0, M),) if s < slots - 1 else ((0, HALF), (HALF, M - HALF)):
-                home, shift = ("xg_high", 0) if (s, m0) == (slots - 1, 0) else ("weights", 4 * s)
-                scaled = place("weights%d_%d" % (s, m0), [P, width], F32, home, shift)
-                if s < WEIGHTS_BY_SCALAR:
-                    nc.scalar.activation(scaled[:], wgt_sb[:, m0 : m0 + width], ACT.Copy, scale=gain_sb[:, s : s + 1])
-                else:
-                    nc.gpsimd.tensor_scalar(
-                        scaled[:], wgt_sb[:, m0 : m0 + width], gain_sb[:, s : s + 1], 0.0, ALU.mult, ALU.add
-                    )
-                weights[s, m0] = scaled[:]
-            if s < slots - 1:
-                weights[s, HALF] = weights[s, 0][:, HALF:]
+            scaled = place("weights%d" % s, [P, M], F32, "weights", 4 * s)
+            if s < WEIGHTS_BY_SCALAR:
+                nc.scalar.activation(scaled[:], wgt_sb[:], ACT.Copy, scale=gain_sb[:, s : s + 1])
+            else:
+                nc.gpsimd.tensor_scalar(scaled[:], wgt_sb[:], gain_sb[:, s : s + 1], 0.0, ALU.mult, ALU.add)
+            weights[s] = scaled
 
         for c in range(pieces):
             entries = idx[:, c * BANK // PER_COL : (c + 1) * BANK // PER_COL]
@@ -166,6 +159,20 @@ def tile_list_cochlear_spread_levels_kernel(
         sp_w = place("sp_w", [P, groups, passes, PASS], U32, "sp_w")
         sp_s = place("sp_s", [P, groups, passes, PASS], U8, "sp_s")
         rounded = {}
+
+        def round_half(b, g, u, engine, home, shift):
+            rounded[b, g, u] = place("rounded%d%d%d" % (b, g, u), [P, PASS * PAIR], BF16, home, shift)[:]
+            copy = engine.tensor_copy if engine is nc.vector else engine.copy
+            copy(
+                rounded[b, g, u].rearrange("p (e m j) -> p m j e", e=PAIR, j=PACK),
+                spread_raw[b, g][0][:].rearrange("p j (m u e) -> p u m j e", u=PACK // PAIR, e=PAIR)[:, u],
+            )
+
+        def quantise_half(b, g, u):
+            cols = slice(u * PAIR * P, (u + 1) * PAIR * P)
+            nc.vector.quantize_mx(
+                out=sp_w[:, g, b, cols].bitcast(FP8X4), scales=sp_s[:, g, b, cols], in_=rounded[b, g, u]
+            )
 
         def round_spread(b, g, engine, m0, m1):
             width = P // len(spread_raw[b, g])
@@ -186,16 +193,17 @@ def tile_list_cochlear_spread_levels_kernel(
         def quantise_spread(b, g):
             nc.vector.quantize_mx(out=sp_w[:, g, b].bitcast(FP8X4), scales=sp_s[:, g, b], in_=rounded[b, g])
 
-        for n, (b, g) in enumerate(((0, 0), (0, 1))):
+        for n, (b, g) in enumerate(((0, 0), (1, 0))):
             rounded[b, g] = place("rounded%d%d" % (b, g), [P, PASS * PACK], BF16, "rounded", 4 * n)[:]
         round_spread(0, 0, nc.gpsimd, 0, P // 2)
         round_spread(0, 0, nc.gpsimd, P // 2, SPREAD_BY_GPSIMD)
         round_spread(0, 0, nc.vector, SPREAD_BY_GPSIMD, P)
         quantise_spread(0, 0)
+        round_spread(1, 0, nc.vector, 0, P)
 
         h = [place("h", [P, S], F32, "h", bufs=PACK + 1) for s in range(EARLY_SLOTS)]
         xg_first = place("xg_first", [P, PACK, M], F32, "xg_first")
-        xg_low = place("xg_low", [P, PACK, HALF], F32, "xg_low")
+        xg_second = place("xg_second", [P, PACK, M], F32, "xg_low")
 
         def band_response(s, c):
             bank = psum.tile([P, BANK], F32, name="bank")
@@ -212,7 +220,7 @@ def tile_list_cochlear_spread_levels_kernel(
 
         def pick(s, out, m0, width):
             entries = idx2[:, m0 // PER_COL : (m0 + width) // PER_COL]
-            nc.vector.tensor_tensor(out, h[s][:].indirect(entries), weights[s, m0][:, :width], ALU.mult)
+            nc.vector.tensor_tensor(out, h[s][:].indirect(entries), weights[s][:, m0 : m0 + width], ALU.mult)
 
         for c in range(pieces):
             for s in range(EARLY_SLOTS):
@@ -225,32 +233,36 @@ def tile_list_cochlear_spread_levels_kernel(
             if s < PACK:
                 pick(s, xg_first[:, s, :], 0, M)
                 if s == 0:
-                    rounded[1, 0] = weights[0, 0].bitcast(BF16)
-                    round_spread(1, 0, nc.vector, 0, P)
                     quantise_spread(1, 0)
-                if s == PACK - 1:
-                    rounded[1, 1] = place("rounded11", [P, PASS * PACK], BF16, "weights", 4 * s)[:]
-                    round_spread(1, 1, nc.vector, 0, LAST_SPREAD_BY_VECTOR)
+            elif s < slots - 1:
+                pick(s, xg_second[:, s - PACK, :], 0, M)
             else:
-                pick(s, xg_low[:, s - PACK, :], 0, HALF)
-        xg_high = place("xg_high", [P, PACK, M - HALF], F32, "xg_high")
-        for i in range(PACK):
-            pick(PACK + i, xg_high[:, i, :], HALF, M - HALF)
+                for m0 in (0, HALF):
+                    pick(s, xg_second[:, s - PACK, m0 : m0 + HALF], m0, HALF)
 
         z_w = [place("z_w%d" % k, [P, passes, w], U32, "z_w", starts[k] / SPAN) for k, w in enumerate(WIDTHS)]
         z_s = [place("z_s%d" % k, [P, passes, w], U8, "z_s", starts[k] / BANK) for k, w in enumerate(WIDTHS)]
         y_w = place("y_w", [P, groups, M], U32, "y_w")
         y_s = place("y_s", [P, groups, M], U8, "y_s")
         inv_home = {
-            (0, 0): ("tab_w", 0), (1, 0): ("tab_w", 4), (0, 1): ("tab_w", 8), (1, 1): ("tab_w", 12),
+            (0, 0): ("tab_w", 0), (1, 0): ("tab_w", 8), (1, 1): ("tab_w", 12),
             (0, 2): ("spread", 8), (1, 2): ("spread", 12), (0, 3): ("tab_s", 0), (1, 3): ("tab_s", 2),
             (0, 4): ("wgt", 0), (1, 4): ("wgt", 2),
         }
-        roots_home = {1: ("spread", 0), 2: ("v_w", 0), 3: ("h", 0), 4: ("h", 16)}
-        y_bf_home = {
-            (0, 0): ("spread", 12), (1, 0): ("tab_s", 1), (0, 1): ("tab_s", 3), (1, 1): ("weights", 4),
-            (0, 2): ("weights", 6), (1, 2): ("weights", 8), (0, 3): ("weights", 10), (1, 3): ("weights", 11),
-            (0, 4): ("weights", 16), (1, 4): ("weights", 17),
+        roots_home = {(1, 0): ("rounded", 8, 4), (1, 1): ("w1_w_raw", 0, 12), (1, 2): ("spread", 0, 6), (1, 4): ("weights", 4, 2)}
+        z_bf_home = {0: ("z_bf", 0), 1: ("z_bf", 4), 2: ("z_bf", 8), 3: ("rounded", 10), 4: ("spread", 24)}
+        y_home = {
+            (0, 0): ("w1_w_raw", 0), (0, 1): ("spread", 24), (1, 0): ("spread", 28), (1, 1): ("spread", 0),
+            (0, 2): ("h", 12), (1, 2): ("h", 16), (0, 3): ("h", 20), (1, 3): ("h", 22), (0, 4): ("h", 24),
+            (1, 4): ("h", 26),
+        }
+        staged = {
+            (0, 0, 0): (nc.gpsimd, 256, "w1_w_raw", 10), (1, 0, 0): (nc.scalar, 256, "spread", 4),
+            (0, 1, 0): (nc.gpsimd, 256, "rounded", 10),
+            (1, 1, 0): (nc.scalar, 256, "weights", 4), (0, 2, 0): (nc.scalar, 256, "weights", 6),
+            (1, 2, 0): (nc.scalar, 256, "weights", 12), (0, 3, 0): (nc.scalar, 128, "weights", 14),
+            (1, 3, 0): (nc.scalar, 128, "weights", 15), (0, 4, 0): (nc.scalar, 128, "weights", 16),
+            (1, 4, 0): (nc.vector, 128, "weights", 17),
         }
         xg, inv, z_bf, y, y_bf = {}, {}, {}, {}, {}
 
@@ -259,29 +271,31 @@ def tile_list_cochlear_spread_levels_kernel(
 
         for k in range(chunks):
             xg[0, k] = xg_first[:, :, cols_of(k)]
-            if starts[k] < HALF:
-                xg[1, k] = xg_low[:, :, cols_of(k)]
-            else:
-                xg[1, k] = xg_high[:, :, starts[k] - HALF : starts[k] - HALF + WIDTHS[k]]
+            xg[1, k] = xg_second[:, :, cols_of(k)]
 
-        def inverse(b, k):
-            inv[b, k] = place("inv%d%d" % (b, k), [P, PACK, WIDTHS[k]], F32, *inv_home[b, k])[:]
-            roots = inv[b, k]
-            if b == passes - 1 and k > 0:
-                length = sum(PACK * WIDTHS[c] for g, c in DUE[k])
-                roots = place("roots%d" % k, [P, length], F32, *roots_home[k])[:, : PACK * WIDTHS[k]]
+        def inverse(b, *ks):
+            k = ks[0]
+            width = sum(WIDTHS[c] for c in ks)
+            source = xg_first if b == 0 else xg_second
+            whole = place("inv%d%d" % (b, k), [P, PACK, width], F32, *inv_home[b, k])[:]
+            roots = whole
+            if (b, k) in roots_home:
+                home, shift, length = roots_home[b, k]
+                roots = place("roots%d%d" % (b, k), [P, length * KIB // 4], F32, home, shift)[:, : PACK * width]
                 roots = roots.rearrange("p (i m) -> p i m", i=PACK)
             for i in range(PACK):
                 s = PACK * b + i
                 nc.scalar.activation(
-                    roots[:, i, :], xg[b, k][:, i, :], ACT.Abs_reciprocal_sqrt,
+                    roots[:, i, :], source[:, i, starts[k] : starts[k] + width], ACT.Abs_reciprocal_sqrt,
                     bias=half_signed[:, s : s + 1], scale=gain_inv[:, s : s + 1],
                 )
-            nc.scalar.activation(inv[b, k], roots, ACT.Square)
+            nc.scalar.activation(whole, roots, ACT.Square)
+            for c in ks:
+                inv[b, c] = whole[:, :, starts[c] - starts[k] : starts[c] - starts[k] + WIDTHS[c]]
 
         def saturate(b, k):
             if b == 0:
-                z_bf[k] = place("z_bf", [P, passes, WIDTHS[0] * PACK], BF16, "z_bf", bufs=3)[:, :, : WIDTHS[k] * PACK] if WIDTHS[k] == WIDTHS[0] else place("z_bf_narrow%d" % k, [P, passes, WIDTHS[k] * PACK], BF16, "rounded", 8 + 2 * (k % 2))[:]
+                z_bf[k] = place("z_bf%d" % k, [P, passes, WIDTHS[k] * PACK], BF16, *z_bf_home[k])[:]
             nc.vector.tensor_tensor(
                 z_bf[k][:, b, :].rearrange("p (c e i) -> p c i e", e=RUN, i=PACK),
                 xg[b, k].rearrange("p i (c e) -> p c i e", e=RUN),
@@ -296,83 +310,121 @@ def tile_list_cochlear_spread_levels_kernel(
                 in_=z_bf[k].rearrange("p b m -> p (b m)"),
             )
 
-        def levels(g, k, home, shift):
-            y[g, k] = place("y%d%d" % (g, k), [P, PACK, WIDTHS[k]], F32, home, shift)
-            for part in range(WIDTHS[k] // SPAN):
-                cols = slice(part * SPAN, (part + 1) * SPAN)
-                bank = psum.tile([P, PACK, SPAN], F32, name="bank")
-                for t in range(PACK):
-                    n_cols = slice(t * P, (t + 1) * P)
+        def levels(g, k):
+            y[g, k] = place("y%d%d" % (g, k), [P, PACK, WIDTHS[k]], F32, *y_home[g, k])
+            share = BANK // WIDTHS[k]
+            for t0 in range(0, PACK, share):
+                bank = psum.tile([P, share, WIDTHS[k]], F32, name="bank")
+                for t in range(share):
+                    n_cols = slice((t0 + t) * P, (t0 + t + 1) * P)
                     for b in range(passes):
                         nc.tensor.matmul_mx(
                             out=bank[:, t, :],
                             lhsT=sp_w[:, g, b, n_cols].bitcast(FP8X4),
                             lhsT_scale=sp_s[:, g, b, n_cols],
-                            rhs=z_w[k][:, b, cols].bitcast(FP8X4),
-                            rhs_scale=z_s[k][:, b, cols],
+                            rhs=z_w[k][:, b].bitcast(FP8X4),
+                            rhs_scale=z_s[k][:, b],
                             start=(b == 0),
                             stop=(b == passes - 1),
                         )
-                limit = comfort_sb[:, PACK * g : PACK * (g + 1)]
+                limit = comfort_sb[:, PACK * g + t0 : PACK * g + t0 + share]
                 nc.vector.tensor_tensor(
-                    y[g, k][:, :, cols], bank[:], limit.unsqueeze(2).to_broadcast([P, PACK, SPAN]), ALU.min
+                    y[g, k][:, t0 : t0 + share], bank[:], limit.unsqueeze(2).to_broadcast([P, share, WIDTHS[k]]), ALU.min
                 )
             rows = out_0[g * PASS : (g + 1) * PASS, cols_of(k)]
             queue = nc.scalar if (g, k) == (groups - 1, chunks - 1) else nc.sync
             queue.dma_start(rows.rearrange("(p t) m -> p t m", t=PACK), y[g, k][:])
 
-        def round_y(g, k):
-            y_bf[g, k] = place("y_bf%d%d" % (g, k), [P, WIDTHS[k] * PACK], BF16, *y_bf_home[g, k])[:]
-            lo = ROUNDED_BY_GPSIMD.get((g, k), 0)
-            if lo:
-                nc.gpsimd.tensor_scalar(
-                    y_bf[g, k][:, : lo * PACK].rearrange("p (m t) -> p m t", t=PACK),
-                    y[g, k][:, :, :lo].rearrange("p t m -> p m t"),
+        def round_y(g, k, m0=0):
+            engine, width, home, shift = staged[g, k, m0]
+            y_bf[g, k, m0] = place("y_bf%d%d_%d" % (g, k, m0), [P, width * PACK], BF16, home, shift)[:]
+            source = y[g, k][:, :, m0 : m0 + width]
+            if engine is nc.gpsimd:
+                engine.tensor_scalar(
+                    y_bf[g, k, m0].rearrange("p (m t) -> p m t", t=PACK), source.rearrange("p t m -> p m t"),
                     1.0, 0.0, ALU.mult, ALU.add,
                 )
-            if lo < WIDTHS[k]:
-                copy = nc.vector.tensor_copy if (g, k) == (groups - 1, chunks - 1) else nc.scalar.copy
+            else:
+                copy = engine.tensor_copy if engine is nc.vector else engine.copy
                 copy(
-                    y_bf[g, k][:, lo * PACK :].rearrange("p (c e t) -> p c t e", e=RUN, t=PACK),
-                    y[g, k][:, :, lo:].rearrange("p t (c e) -> p c t e", e=RUN),
+                    y_bf[g, k, m0].rearrange("p (c e t) -> p c t e", e=RUN, t=PACK),
+                    source.rearrange("p t (c e) -> p c t e", e=RUN),
                 )
 
-        def quantise_y(g, k):
-            cols = cols_of(k)
-            nc.vector.quantize_mx(out=y_w[:, g, cols].bitcast(FP8X4), scales=y_s[:, g, cols], in_=y_bf[g, k])
-            if g == groups - 1:
-                queue = nc.scalar if k == chunks - 1 else nc.sync
-                queue.dma_start(
-                    out_1[:, :, cols, :].rearrange("g p m t -> p g (m t)").bitcast(I32),
-                    y_w[:, :, cols].bitcast(I32),
-                )
+        def quantise_y(g, k, m0=0):
+            cols = slice(starts[k] + m0, starts[k] + m0 + staged[g, k, m0][1])
+            nc.vector.quantize_mx(out=y_w[:, g, cols].bitcast(FP8X4), scales=y_s[:, g, cols], in_=y_bf[g, k, m0])
 
-        for k in range(chunks):
-            for b in range(passes):
-                inverse(b, k)
-            if k == 1:
-                round_spread(0, 1, nc.scalar, 0, P)
-                round_spread(1, 1, nc.scalar, LAST_SPREAD_BY_VECTOR, P)
-        for k in range(chunks + 2):
-            last = k == chunks - 1
-            if k < chunks:
-                for b in range(passes):
-                    saturate(b, k)
-            if last:
-                quantise_z(k)
-            home, shift = roots_home.get(k, ("h", 24))
-            for g, c in DUE.get(k, ()):
-                levels(g, c, home, shift)
-                shift = shift + WIDTHS[c] * PACK * 4 / KIB
-            if k < chunks and not last:
-                quantise_z(k)
-            if k == 1:
-                quantise_spread(0, 1)
-                quantise_spread(1, 1)
-            for g, c in PLANES.get(k, ()):
-                round_y(g, c)
-            for g, c in PLANES.get(k, ()):
-                quantise_y(g, c)
+        def store_words(k):
+            queue = nc.scalar if k == chunks - 1 else nc.sync
+            queue.dma_start(
+                out_1[:, :, cols_of(k), :].rearrange("g p m t -> p g (m t)").bitcast(I32),
+                y_w[:, :, cols_of(k)].bitcast(I32),
+            )
+
+        inverse(0, 0, 1)
+        inverse(1, 0)
+        inverse(1, 1)
+        rounded[0, 1] = place("rounded01", [P, PASS * PACK], BF16, "w1_w_raw", 4)[:]
+        round_spread(0, 1, nc.scalar, 0, P)
+        round_half(1, 1, 1, nc.scalar, "w1_w_raw", 10)
+        inverse(0, 2)
+        inverse(1, 2)
+
+        saturate(0, 0)
+        saturate(0, 1)
+        saturate(1, 0)
+        round_half(1, 1, 0, nc.vector, "rounded", 8)
+        quantise_z(0)
+        saturate(1, 1)
+        quantise_half(1, 1, 0)
+        quantise_z(1)
+        levels(0, 0)
+        quantise_spread(0, 1)
+        quantise_half(1, 1, 1)
+        levels(0, 1)
+        levels(1, 0)
+        round_y(0, 0)
+        round_y(1, 0)
+        for k in (3, 4):
+            inverse(0, k)
+            inverse(1, k)
+        saturate(0, 2)
+        saturate(1, 2)
+        quantise_z(2)
+        levels(1, 1)
+        saturate(0, 3)
+        quantise_y(0, 0)
+        saturate(1, 3)
+        quantise_y(1, 0)
+        store_words(0)
+        quantise_z(3)
+        round_y(0, 1)
+        round_y(1, 1)
+        levels(0, 2)
+        levels(1, 2)
+        saturate(0, 4)
+        saturate(1, 4)
+        levels(0, 3)
+        quantise_z(4)
+        levels(1, 3)
+        for k in (2, 3):
+            round_y(0, k)
+            round_y(1, k)
+        quantise_y(0, 1)
+        quantise_y(1, 1)
+        store_words(1)
+        for k in (2, 3):
+            quantise_y(0, k)
+            quantise_y(1, k)
+            store_words(k)
+        levels(0, 4)
+        levels(1, 4)
+        round_y(0, 4)
+        round_y(1, 4)
+        quantise_y(0, 4)
+        quantise_y(1, 4)
+        store_words(4)
 
         for r in range(ROWS):
             nc.scalar.dma_start(

@@ -27,6 +27,7 @@ PER_COL = 16
 PAIR = 2
 RUN = 4
 SPAN = BANK // PACK
+FIRST_ROW = 112
 ALIGN = 64
 
 WIDTHS = (256, 256, 256, 128, 128)
@@ -82,9 +83,11 @@ def tile_list_cochlear_spread_levels_kernel(
         gain_sb = lists.tile([P, slots], F32, name="gain_sb")
         comfort_sb = lists.tile([P, groups * PACK], F32, name="comfort_sb")
 
-        nc.vector.memset(tab_s[:].bitcast(I32)[:, :ZEROED_BY_VECTOR], 0)
-        nc.gpsimd.memset(tab_s[:].bitcast(I32)[:, ZEROED_BY_VECTOR:], 0)
+        nc.vector.memset(tab_s[:FIRST_ROW].bitcast(I32)[:, :ZEROED_BY_VECTOR], 0)
+        nc.gpsimd.memset(tab_s[:FIRST_ROW].bitcast(I32)[:, ZEROED_BY_VECTOR:], 0)
         nc.gpsimd.memset(w1_s_raw[:].bitcast(I32), 0)
+        v_s = place("v_s", [P, S], U8, "v_s")
+        nc.gpsimd.memset(v_s[:].bitcast(I32), 0)
 
         def load_by_slot(tile, vector):
             nc.sync.dma_start(
@@ -96,12 +99,18 @@ def tile_list_cochlear_spread_levels_kernel(
                 nc.sync.dma_start(tile[r:P:QUADRANT, :].bitcast(I32), rows[r::ROWS, :].bitcast(I32))
 
         nc.sync.dma_start(idx[:], offs)
-        load_scale_rows(tab_s, tab_scales[0])
+        nc.sync.dma_start(tab_s[FIRST_ROW:, :].bitcast(I32), tab_scales[0].bitcast(I32))
         load_by_slot(gain_sb, gain)
         nc.sync.dma_start(wgt_sb[:], wgt)
         nc.sync.dma_start(w1_w_raw[:].bitcast(I32), w1_words[0].bitcast(I32))
         load_scale_rows(w1_s_raw, w1_scales[0])
         nc.sync.dma_start(tab_w[:].bitcast(I32), tab_words[0].rearrange("p t i -> p (t i)").bitcast(I32))
+        load_by_slot(half_sb, half)
+        nc.sync.dma_start(idx2[:], offs2)
+        picked_s = place("picked_s", [P, S], U8, "z_bf")
+        nc.vector.tensor_copy(picked_s[:], tab_s[:].indirect(idx[:]))
+        for r in range(ROWS):
+            nc.sync.dma_start(v_s[r:P:QUADRANT, :].bitcast(I32), picked_s[FIRST_ROW + r : P : ROWS, :].bitcast(I32))
         spread_raw = {}
         for g in range(groups):
             for b in range(passes):
@@ -114,20 +123,14 @@ def tile_list_cochlear_spread_levels_kernel(
                     rows = spread[b * PASS : (b + 1) * PASS, n0 : n0 + width]
                     nc.sync.dma_start(raw[:], rows.rearrange("(p j) n -> p j n", j=PACK))
                     spread_raw[b, g].append(raw)
-                    if (b, g, part) == (0, 0, 0):
-                        load_by_slot(half_sb, half)
-                    if (b, g, part) == (0, 0, 1):
-                        nc.sync.dma_start(idx2[:], offs2)
                     if (b, g) == (1, 0):
                         load_by_slot(comfort_sb, comfort)
 
-        v_s = place("v_s", [P, S], U8, "v_s")
         v_w = place("v_w", [P, S], U32, "v_w")
         nc.vector.tensor_copy(
             w1_w[:].bitcast(U16).rearrange("p (b i m) -> p b i m", b=passes, i=PACK),
             w1_w_raw[:].bitcast(U16).rearrange("p (b m i) -> p b i m", b=passes, i=PACK),
         )
-        nc.vector.tensor_copy(v_s[:], tab_s[:].indirect(idx[:]))
         nc.vector.tensor_copy(
             w1_s[:].rearrange("p (b i m) -> p b i m", b=passes, i=PACK),
             w1_s_raw[:].rearrange("p (b m i) -> p b i m", b=passes, i=PACK),
@@ -303,11 +306,11 @@ def tile_list_cochlear_spread_levels_kernel(
                 ALU.mult,
             )
 
-        def quantise_z(k):
+        def quantise_z(k, b0=0, b1=passes):
             nc.vector.quantize_mx(
-                out=z_w[k][:].rearrange("p b m -> p (b m)").bitcast(FP8X4),
-                scales=z_s[k][:].rearrange("p b m -> p (b m)"),
-                in_=z_bf[k].rearrange("p b m -> p (b m)"),
+                out=z_w[k][:, b0:b1].rearrange("p b m -> p (b m)").bitcast(FP8X4),
+                scales=z_s[k][:, b0:b1].rearrange("p b m -> p (b m)"),
+                in_=z_bf[k][:, b0:b1].rearrange("p b m -> p (b m)"),
             )
 
         def levels(g, k):
@@ -315,17 +318,17 @@ def tile_list_cochlear_spread_levels_kernel(
             share = BANK // WIDTHS[k]
             for t0 in range(0, PACK, share):
                 bank = psum.tile([P, share, WIDTHS[k]], F32, name="bank")
-                for t in range(share):
-                    n_cols = slice((t0 + t) * P, (t0 + t + 1) * P)
-                    for b in range(passes):
+                for b in range(passes):
+                    for t in range(share):
+                        n_cols = slice((t0 + t) * P, (t0 + t + 1) * P)
                         nc.tensor.matmul_mx(
                             out=bank[:, t, :],
                             lhsT=sp_w[:, g, b, n_cols].bitcast(FP8X4),
                             lhsT_scale=sp_s[:, g, b, n_cols],
                             rhs=z_w[k][:, b].bitcast(FP8X4),
                             rhs_scale=z_s[k][:, b],
-                            start=(b == 0),
-                            stop=(b == passes - 1),
+                            start=((b, t) == (0, 0)),
+                            stop=((b, t) == (passes - 1, share - 1)),
                         )
                 limit = comfort_sb[:, PACK * g + t0 : PACK * g + t0 + share]
                 nc.vector.tensor_tensor(
@@ -355,11 +358,10 @@ def tile_list_cochlear_spread_levels_kernel(
             cols = slice(starts[k] + m0, starts[k] + m0 + staged[g, k, m0][1])
             nc.vector.quantize_mx(out=y_w[:, g, cols].bitcast(FP8X4), scales=y_s[:, g, cols], in_=y_bf[g, k, m0])
 
-        def store_words(k):
-            queue = nc.scalar if k == chunks - 1 else nc.sync
-            queue.dma_start(
-                out_1[:, :, cols_of(k), :].rearrange("g p m t -> p g (m t)").bitcast(I32),
-                y_w[:, :, cols_of(k)].bitcast(I32),
+        def store_words(first, last):
+            cols = slice(starts[first], starts[last] + WIDTHS[last])
+            nc.sync.dma_start(
+                out_1[:, :, cols, :].rearrange("g p m t -> p g (m t)").bitcast(I32), y_w[:, :, cols].bitcast(I32)
             )
 
         inverse(0, 0, 1)
@@ -397,7 +399,7 @@ def tile_list_cochlear_spread_levels_kernel(
         quantise_y(0, 0)
         saturate(1, 3)
         quantise_y(1, 0)
-        store_words(0)
+        store_words(0, 0)
         quantise_z(3)
         round_y(0, 1)
         round_y(1, 1)
@@ -405,29 +407,31 @@ def tile_list_cochlear_spread_levels_kernel(
         levels(1, 2)
         saturate(0, 4)
         saturate(1, 4)
+        quantise_z(4, 0, 1)
+        quantise_z(4, 1, 2)
         levels(0, 3)
-        quantise_z(4)
         levels(1, 3)
         for k in (2, 3):
             round_y(0, k)
             round_y(1, k)
-        quantise_y(0, 1)
-        quantise_y(1, 1)
-        store_words(1)
-        for k in (2, 3):
+        for k in (1, 2):
             quantise_y(0, k)
             quantise_y(1, k)
-            store_words(k)
+            store_words(k, k)
         levels(0, 4)
-        levels(1, 4)
         round_y(0, 4)
+        quantise_y(0, 3)
+        levels(1, 4)
+        quantise_y(1, 3)
+        store_words(3, 3)
         round_y(1, 4)
         quantise_y(0, 4)
         quantise_y(1, 4)
-        store_words(4)
 
         for r in range(ROWS):
-            nc.scalar.dma_start(
+            queue = nc.scalar if r % 2 else nc.sync
+            queue.dma_start(
                 out_2[:, r::ROWS, :].rearrange("g q m -> q g m").bitcast(I32),
                 y_s[r:P:QUADRANT].bitcast(I32),
             )
+        store_words(4, 4)

@@ -35,7 +35,7 @@ HALF = M // 2
 ZEROED_BY_VECTOR = 256
 WEIGHTS_BY_SCALAR = 5
 EARLY_SLOTS = 2
-SPREAD_BY_GPSIMD = 96
+SPREAD_BY_GPSIMD = 64
 ROUNDED_BY_GPSIMD = {(0, 0): 256, (1, 0): 256, (0, 1): 128}
 DUE = {1: [(0, 0)], 2: [(1, 0), (0, 1)], 3: [(1, 1), (0, 2), (1, 2)], 4: [(0, 3), (1, 3)], 5: [(0, 4), (1, 4)]}
 PLANES = {2: [(0, 0)], 3: [(1, 0)], 4: [(0, 1), (1, 1), (0, 2), (1, 2)], 5: [(0, 3), (1, 3)], 6: [(0, 4), (1, 4)]}
@@ -102,9 +102,9 @@ def tile_list_cochlear_spread_levels_kernel(
         nc.sync.dma_start(tab_s[FIRST_ROW:, :].bitcast(I32), tab_scales[0].bitcast(I32))
         load_by_slot(gain_sb, gain)
         nc.sync.dma_start(wgt_sb[:], wgt)
-        nc.sync.dma_start(w1_w_raw[:].bitcast(I32), w1_words[0].bitcast(I32))
         load_scale_rows(w1_s_raw, w1_scales[0])
         nc.sync.dma_start(tab_w[:].bitcast(I32), tab_words[0].rearrange("p t i -> p (t i)").bitcast(I32))
+        nc.sync.dma_start(w1_w_raw[:].bitcast(I32), w1_words[0].bitcast(I32))
         load_by_slot(half_sb, half)
         nc.sync.dma_start(idx2[:], offs2)
         picked_s = place("picked_s", [P, S], U8, "z_bf")
@@ -127,10 +127,11 @@ def tile_list_cochlear_spread_levels_kernel(
                         load_by_slot(comfort_sb, comfort)
 
         v_w = place("v_w", [P, S], U32, "v_w")
-        nc.vector.tensor_copy(
-            w1_w[:].bitcast(U16).rearrange("p (b i m) -> p b i m", b=passes, i=PACK),
-            w1_w_raw[:].bitcast(U16).rearrange("p (b m i) -> p b i m", b=passes, i=PACK),
-        )
+        for b in range(passes):
+            nc.scalar.copy(
+                w1_w[:].bitcast(U16).rearrange("p (b i m) -> p b i m", b=passes, i=PACK)[:, b],
+                w1_w_raw[:].bitcast(U16).rearrange("p (b m i) -> p b i m", b=passes, i=PACK)[:, b],
+            )
         nc.vector.tensor_copy(
             w1_s[:].rearrange("p (b i m) -> p b i m", b=passes, i=PACK),
             w1_s_raw[:].rearrange("p (b m i) -> p b i m", b=passes, i=PACK),
@@ -196,13 +197,11 @@ def tile_list_cochlear_spread_levels_kernel(
         def quantise_spread(b, g):
             nc.vector.quantize_mx(out=sp_w[:, g, b].bitcast(FP8X4), scales=sp_s[:, g, b], in_=rounded[b, g])
 
-        for n, (b, g) in enumerate(((0, 0), (1, 0))):
+        for n, (b, g) in enumerate(((0, 0),)):
             rounded[b, g] = place("rounded%d%d" % (b, g), [P, PASS * PACK], BF16, "rounded", 4 * n)[:]
-        round_spread(0, 0, nc.gpsimd, 0, P // 2)
-        round_spread(0, 0, nc.gpsimd, P // 2, SPREAD_BY_GPSIMD)
+        round_spread(0, 0, nc.gpsimd, 0, SPREAD_BY_GPSIMD)
         round_spread(0, 0, nc.vector, SPREAD_BY_GPSIMD, P)
         quantise_spread(0, 0)
-        round_spread(1, 0, nc.vector, 0, P)
 
         h = [place("h", [P, S], F32, "h", bufs=PACK + 1) for s in range(EARLY_SLOTS)]
         xg_first = place("xg_first", [P, PACK, M], F32, "xg_first")
@@ -225,8 +224,11 @@ def tile_list_cochlear_spread_levels_kernel(
             entries = idx2[:, m0 // PER_COL : (m0 + width) // PER_COL]
             nc.vector.tensor_tensor(out, h[s][:].indirect(entries), weights[s][:, m0 : m0 + width], ALU.mult)
 
-        for c in range(pieces):
+        for c in range(pieces - 2):
             for s in range(EARLY_SLOTS):
+                band_response(s, c)
+        for s in range(EARLY_SLOTS):
+            for c in range(pieces - 2, pieces):
                 band_response(s, c)
         for s in range(slots):
             if s >= EARLY_SLOTS:
@@ -236,6 +238,9 @@ def tile_list_cochlear_spread_levels_kernel(
             if s < PACK:
                 pick(s, xg_first[:, s, :], 0, M)
                 if s == 0:
+                    rounded[1, 0] = place("rounded10", [P, PASS * PACK], BF16, "weights", 0)[:]
+                    round_spread(1, 0, nc.vector, 0, P)
+                if s == 2:
                     quantise_spread(1, 0)
             elif s < slots - 1:
                 pick(s, xg_second[:, s - PACK, :], 0, M)
@@ -252,17 +257,17 @@ def tile_list_cochlear_spread_levels_kernel(
             (0, 2): ("spread", 8), (1, 2): ("spread", 12), (0, 3): ("tab_s", 0), (1, 3): ("tab_s", 2),
             (0, 4): ("wgt", 0), (1, 4): ("wgt", 2),
         }
-        roots_home = {(1, 0): ("rounded", 8, 4), (1, 1): ("w1_w_raw", 0, 12), (1, 2): ("spread", 0, 6), (1, 4): ("weights", 4, 2)}
-        z_bf_home = {0: ("z_bf", 0), 1: ("z_bf", 4), 2: ("z_bf", 8), 3: ("rounded", 10), 4: ("spread", 24)}
+        roots_home = {(1, 0): ("rounded", 8, 4), (1, 1): ("w1_w_raw", 0, 12), (1, 2): ("spread", 4, 4), (0, 3): ("spread", 0, 4), (1, 4): ("weights", 6, 2)}
+        z_bf_home = {0: ("z_bf", 0), 1: ("z_bf", 4), 2: ("z_bf", 8), 3: ("rounded", 10), 4: ("weights", 20)}
         y_home = {
-            (0, 0): ("w1_w_raw", 0), (0, 1): ("spread", 24), (1, 0): ("spread", 28), (1, 1): ("spread", 0),
+            (0, 0): ("w1_w_raw", 0), (0, 1): ("spread", 24), (1, 0): ("spread", 28), (1, 1): ("h", 28),
             (0, 2): ("h", 12), (1, 2): ("h", 16), (0, 3): ("h", 20), (1, 3): ("h", 22), (0, 4): ("h", 24),
             (1, 4): ("h", 26),
         }
         staged = {
             (0, 0, 0): (nc.gpsimd, 256, "w1_w_raw", 10), (1, 0, 0): (nc.scalar, 256, "spread", 4),
-            (0, 1, 0): (nc.gpsimd, 256, "rounded", 10),
-            (1, 1, 0): (nc.scalar, 256, "weights", 4), (0, 2, 0): (nc.scalar, 256, "weights", 6),
+            (0, 1, 0): (nc.gpsimd, 256, "weights", 0),
+            (1, 1, 0): (nc.scalar, 256, "spread", 2), (0, 2, 0): (nc.scalar, 256, "weights", 6),
             (1, 2, 0): (nc.scalar, 256, "weights", 12), (0, 3, 0): (nc.scalar, 128, "weights", 14),
             (1, 3, 0): (nc.scalar, 128, "weights", 15), (0, 4, 0): (nc.scalar, 128, "weights", 16),
             (1, 4, 0): (nc.vector, 128, "weights", 17),
@@ -364,6 +369,13 @@ def tile_list_cochlear_spread_levels_kernel(
                 out_1[:, :, cols, :].rearrange("g p m t -> p g (m t)").bitcast(I32), y_w[:, :, cols].bitcast(I32)
             )
 
+        def store_scales(m0, m1, queues):
+            for r in range(ROWS):
+                queues[r % len(queues)].dma_start(
+                    out_2[:, r::ROWS, m0:m1].rearrange("g q m -> q g m").bitcast(I32),
+                    y_s[r:P:QUADRANT, :, m0:m1].bitcast(I32),
+                )
+
         inverse(0, 0, 1)
         inverse(1, 0)
         inverse(1, 1)
@@ -386,24 +398,28 @@ def tile_list_cochlear_spread_levels_kernel(
         quantise_half(1, 1, 1)
         levels(0, 1)
         levels(1, 0)
-        round_y(0, 0)
-        round_y(1, 0)
-        for k in (3, 4):
-            inverse(0, k)
-            inverse(1, k)
+        levels(1, 1)
+        for g, k in ((0, 0), (0, 1), (1, 0)):
+            round_y(g, k)
+        inverse(0, 3)
+        inverse(1, 3)
+        round_y(1, 1)
+        inverse(0, 4)
+        inverse(1, 4)
         saturate(0, 2)
         saturate(1, 2)
-        quantise_z(2)
-        levels(1, 1)
-        saturate(0, 3)
         quantise_y(0, 0)
-        saturate(1, 3)
+        quantise_z(2)
         quantise_y(1, 0)
         store_words(0, 0)
-        quantise_z(3)
-        round_y(0, 1)
-        round_y(1, 1)
+        quantise_y(0, 1)
+        saturate(0, 3)
+        quantise_y(1, 1)
+        store_words(1, 1)
+        store_scales(0, HALF, (nc.sync,))
+        saturate(1, 3)
         levels(0, 2)
+        quantise_z(3)
         levels(1, 2)
         saturate(0, 4)
         saturate(1, 4)
@@ -414,10 +430,9 @@ def tile_list_cochlear_spread_levels_kernel(
         for k in (2, 3):
             round_y(0, k)
             round_y(1, k)
-        for k in (1, 2):
-            quantise_y(0, k)
-            quantise_y(1, k)
-            store_words(k, k)
+        quantise_y(0, 2)
+        quantise_y(1, 2)
+        store_words(2, 2)
         levels(0, 4)
         round_y(0, 4)
         quantise_y(0, 3)
@@ -428,10 +443,5 @@ def tile_list_cochlear_spread_levels_kernel(
         quantise_y(0, 4)
         quantise_y(1, 4)
 
-        for r in range(ROWS):
-            queue = nc.scalar if r % 2 else nc.sync
-            queue.dma_start(
-                out_2[:, r::ROWS, :].rearrange("g q m -> q g m").bitcast(I32),
-                y_s[r:P:QUADRANT].bitcast(I32),
-            )
+        store_scales(HALF, M, (nc.sync, nc.scalar))
         store_words(4, 4)

@@ -75,7 +75,7 @@ def tile_list_cochlear_spread_levels_kernel(
         tab_w = place("tab_w", [P, T], U32, "tab_w")
         tab_s = place("tab_s", [P, T], U8, "tab_s")
         w1_w_raw = place("w1_w_raw", [P, 2 * H], U8, "w1_w_raw")
-        w1_s_raw = place("w1_s_raw", [P, H], U8, "w1_s_raw")
+        w1_s_raw = place("w1_s_raw", [P, H], U8, "weights", 28)
         w1_w = place("w1_w", [P, 2 * H], U8, "w1_w")
         w1_s = place("w1_s", [P, H], U8, "w1_s")
         wgt_sb = place("wgt_sb", [P, M], F32, "wgt")

@@ -438,10 +438,9 @@ def tile_list_cochlear_spread_levels_kernel(
         quantise_y(0, 3)
         levels(1, 4)
         quantise_y(1, 3)
-        store_words(3, 3)
         round_y(1, 4)
         quantise_y(0, 4)
         quantise_y(1, 4)
 
-        store_scales(HALF, M, (nc.sync, nc.scalar))
-        store_words(4, 4)
+        store_words(3, 4)
+        store_scales(HALF, M, (nc.scalar, nc.sync))

@@ -36,6 +36,7 @@ ZEROED_BY_VECTOR = 256
 WEIGHTS_BY_SCALAR = 5
 EARLY_SLOTS = 2
 SPREAD_BY_GPSIMD = 64
+SPREAD_BY_VECTOR = 96
 ROUNDED_BY_GPSIMD = {(0, 0): 256, (1, 0): 256, (0, 1): 128}
 DUE = {1: [(0, 0)], 2: [(1, 0), (0, 1)], 3: [(1, 1), (0, 2), (1, 2)], 4: [(0, 3), (1, 3)], 5: [(0, 4), (1, 4)]}
 PLANES = {2: [(0, 0)], 3: [(1, 0)], 4: [(0, 1), (1, 1), (0, 2), (1, 2)], 5: [(0, 3), (1, 3)], 6: [(0, 4), (1, 4)]}
@@ -57,7 +58,6 @@ def tile_list_cochlear_spread_levels_kernel(
     passes = H // PASS
     slots = passes * PACK
     groups = N // PASS
-    pieces = S // BANK
     chunks = len(WIDTHS)
     starts = [sum(WIDTHS[:k]) for k in range(chunks)]
 
@@ -103,10 +103,10 @@ def tile_list_cochlear_spread_levels_kernel(
         load_by_slot(gain_sb, gain)
         nc.sync.dma_start(wgt_sb[:], wgt)
         load_scale_rows(w1_s_raw, w1_scales[0])
+        nc.sync.dma_start(idx2[:], offs2)
         nc.sync.dma_start(tab_w[:].bitcast(I32), tab_words[0].rearrange("p t i -> p (t i)").bitcast(I32))
         nc.sync.dma_start(w1_w_raw[:].bitcast(I32), w1_words[0].bitcast(I32))
         load_by_slot(half_sb, half)
-        nc.sync.dma_start(idx2[:], offs2)
         picked_s = place("picked_s", [P, S], U8, "z_bf")
         nc.vector.tensor_copy(picked_s[:], tab_s[:].indirect(idx[:]))
         for r in range(ROWS):
@@ -127,10 +127,10 @@ def tile_list_cochlear_spread_levels_kernel(
                         load_by_slot(comfort_sb, comfort)
 
         v_w = place("v_w", [P, S], U32, "v_w")
-        for b in range(passes):
+        for b, i0, i1 in ((0, 0, EARLY_SLOTS), (0, EARLY_SLOTS, PACK), (1, 0, PACK)):
             nc.scalar.copy(
-                w1_w[:].bitcast(U16).rearrange("p (b i m) -> p b i m", b=passes, i=PACK)[:, b],
-                w1_w_raw[:].bitcast(U16).rearrange("p (b m i) -> p b i m", b=passes, i=PACK)[:, b],
+                w1_w[:].bitcast(U16).rearrange("p (b i m) -> p b i m", b=passes, i=PACK)[:, b, i0:i1],
+                w1_w_raw[:].bitcast(U16).rearrange("p (b m i) -> p b i m", b=passes, i=PACK)[:, b, i0:i1],
             )
         nc.vector.tensor_copy(
             w1_s[:].rearrange("p (b i m) -> p b i m", b=passes, i=PACK),
@@ -156,9 +156,10 @@ def tile_list_cochlear_spread_levels_kernel(
                 nc.gpsimd.tensor_scalar(scaled[:], wgt_sb[:], gain_sb[:, s : s + 1], 0.0, ALU.mult, ALU.add)
             weights[s] = scaled
 
-        for c in range(pieces):
-            entries = idx[:, c * BANK // PER_COL : (c + 1) * BANK // PER_COL]
-            nc.vector.tensor_copy(v_w[:, c * BANK : (c + 1) * BANK], tab_w[:].indirect(entries))
+        short = BANK // 2
+        cuts = [0, short] + list(range(BANK, S - BANK + 1, BANK)) + [S - short, S]
+        for j0, j1 in zip(cuts, cuts[1:]):
+            nc.vector.tensor_copy(v_w[:, j0:j1], tab_w[:].indirect(idx[:, j0 // PER_COL : j1 // PER_COL]))
 
         sp_w = place("sp_w", [P, groups, passes, PASS], U32, "sp_w")
         sp_s = place("sp_s", [P, groups, passes, PASS], U8, "sp_s")
@@ -207,40 +208,45 @@ def tile_list_cochlear_spread_levels_kernel(
         xg_first = place("xg_first", [P, PACK, M], F32, "xg_first")
         xg_second = place("xg_second", [P, PACK, M], F32, "xg_low")
 
-        def band_response(s, c):
+        def band_response(s, j0, j1):
             bank = psum.tile([P, BANK], F32, name="bank")
             nc.tensor.matmul_mx(
-                out=bank[:],
+                out=bank[:, : j1 - j0],
                 lhsT=w1_w[:, 2 * P * s : 2 * P * (s + 1)].bitcast(FP4X4),
                 lhsT_scale=w1_s[:, P * s : P * (s + 1)],
-                rhs=v_w[:, c * BANK : (c + 1) * BANK].bitcast(FP8X4),
-                rhs_scale=v_s[:, c * BANK : (c + 1) * BANK],
+                rhs=v_w[:, j0:j1].bitcast(FP8X4),
+                rhs_scale=v_s[:, j0:j1],
                 start=True,
                 stop=True,
             )
-            nc.scalar.activation(h[s][:, c * BANK : (c + 1) * BANK], bank[:], ACT.Square)
+            nc.scalar.activation(h[s][:, j0:j1], bank[:, : j1 - j0], ACT.Square)
 
         def pick(s, out, m0, width):
             entries = idx2[:, m0 // PER_COL : (m0 + width) // PER_COL]
             nc.vector.tensor_tensor(out, h[s][:].indirect(entries), weights[s][:, m0 : m0 + width], ALU.mult)
 
-        for c in range(pieces - 2):
+        for j0, j1 in zip(cuts[:3], cuts[1:4]):
             for s in range(EARLY_SLOTS):
-                band_response(s, c)
-        for s in range(EARLY_SLOTS):
-            for c in range(pieces - 2, pieces):
-                band_response(s, c)
+                band_response(s, j0, j1)
+        band_response(0, cuts[3], cuts[4])
+        band_response(0, cuts[4], cuts[5])
+        band_response(0, cuts[5], cuts[6])
+        for s in range(1, EARLY_SLOTS):
+            for j0 in range(cuts[3], S, BANK):
+                band_response(s, j0, j0 + BANK)
         for s in range(slots):
             if s >= EARLY_SLOTS:
                 h.append(place("h", [P, S], F32, "h", bufs=PACK + 1))
-                for c in range(pieces):
-                    band_response(s, c)
+                for j0 in range(0, S, BANK):
+                    band_response(s, j0, j0 + BANK)
             if s < PACK:
                 pick(s, xg_first[:, s, :], 0, M)
                 if s == 0:
                     rounded[1, 0] = place("rounded10", [P, PASS * PACK], BF16, "weights", 0)[:]
-                    round_spread(1, 0, nc.vector, 0, P)
+                    round_spread(1, 0, nc.vector, 0, SPREAD_BY_VECTOR)
                 if s == 2:
+                    round_spread(1, 0, nc.scalar, SPREAD_BY_VECTOR, P)
+                if s == 3:
                     quantise_spread(1, 0)
             elif s < slots - 1:
                 pick(s, xg_second[:, s - PACK, :], 0, M)
@@ -297,9 +303,10 @@ def tile_list_cochlear_spread_levels_kernel(
                     roots[:, i, :], source[:, i, starts[k] : starts[k] + width], ACT.Abs_reciprocal_sqrt,
                     bias=half_signed[:, s : s + 1], scale=gain_inv[:, s : s + 1],
                 )
-            nc.scalar.activation(whole, roots, ACT.Square)
             for c in ks:
-                inv[b, c] = whole[:, :, starts[c] - starts[k] : starts[c] - starts[k] + WIDTHS[c]]
+                cols = slice(starts[c] - starts[k], starts[c] - starts[k] + WIDTHS[c])
+                inv[b, c] = whole[:, :, cols]
+                nc.scalar.activation(inv[b, c], roots[:, :, cols], ACT.Square)
 
         def saturate(b, k):
             if b == 0:
@@ -387,12 +394,14 @@ def tile_list_cochlear_spread_levels_kernel(
 
         saturate(0, 0)
         saturate(0, 1)
+        quantise_z(0, 0, 1)
+        quantise_z(1, 0, 1)
         saturate(1, 0)
         round_half(1, 1, 0, nc.vector, "rounded", 8)
-        quantise_z(0)
+        quantise_z(0, 1, 2)
         saturate(1, 1)
         quantise_half(1, 1, 0)
-        quantise_z(1)
+        quantise_z(1, 1, 2)
         levels(0, 0)
         quantise_spread(0, 1)
         quantise_half(1, 1, 1)
@@ -407,11 +416,12 @@ def tile_list_cochlear_spread_levels_kernel(
         inverse(0, 4)
         inverse(1, 4)
         saturate(0, 2)
-        saturate(1, 2)
         quantise_y(0, 0)
-        quantise_z(2)
+        quantise_z(2, 0, 1)
+        saturate(1, 2)
         quantise_y(1, 0)
         store_words(0, 0)
+        quantise_z(2, 1, 2)
         quantise_y(0, 1)
         saturate(0, 3)
         quantise_y(1, 1)

from contextlib import ExitStack

import concourse.mybir as mybir

K, H, N, T, S, M = 512, 1024, 1024, 4096, 2048, 1024
FLOPS = 2 * K * H * S + 2 * H * N * M

F32 = mybir.dt.float32
BF16 = mybir.dt.bfloat16
I32 = mybir.dt.int32
U32 = mybir.dt.uint32
U16 = mybir.dt.uint16
U8 = mybir.dt.uint8
FP8X4 = mybir.dt.float8_e4m3fn_x4
FP4X4 = mybir.dt.float4_e2m1fn_x4
ACT = mybir.ActivationFunctionType
ALU = mybir.AluOpType

P = 128
PACK = 4
PASS = P * PACK
QUADRANT = 32
ROWS = 4
BANK = 512
BANKS = 8
PER_COL = 16
PAIR = 2
RUN = 4
SPAN = BANK // PACK
FIRST_ROW = 112
ALIGN = 64

WIDTHS = (256, 256, 256, 128, 128)
HALF = M // 2
ZEROED_BY_VECTOR = 256
WEIGHTS_BY_SCALAR = 5
EARLY_SLOTS = 2
SPREAD_BY_GPSIMD = 64
SPREAD_BY_VECTOR = 96
ROUNDED_BY_GPSIMD = {(0, 0): 256, (1, 0): 256, (0, 1): 128}
DUE = {1: [(0, 0)], 2: [(1, 0), (0, 1)], 3: [(1, 1), (0, 2), (1, 2)], 4: [(0, 3), (1, 3)], 5: [(0, 4), (1, 4)]}
PLANES = {2: [(0, 0)], 3: [(1, 0)], 4: [(0, 1), (1, 1), (0, 2), (1, 2)], 5: [(0, 3), (1, 3)], 6: [(0, 4), (1, 4)]}
KIB = 1024
HOME = {
    "h": 0, "tab_w": 40, "tab_s": 56, "w1_w_raw": 60, "w1_s_raw": 62, "w1_w": 63, "w1_s": 65, "v_s": 66,
    "v_w": 68, "wgt": 76, "weights": 80, "spread": 112, "sp_w": 144, "sp_s": 152, "xg_first": 154,
    "xg_low": 170, "xg_high": 178, "z_w": 186, "z_s": 194, "y_w": 196, "y_s": 204, "rounded": 206,
    "z_bf": 218,
}
ROOT_CAP = 2.0**60


def tile_list_cochlear_spread_levels_kernel(
    tc, tab_words, tab_scales, offs, w1_words, w1_scales, offs2, wgt, half, gain, spread, comfort,
    out_0, out_1, out_2,
):
    nc = tc.nc
    passes = H // PASS
    slots = passes * PACK
    groups = N // PASS
    chunks = len(WIDTHS)
    starts = [sum(WIDTHS[:k]) for k in range(chunks)]

    with ExitStack() as ctx:
        lists = ctx.enter_context(tc.tile_pool(name="lists", bufs=1))
        keep = ctx.enter_context(tc.tile_pool(name="keep", bufs=1))

        def place(name, shape, dtype, home, shift=0, bufs=1):
            return keep.tile(shape, dtype, name=name, bufs=bufs, align_bytes=ALIGN, offset=int((HOME[home] + shift) * KIB))

        psum = ctx.enter_context(tc.psum_pool(name="psum", bufs=BANKS))

        idx = lists.tile([P, S // PER_COL], U16, name="idx")
        idx2 = lists.tile([P, M // PER_COL], U16, name="idx2")
        tab_w = place("tab_w", [P, T], U32, "tab_w")
        tab_s = place("tab_s", [P, T], U8, "tab_s")
        w1_w_raw = place("w1_w_raw", [P, 2 * H], U8, "w1_w_raw")
        w1_s_raw = place("w1_s_raw", [P, H], U8, "weights", 28)
        w1_w = place("w1_w", [P, 2 * H], U8, "w1_w")
        w1_s = place("w1_s", [P, H], U8, "w1_s")
        wgt_sb = place("wgt_sb", [P, M], F32, "wgt")
        half_sb = lists.tile([P, slots], F32, name="half_sb")
        gain_sb = lists.tile([P, slots], F32, name="gain_sb")
        comfort_sb = lists.tile([P, groups * PACK], F32, name="comfort_sb")

        nc.vector.memset(tab_s[:FIRST_ROW].bitcast(I32)[:, :ZEROED_BY_VECTOR], 0)
        nc.gpsimd.memset(tab_s[:FIRST_ROW].bitcast(I32)[:, ZEROED_BY_VECTOR:], 0)
        nc.gpsimd.memset(w1_s_raw[:].bitcast(I32), 0)
        v_s = place("v_s", [P, S], U8, "v_s")
        nc.gpsimd.memset(v_s[:].bitcast(I32), 0)

        def load_by_slot(tile, vector):
            nc.sync.dma_start(
                tile[:].rearrange("p (a i) -> p a i", i=PACK), vector.rearrange("(a p i) -> p a i", p=P, i=PACK)
            )

        def load_scale_rows(tile, rows):
            for r in range(ROWS):
                nc.sync.dma_start(tile[r:P:QUADRANT, :].bitcast(I32), rows[r::ROWS, :].bitcast(I32))

        nc.sync.dma_start(idx[:], offs)
        nc.sync.dma_start(tab_s[FIRST_ROW:, :].bitcast(I32), tab_scales[0].bitcast(I32))
        load_by_slot(gain_sb, gain)
        nc.sync.dma_start(wgt_sb[:], wgt)
        load_scale_rows(w1_s_raw, w1_scales[0])
        nc.sync.dma_start(idx2[:], offs2)
        nc.sync.dma_start(tab_w[:].bitcast(I32), tab_words[0].rearrange("p t i -> p (t i)").bitcast(I32))
        nc.sync.dma_start(w1_w_raw[:].bitcast(I32), w1_words[0].bitcast(I32))
        load_by_slot(half_sb, half)
        picked_s = place("picked_s", [P, S], U8, "z_bf")
        nc.vector.tensor_copy(picked_s[:], tab_s[:].indirect(idx[:]))
        for r in range(ROWS):
            nc.sync.dma_start(v_s[r:P:QUADRANT, :].bitcast(I32), picked_s[FIRST_ROW + r : P : ROWS, :].bitcast(I32))
        spread_raw = {}
        for g in range(groups):
            for b in range(passes):
                parts = 2 if (b, g) == (0, 0) else 1
                width = PASS // parts
                spread_raw[b, g] = []
                for part in range(parts):
                    raw = place("spread_raw%d%d%d" % (b, g, part), [P, PACK, width], F32, "spread", 16 * g + 8 * b + 4 * part)
                    n0 = g * PASS + part * width
                    rows = spread[b * PASS : (b + 1) * PASS, n0 : n0 + width]
                    nc.sync.dma_start(raw[:], rows.rearrange("(p j) n -> p j n", j=PACK))
                    spread_raw[b, g].append(raw)
                    if (b, g) == (1, 0):
                        load_by_slot(comfort_sb, comfort)

        v_w = place("v_w", [P, S], U32, "v_w")
        for b, i0, i1 in ((0, 0, EARLY_SLOTS), (0, EARLY_SLOTS, PACK), (1, 0, PACK)):
            nc.scalar.copy(
                w1_w[:].bitcast(U16).rearrange("p (b i m) -> p b i m", b=passes, i=PACK)[:, b, i0:i1],
                w1_w_raw[:].bitcast(U16).rearrange("p (b m i) -> p b i m", b=passes, i=PACK)[:, b, i0:i1],
            )
        nc.vector.tensor_copy(
            w1_s[:].rearrange("p (b i m) -> p b i m", b=passes, i=PACK),
            w1_s_raw[:].rearrange("p (b m i) -> p b i m", b=passes, i=PACK),
        )

        root = lists.tile([P, slots], F32, name="root")
        gain_inv = lists.tile([P, slots], F32, name="gain_inv")
        sign = lists.tile([P, slots], F32, name="sign")
        half_signed = lists.tile([P, slots], F32, name="half_signed")
        nc.scalar.activation(root[:], gain_sb[:], ACT.Abs_reciprocal_sqrt)
        nc.gpsimd.tensor_scalar(root[:], root[:], ROOT_CAP, 0.0, ALU.min, ALU.add)
        nc.gpsimd.tensor_tensor(gain_inv[:], root[:], root[:], ALU.mult)
        nc.gpsimd.tensor_scalar(sign[:], gain_sb[:], 0.0, 0.5, ALU.is_ge, ALU.subtract)
        nc.gpsimd.tensor_scalar(sign[:], sign[:], 2.0, 0.0, ALU.mult, ALU.add)
        nc.gpsimd.tensor_tensor(half_signed[:], sign[:], half_sb[:], ALU.mult)
        weights = {}
        for s in range(slots):
            scaled = place("weights%d" % s, [P, M], F32, "weights", 4 * s)
            if s < WEIGHTS_BY_SCALAR:
                nc.scalar.activation(scaled[:], wgt_sb[:], ACT.Copy, scale=gain_sb[:, s : s + 1])
            else:
                nc.gpsimd.tensor_scalar(scaled[:], wgt_sb[:], gain_sb[:, s : s + 1], 0.0, ALU.mult, ALU.add)
            weights[s] = scaled

        short = BANK // 2
        cuts = [0, short] + list(range(BANK, S - BANK + 1, BANK)) + [S - short, S]
        for j0, j1 in zip(cuts, cuts[1:]):
            nc.vector.tensor_copy(v_w[:, j0:j1], tab_w[:].indirect(idx[:, j0 // PER_COL : j1 // PER_COL]))

        sp_w = place("sp_w", [P, groups, passes, PASS], U32, "sp_w")
        sp_s = place("sp_s", [P, groups, passes, PASS], U8, "sp_s")
        rounded = {}

        def round_half(b, g, u, engine, home, shift):
            rounded[b, g, u] = place("rounded%d%d%d" % (b, g, u), [P, PASS * PAIR], BF16, home, shift)[:]
            copy = engine.tensor_copy if engine is nc.vector else engine.copy
            copy(
                rounded[b, g, u].rearrange("p (e m j) -> p m j e", e=PAIR, j=PACK),
                spread_raw[b, g][0][:].rearrange("p j (m u e) -> p u m j e", u=PACK // PAIR, e=PAIR)[:, u],
            )

        def quantise_half(b, g, u):
            cols = slice(u * PAIR * P, (u + 1) * PAIR * P)
            nc.vector.quantize_mx(
                out=sp_w[:, g, b, cols].bitcast(FP8X4), scales=sp_s[:, g, b, cols], in_=rounded[b, g, u]
            )

        def round_spread(b, g, engine, m0, m1):
            width = P // len(spread_raw[b, g])
            raw = spread_raw[b, g][m0 // width][:, :, PACK * (m0 % width) : PACK * (m0 % width + m1 - m0)]
            if engine is nc.gpsimd:
                engine.tensor_scalar(
                    rounded[b, g].rearrange("p (t m j) -> p m t j", t=PACK, j=PACK)[:, m0:m1],
                    raw.rearrange("p j (m t) -> p m t j", t=PACK),
                    1.0, 0.0, ALU.mult, ALU.add,
                )
            else:
                copy = engine.tensor_copy if engine is nc.vector else engine.copy
                copy(
                    rounded[b, g].rearrange("p (u e m j) -> p u m j e", u=PACK // PAIR, e=PAIR, j=PACK)[:, :, m0:m1],
                    raw.rearrange("p j (m u e) -> p u m j e", u=PACK // PAIR, e=PAIR),
                )

        def quantise_spread(b, g):
            nc.vector.quantize_mx(out=sp_w[:, g, b].bitcast(FP8X4), scales=sp_s[:, g, b], in_=rounded[b, g])

        for n, (b, g) in enumerate(((0, 0),)):
            rounded[b, g] = place("rounded%d%d" % (b, g), [P, PASS * PACK], BF16, "rounded", 4 * n)[:]
        round_spread(0, 0, nc.gpsimd, 0, SPREAD_BY_GPSIMD)
        round_spread(0, 0, nc.vector, SPREAD_BY_GPSIMD, P)
        quantise_spread(0, 0)

        h = [place("h", [P, S], F32, "h", bufs=PACK + 1) for s in range(EARLY_SLOTS)]
        xg_first = place("xg_first", [P, PACK, M], F32, "xg_first")
        xg_second = place("xg_second", [P, PACK, M], F32, "xg_low")

        def band_response(s, j0, j1):
            bank = psum.tile([P, BANK], F32, name="bank")
            nc.tensor.matmul_mx(
                out=bank[:, : j1 - j0],
                lhsT=w1_w[:, 2 * P * s : 2 * P * (s + 1)].bitcast(FP4X4),
                lhsT_scale=w1_s[:, P * s : P * (s + 1)],
                rhs=v_w[:, j0:j1].bitcast(FP8X4),
                rhs_scale=v_s[:, j0:j1],
                start=True,
                stop=True,
            )
            nc.scalar.activation(h[s][:, j0:j1], bank[:, : j1 - j0], ACT.Square)

        def pick(s, out, m0, width):
            entries = idx2[:, m0 // PER_COL : (m0 + width) // PER_COL]
            nc.vector.tensor_tensor(out, h[s][:].indirect(entries), weights[s][:, m0 : m0 + width], ALU.mult)

        for j0, j1 in zip(cuts[:3], cuts[1:4]):
            for s in range(EARLY_SLOTS):
                band_response(s, j0, j1)
        band_response(0, cuts[3], cuts[4])
        band_response(0, cuts[4], cuts[5])
        band_response(0, cuts[5], cuts[6])
        for s in range(1, EARLY_SLOTS):
            for j0 in range(cuts[3], S, BANK):
                band_response(s, j0, j0 + BANK)
        for s in range(slots):
            if s >= EARLY_SLOTS:
                h.append(place("h", [P, S], F32, "h", bufs=PACK + 1))
                for j0 in range(0, S, BANK):
                    band_response(s, j0, j0 + BANK)
            if s < PACK:
                pick(s, xg_first[:, s, :], 0, M)
                if s == 0:
                    rounded[1, 0] = place("rounded10", [P, PASS * PACK], BF16, "weights", 0)[:]
                    round_spread(1, 0, nc.vector, 0, SPREAD_BY_VECTOR)
                if s == 2:
                    round_spread(1, 0, nc.scalar, SPREAD_BY_VECTOR, P)
                if s == 3:
                    quantise_spread(1, 0)
            elif s < slots - 1:
                pick(s, xg_second[:, s - PACK, :], 0, M)
            else:
                for m0 in (0, HALF):
                    pick(s, xg_second[:, s - PACK, m0 : m0 + HALF], m0, HALF)

        z_w = [place("z_w%d" % k, [P, passes, w], U32, "z_w", starts[k] / SPAN) for k, w in enumerate(WIDTHS)]
        z_s = [place("z_s%d" % k, [P, passes, w], U8, "z_s", starts[k] / BANK) for k, w in enumerate(WIDTHS)]
        y_w = place("y_w", [P, groups, M], U32, "y_w")
        y_s = place("y_s", [P, groups, M], U8, "y_s")
        inv_home = {
            (0, 0): ("tab_w", 0), (1, 0): ("tab_w", 8), (1, 1): ("tab_w", 12),
            (0, 2): ("spread", 8), (1, 2): ("spread", 12), (0, 3): ("tab_s", 0), (1, 3): ("tab_s", 2),
            (0, 4): ("wgt", 0), (1, 4): ("wgt", 2),
        }
        roots_home = {(1, 0): ("rounded", 8, 4), (1, 1): ("w1_w_raw", 0, 12), (1, 2): ("spread", 4, 4), (0, 3): ("spread", 0, 4), (1, 4): ("weights", 6, 2)}
        z_bf_home = {0: ("z_bf", 0), 1: ("z_bf", 4), 2: ("z_bf", 8), 3: ("rounded", 10), 4: ("weights", 20)}
        y_home = {
            (0, 0): ("w1_w_raw", 0), (0, 1): ("spread", 24), (1, 0): ("spread", 28), (1, 1): ("h", 28),
            (0, 2): ("h", 12), (1, 2): ("h", 16), (0, 3): ("h", 20), (1, 3): ("h", 22), (0, 4): ("h", 24),
            (1, 4): ("h", 26),
        }
        staged = {
            (0, 0, 0): (nc.gpsimd, 256, "w1_w_raw", 10), (1, 0, 0): (nc.scalar, 256, "spread", 4),
            (0, 1, 0): (nc.gpsimd, 256, "weights", 0),
            (1, 1, 0): (nc.scalar, 256, "spread", 2), (0, 2, 0): (nc.scalar, 256, "weights", 6),
            (1, 2, 0): (nc.scalar, 256, "weights", 12), (0, 3, 0): (nc.scalar, 128, "weights", 14),
            (1, 3, 0): (nc.scalar, 128, "weights", 15), (0, 4, 0): (nc.scalar, 128, "weights", 16),
            (1, 4, 0): (nc.vector, 128, "weights", 17),
        }
        xg, inv, z_bf, y, y_bf = {}, {}, {}, {}, {}

        def cols_of(k):
            return slice(starts[k], starts[k] + WIDTHS[k])

        for k in range(chunks):
            xg[0, k] = xg_first[:, :, cols_of(k)]
            xg[1, k] = xg_second[:, :, cols_of(k)]

        def inverse(b, *ks):
            k = ks[0]
            width = sum(WIDTHS[c] for c in ks)
            source = xg_first if b == 0 else xg_second
            whole = place("inv%d%d" % (b, k), [P, PACK, width], F32, *inv_home[b, k])[:]
            roots = whole
            if (b, k) in roots_home:
                home, shift, length = roots_home[b, k]
                roots = place("roots%d%d" % (b, k), [P, length * KIB // 4], F32, home, shift)[:, : PACK * width]
                roots = roots.rearrange("p (i m) -> p i m", i=PACK)
            for i in range(PACK):
                s = PACK * b + i
                nc.scalar.activation(
                    roots[:, i, :], source[:, i, starts[k] : starts[k] + width], ACT.Abs_reciprocal_sqrt,
                    bias=half_signed[:, s : s + 1], scale=gain_inv[:, s : s + 1],
                )
            for c in ks:
                cols = slice(starts[c] - starts[k], starts[c] - starts[k] + WIDTHS[c])
                inv[b, c] = whole[:, :, cols]
                nc.scalar.activation(inv[b, c], roots[:, :, cols], ACT.Square)

        def saturate(b, k):
            if b == 0:
                z_bf[k] = place("z_bf%d" % k, [P, passes, WIDTHS[k] * PACK], BF16, *z_bf_home[k])[:]
            nc.vector.tensor_tensor(
                z_bf[k][:, b, :].rearrange("p (c e i) -> p c i e", e=RUN, i=PACK),
                xg[b, k].rearrange("p i (c e) -> p c i e", e=RUN),
                inv[b, k].rearrange("p i (c e) -> p c i e", e=RUN),
                ALU.mult,
            )

        def quantise_z(k, b0=0, b1=passes):
            nc.vector.quantize_mx(
                out=z_w[k][:, b0:b1].rearrange("p b m -> p (b m)").bitcast(FP8X4),
                scales=z_s[k][:, b0:b1].rearrange("p b m -> p (b m)"),
                in_=z_bf[k][:, b0:b1].rearrange("p b m -> p (b m)"),
            )

        def levels(g, k):
            y[g, k] = place("y%d%d" % (g, k), [P, PACK, WIDTHS[k]], F32, *y_home[g, k])
            share = BANK // WIDTHS[k]
            for t0 in range(0, PACK, share):
                bank = psum.tile([P, share, WIDTHS[k]], F32, name="bank")
                for b in range(passes):
                    for t in range(share):
                        n_cols = slice((t0 + t) * P, (t0 + t + 1) * P)
                        nc.tensor.matmul_mx(
                            out=bank[:, t, :],
                            lhsT=sp_w[:, g, b, n_cols].bitcast(FP8X4),
                            lhsT_scale=sp_s[:, g, b, n_cols],
                            rhs=z_w[k][:, b].bitcast(FP8X4),
                            rhs_scale=z_s[k][:, b],
                            start=((b, t) == (0, 0)),
                            stop=((b, t) == (passes - 1, share - 1)),
                        )
                limit = comfort_sb[:, PACK * g + t0 : PACK * g + t0 + share]
                nc.vector.tensor_tensor(
                    y[g, k][:, t0 : t0 + share], bank[:], limit.unsqueeze(2).to_broadcast([P, share, WIDTHS[k]]), ALU.min
                )
            rows = out_0[g * PASS : (g + 1) * PASS, cols_of(k)]
            queue = nc.scalar if (g, k) == (groups - 1, chunks - 1) else nc.sync
            queue.dma_start(rows.rearrange("(p t) m -> p t m", t=PACK), y[g, k][:])

        def round_y(g, k, m0=0):
            engine, width, home, shift = staged[g, k, m0]
            y_bf[g, k, m0] = place("y_bf%d%d_%d" % (g, k, m0), [P, width * PACK], BF16, home, shift)[:]
            source = y[g, k][:, :, m0 : m0 + width]
            if engine is nc.gpsimd:
                engine.tensor_scalar(
                    y_bf[g, k, m0].rearrange("p (m t) -> p m t", t=PACK), source.rearrange("p t m -> p m t"),
                    1.0, 0.0, ALU.mult, ALU.add,
                )
            else:
                copy = engine.tensor_copy if engine is nc.vector else engine.copy
                copy(
                    y_bf[g, k, m0].rearrange("p (c e t) -> p c t e", e=RUN, t=PACK),
                    source.rearrange("p t (c e) -> p c t e", e=RUN),
                )

        def quantise_y(g, k, m0=0):
            cols = slice(starts[k] + m0, starts[k] + m0 + staged[g, k, m0][1])
            nc.vector.quantize_mx(out=y_w[:, g, cols].bitcast(FP8X4), scales=y_s[:, g, cols], in_=y_bf[g, k, m0])

        def store_words(first, last):
            cols = slice(starts[first], starts[last] + WIDTHS[last])
            nc.sync.dma_start(
                out_1[:, :, cols, :].rearrange("g p m t -> p g (m t)").bitcast(I32), y_w[:, :, cols].bitcast(I32)
            )

        def store_scales(m0, m1, queues):
            for r in range(ROWS):
                queues[r % len(queues)].dma_start(
                    out_2[:, r::ROWS, m0:m1].rearrange("g q m -> q g m").bitcast(I32),
                    y_s[r:P:QUADRANT, :, m0:m1].bitcast(I32),
                )

        inverse(0, 0, 1)
        inverse(1, 0)
        inverse(1, 1)
        rounded[0, 1] = place("rounded01", [P, PASS * PACK], BF16, "w1_w_raw", 4)[:]
        round_spread(0, 1, nc.scalar, 0, P)
        round_half(1, 1, 1, nc.scalar, "w1_w_raw", 10)
        inverse(0, 2)
        inverse(1, 2)

        saturate(0, 0)
        saturate(0, 1)
        quantise_z(0, 0, 1)
        quantise_z(1, 0, 1)
        saturate(1, 0)
        round_half(1, 1, 0, nc.vector, "rounded", 8)
        quantise_z(0, 1, 2)
        saturate(1, 1)
        quantise_half(1, 1, 0)
        quantise_z(1, 1, 2)
        levels(0, 0)
        quantise_spread(0, 1)
        quantise_half(1, 1, 1)
        levels(0, 1)
        levels(1, 0)
        levels(1, 1)
        for g, k in ((0, 0), (0, 1), (1, 0)):
            round_y(g, k)
        inverse(0, 3)
        inverse(1, 3)
        round_y(1, 1)
        inverse(0, 4)
        inverse(1, 4)
        saturate(0, 2)
        quantise_y(0, 0)
        quantise_z(2, 0, 1)
        saturate(1, 2)
        quantise_y(1, 0)
        store_words(0, 0)
        quantise_z(2, 1, 2)
        quantise_y(0, 1)
        saturate(0, 3)
        quantise_y(1, 1)
        store_words(1, 1)
        store_scales(0, HALF, (nc.sync,))
        saturate(1, 3)
        levels(0, 2)
        quantise_z(3)
        levels(1, 2)
        saturate(0, 4)
        saturate(1, 4)
        quantise_z(4, 0, 1)
        quantise_z(4, 1, 2)
        levels(0, 3)
        levels(1, 3)
        for k in (2, 3):
            round_y(0, k)
            round_y(1, k)
        quantise_y(0, 2)
        quantise_y(1, 2)
        store_words(2, 2)
        levels(0, 4)
        round_y(0, 4)
        quantise_y(0, 3)
        levels(1, 4)
        quantise_y(1, 3)
        round_y(1, 4)
        quantise_y(0, 4)
        quantise_y(1, 4)

        store_words(3, 4)
        store_scales(HALF, M, (nc.scalar, nc.sync))
